import numpy as np, ml_dtypes
CORES = [16,18,20,22]
N = 4
BF = ml_dtypes.bfloat16
W, L, VI, HOP = 4096, 256, 5, 1
def cols(a, j):
    return np.take_along_axis(a, j[:, :, None, :], 3)
def deal(rng, lo, hi, ends=0, two=False):
    o = rng.permutation(W); n = rng.integers(lo, hi + 1, W)
    if two: n = rng.choice(np.array([lo, hi]), W)
    rest = o[(o > 0) & (o < W - 1)]
    if ends == 1: o = np.concatenate([np.array([0, W - 1]), rest]); n[0] = 16
    if ends == 2: o = np.concatenate([np.array([0]), rest[:15], np.array([W - 1]), rest[15:]]); n[:2] = 16
    start = np.add.accumulate(n) - n; nc = int(np.searchsorted(start, W)); start = start[:nc]
    size = np.minimum(n[:nc], W - start); cid = np.repeat(np.arange(nc), size); pos = np.arange(W) - start[cid]
    sl = np.argsort(rng.random((nc, 16)), axis=1); head = o[start + (size * rng.random(nc)).astype(np.int64)]
    if ends == 1: sl[0] = np.concatenate([np.array([0, 15]), 1 + rng.permutation(14)]); head[0] = (W - 1) * int(rng.integers(0, 2))
    if ends == 2: sl[0] = np.concatenate([np.array([0]), 1 + rng.permutation(15)]); sl[1] = np.concatenate([np.array([15]), rng.permutation(15)]); head[0] = 0; head[1] = W - 1
    r = np.zeros(W, np.int64); r[o] = head[cid]
    cl = np.full((16, W), -1, np.int64); cl[sl[cid, pos], r[o]] = o
    return cl, r
def parts(rng):
    x = rng.integers(0, 256, (N, 8, 16, W)); cl = np.zeros((N, 8, 16, W), np.int64); r = np.zeros((N, 8, W), np.int64)
    for a in range(N):
        for g in range(8):
            lo, hi = ((1, 16), (1, 16), (8, 16), (1, 6))[int(rng.integers(0, 4)) if g else 0]
            cl[a, g], r[a, g] = deal(rng, lo, hi)
    o = rng.integers(0, W, (N, 8, 16, L)); z = rng.integers(0, 256, (N, 8, 16, L))
    t = np.stack([rng.integers(1300, 1800, (N, 8)), rng.integers(1000, 1600, (N, 8))], axis=-1)
    return x, cl, r, o, z, t
def hold(rng, x, cl, r, o, z, t, g, q, v):
    P = rng.permutation(W); w = np.arange(W); n = max(q)
    zero = P[:16]; due = P[16:16 + N]; hot = P[16 + N:16 + N + N * n].reshape(N, n)
    x[:, g][:, :, P[:16 + N + N * n]] = 0
    o[:, g] = rng.choice(zero, (N, 16, L)); z[:, g] = 0
    t[:, g, 0] = rng.integers(0, 13, N); t[:, g, 1] = 4080
    for a in range(N):
        k = np.full((16, W), -1, np.int64); k[rng.integers(0, 16, W), w] = w; cl[a, g] = k; r[a, g] = w
        c = hot[a, :q[a % 4]]; x[a, g][:, c] = 1; o[a, g, 0, rng.permutation(L - 1)[:len(c)]] = c
        d = int(t[a, g, 0]) + q[a % 4] + (1 if a % 4 == 3 else 0)
        x[a, g, :, int(due[a])] = (d >> 4) + (np.arange(16) < (d & 15))
        o[(a - HOP * v) % N, g, 0, L - 1] = due[a]
def pack(x, cl, r, o, z, t):
    return {"feat": x.reshape(N, 128, W).astype(np.float32).astype(BF), "memb": cl.reshape(N, 128, W).astype(np.int32), "rep": r.astype(np.int32),
            "fact": o.reshape(N, 128, L).astype(np.int32), "z": z.reshape(N, 128, L).astype(np.float32).astype(BF), "thr": t.astype(np.int32)}
def setup_inputs(rng):
    return pack(*parts(rng))
def setup_inputs_spread(rng):
    x, cl, r, o, z, t = parts(rng)
    x = np.floor(rng.random((N, 8, 16, W)) * np.exp2(rng.integers(0, 9, (N, 8, 1, W)))).astype(np.int64)
    z = np.floor(rng.random((N, 8, 16, L)) * np.exp2(rng.integers(0, 9, (N, 8, 1, L)))).astype(np.int64)
    o = np.minimum(np.floor(W * rng.random((N, 8, 16, L)) ** 3).astype(np.int64), W - 1)
    t = np.minimum(np.exp2(12 * rng.random((N, 8, 2))).astype(np.int64), 4080)
    t[:, :2, 0] = rng.integers(200, 1200, (N, 2))
    hold(rng, x, cl, r, o, z, t, 3, (127, 127, 127, 127), 1)
    hold(rng, x, cl, r, o, z, t, 5, (127, 127, 127, 127), min(VI, N) - 1)
    return pack(x, cl, r, o, z, t)
def setup_inputs_ends(rng):
    x, cl, r, o, z, t = parts(rng)
    x = 255 * np.where(rng.random((N, 8, 1, W)) < 0.6, rng.integers(0, 2, (N, 8, 1, W)), rng.integers(0, 2, (N, 8, 16, W)))
    z = 255 * np.where(rng.random((N, 8, 1, L)) < 0.6, rng.integers(0, 2, (N, 8, 1, L)), rng.integers(0, 2, (N, 8, 16, L)))
    o = np.where(rng.random((N, 8, 16, L)) < 0.7, (W - 1) * rng.integers(0, 2, (N, 8, 16, L)), o)
    far = ((((W - 1) * (W - 1)) >> 5) + W - 1) & (W - 1)
    for a in range(N):
        for g in range(8):
            both = 1 if g % 2 == 0 else 2
            cl[a, g], r[a, g] = deal(rng, 1, 16, both)
            t[a, g, 0] = 4080 if (g + a) % 4 == 1 else 0
            t[a, g, 1] = 4080 if (g + a) % 2 == 0 else 0
            x[a, g, :, far] = 255; x[a, g, :, W - 1] = 255
            if both == 1:
                x[a, g, :, int(r[a, g, 0])] = 255
                for b in (0, L - 1):
                    z[a, g, :, b] = 0; o[a, g, 0, b] = 0; o[a, g, 15, b] = W - 1
            else: x[a, g, :, 0] = 0
            if g == 7:
                z[a, g] = 255; z[a, g, :, L - 1] = 0; o[a, g, :, L - 1] = 0; o[a, g, 15, L - 1] = W - 1; o[a, g, int(rng.integers(0, 16)), :L - 1] = 0
    return pack(x, cl, r, o, z, t)
def setup_inputs_corners(rng):
    x, cl, r, o, z, t = parts(rng); w = np.arange(W)
    for a in range(N):
        for g in range(8):
            kind = (g + a) % 4; how = (3 * g + a) % 8
            if kind == 0: cl[a, g], r[a, g] = deal(rng, 16, 16)
            elif kind == 1:
                k = np.full((16, W), -1, np.int64); k[15 * rng.integers(0, 2, W), w] = w; cl[a, g] = k; r[a, g] = w
            elif kind == 2: cl[a, g], r[a, g] = deal(rng, 1, 16, 0, True)
            else: cl[a, g], r[a, g] = deal(rng, 15, 16)
            if how == 0: o[a, g] = r[a, g][o[a, g]]
            elif how == 1:
                no = np.flatnonzero(r[a, g] != w)
                if len(no): o[a, g] = rng.choice(no, (16, L))
            elif how == 2: o[a, g] = (W - 1) * rng.integers(0, 2, (16, L))
            elif how == 3: o[a, g] = rng.integers(0, W, (1, L))
            elif how == 4: o[a, g] = np.arange(L)[None, :]
            t[a, g, 0] = (1300, 0, 4080, 1600)[(g // 2 + a) % 4]
            t[a, g, 1] = (0, 1300, 4080, 1100)[(g + a // 2) % 4]
    z[..., 0::4] = 0; z[..., 1::4] = 255; z[..., 2::4] = cols(x, o[:, :, 0, 2::4])
    mm = W - 3; oo = W - 21; s = (((mm * oo) >> 5) + mm) & (W - 1)
    for a in range(N):
        n = (17, 16, 127, 40)[a % 4]; cl[a, 6], r[a, 6] = deal(rng, 2, 6)
        c = rng.permutation(np.flatnonzero(r[a, 6] == w))[:n]
        x[a, 6][:, c] = 0; z[a, 6, :, :n] = 255; o[a, 6, 0, :n] = c; t[a, 6, 0] = 4079; t[a, 6, 1] = 0
        k, e = deal(rng, 1, 16, 1); h = int(e[0]); p = np.arange(W)
        p[h] = oo; p[oo] = h; p[W - 1 - h] = mm; p[mm] = W - 1 - h
        cl[a, 7] = np.where(k >= 0, p[np.maximum(k, 0)], -1)[:, p]; r[a, 7] = p[e[p]]
        x[a, 7][:, np.array([int(r[a, 7, W - 1]), int(r[a, 7, W - 5]), oo, s])] = 0; x[a, 7][:, np.array([mm, s + 1])] = 255
        z[a, 7, :, 0] = 255; o[a, 7, :, 0] = oo; t[a, 7, 0] = 1000; t[a, 7, 1] = 4079
        z[a, 7, :, L - 8:] = 255; i = int(rng.integers(0, 16)); z[a, 7, i, L - 8:L - 4] = 240; z[a, 7, i, L - 4:] = 252
        o[a, 7, :, L - 8:L - 4] = W - 1; o[a, 7, :, L - 4:] = W - 5
    return pack(x, cl, r, o, z, t)
def setup_inputs_crowd(rng):
    x, cl, r, o, z, t = parts(rng); f = rng.integers(0, W, 8); f[5] = W - 1
    for g in (0, 1, 5): o[:, g] = f[g]
    o[:, 1, :, L - 1] = rng.integers(0, W, (N, 16))
    o[:, 2] = rng.choice(np.array([0, int(f[2]), W - 1]), (N, 16, L))
    t[:, (0, 1, 2, 5), 0] = rng.integers(0, 200, (N, 4))
    h = int(rng.integers(0, N))
    for g in (3, 4):
        j = int(rng.integers(0, W - 37)); w = j + 37
        P = rng.permutation(W); P = np.concatenate([P[(P != j) & (P != w)], np.array([j, w])])
        c = P[:4 * L]; b = P[4 * L:8 * L]; rest = P[8 * L:]; zero = rest[:16]; y = int(rest[-3])
        for a in range(N):
            x[a, g][:, c] = 128; x[a, g][:, b] = 0; x[a, g][:, zero] = 0; x[a, g][:, np.array([j, w, y])] = 0
            sl = np.sort(np.argsort(rng.random((4 * L, 16)), axis=1)[:, :2], axis=1)
            k = np.full((16, W), -1, np.int64); k[sl[:, 0], c] = b; k[sl[:, 1], c] = c; k[rng.integers(0, 16, len(rest)), rest] = rest
            k[:, y] = -1; k[:, w] = -1; k[0, w] = y; k[15, w] = w
            cl[a, g] = k; r[a, g] = np.arange(W); r[a, g][b] = c; r[a, g, y] = w
            p = (a % 4) * L + np.arange(L)
            o[a, g] = rng.choice(zero, (16, L)); o[a, g, 0] = np.where(rng.random(L) < 0.5, c[p], b[p])
            if g == 4: o[a, g, 0, L - 1] = zero[0]
            z[a, g] = 0
        q = L if g == 3 else L - 1
        t[:, g, 0] = 2047 - max([(v * q) & 127 for v in range(VI)]); t[:, g, 1] = 0
        if g == 3:
            x[h, g][:, np.array([j, w])] = 128; o[h, g, 1] = j
        else:
            d = int(t[h, g, 0]) + ((q & 127) >> 1); x[h, g, :, w] = (d >> 4) + (np.arange(16) < (d & 15)); o[(h - HOP) % N, g, 0, L - 1] = w
    n = W >> 4
    for a in range(N):
        for g in (6, 7):
            K = rng.permutation(W).reshape(16, n); c = K[rng.integers(1, 16, n), np.arange(n)]
            k = np.full((16, W), -1, np.int64); k[:, c] = K; cl[a, g] = k; r[a, g][K] = c[None, :]
            p = rng.permutation(n)[:L]; o[a, g] = K[rng.integers(0, 16, (16, L)), p[None, :]]
            if g == 6:
                x[a, g][:, c] = 0; z[a, g] = 255; t[a, g] = rng.integers(0, 200, 2)
            else:
                x[a, g][:, c] = 255; x[a, g][:, K[0]] = 0; z[a, g] = 0; t[a, g, 0] = int(rng.integers(1000, 3000)); t[a, g, 1] = 4080
    return pack(x, cl, r, o, z, t)
def setup_inputs_ties(rng):
    x, cl, r, o, z, t = parts(rng)
    x = 64 * rng.integers(0, 4, x.shape); z = 64 * rng.integers(0, 4, z.shape)
    for g in range(0, 8, 2):
        few = rng.permutation(W)[:64]; o[:, g] = rng.choice(few, (N, 16, L))
    t = np.stack([64 * rng.integers(20, 28, (N, 8)), 64 * rng.integers(16, 25, (N, 8))], axis=-1)
    hold(rng, x, cl, r, o, z, t, 1, (1, 2, 3, 0), 1)
    hold(rng, x, cl, r, o, z, t, 5, (1, 2, 3, 0), min(VI, N) - 1)
    return pack(x, cl, r, o, z, t)
def check_inputs(d):
    bad = []
    for k, lo, hi in (("feat", 0, 255), ("memb", -1, W - 1), ("rep", 0, W - 1), ("fact", 0, W - 1), ("z", 0, 255), ("thr", 0, 4080)):
        v = np.asarray(d[k]).astype(np.float64)
        if not (np.all(v >= lo) and np.all(v <= hi)): bad.append("range of " + k)
        elif not np.all(v == np.floor(v)): bad.append("whole numbers in " + k)
    if bad: return bad
    cl = np.asarray(d["memb"]).astype(np.int64).reshape(N, 8, 16, W); r = np.asarray(d["rep"]).astype(np.int64)
    for a in range(N):
        for g in range(8):
            k, c = np.nonzero(cl[a, g] >= 0); m = cl[a, g][k, c]; q = r[a, g]
            if not np.all(np.bincount(m, minlength=W) == 1): bad.append("memb: every column in exactly one class")
            if not np.all(q[m] == c): bad.append("rep and memb agree")
            if not np.all(q[q] == q): bad.append("rep: a representative is a member of its own class")
    return sorted(set(bad))
def reference(feat, memb, rep, fact, z, thr):
    x = feat.astype(np.float32).astype(np.int64).reshape(N, 8, 16, W); cl = memb.astype(np.int64).reshape(N, 8, 16, W); r = rep.astype(np.int64)
    o = fact.astype(np.int64).reshape(N, 8, 16, L); y = z.astype(np.float32).astype(np.int64).reshape(N, 8, 16, L)
    t1 = thr[:, :, 0].astype(np.int64); t2 = thr[:, :, 1].astype(np.int64); A = np.zeros((N, 8), np.int64)
    row = np.arange(16)[None, None, :, None]
    for v in range(VI):
        n = np.take_along_axis(r, o.reshape(N, 8, 16 * L), 2)
        D = np.sum(np.abs(cols(x, n).reshape(N, 8, 16, 16, L) - y[:, :, :, None, :]), axis=2)
        n = n.reshape(N, 8, 16, L); ks = np.argmax(D, axis=2)[:, :, None, :]
        ds = np.take_along_axis(D, ks, 2)[:, :, 0]; c = np.take_along_axis(n, ks, 2)[:, :, 0]; ob = np.take_along_axis(o, ks, 2)
        want = ds > (t1 + (A & 127))[:, :, None]
        win = np.zeros((N, 8, L), bool)
        for a in range(N):
            for g in range(8):
                win[a, g, np.unique(np.where(want[a, g], c[a, g], W + np.arange(L)), return_index=True)[1]] = True
        win = win & want
        m = cols(cl, c); has = (m >= 0) & win[:, :, None, :]; mm = np.maximum(m, 0)
        s = (((mm * ob) >> 5) + mm) & (W - 1)
        both = np.minimum(cols(x, mm.reshape(N, 8, 16 * L)), cols(x, s.reshape(N, 8, 16 * L))).reshape(N, 8, 16, 16, L)
        e = np.sum(np.abs(both - y[:, :, :, None, :]), axis=2)
        keep = has & (e <= t2[:, :, None, None]); gone = has & ~keep; got = np.any(keep, axis=2)
        best = np.argmin(np.where(keep, e, 2 ** 20), axis=2)[:, :, None, :]
        cp = np.where(got, np.take_along_axis(mm, best, 2)[:, :, 0], 0)
        ynew = np.where(got[:, :, None, :], (y + cols(x, cp)) >> 1, np.abs(y - cols(x, c)))
        for a in range(N):
            for g in range(8):
                k = cl[a, g]; k[:, c[a, g][win[a, g]]] = -1
                ex = m[a, g][gone[a, g]]; k[0, ex] = ex; r[a, g, ex] = ex
                b = np.flatnonzero(got[a, g]); k[:, cp[a, g][b]] = np.where(keep[a, g][:, b], m[a, g][:, b], -1)
                i, b = np.nonzero(keep[a, g]); r[a, g, m[a, g][i, b]] = cp[a, g][b]
        u = np.sum(y, axis=2)[:, :, None, :]
        o = np.where(D > t1[:, :, None, None], (((o * u) >> 5) + o + 37 * row) & (W - 1), o)
        y = ynew; A = A + np.sum(win, axis=2)
        if v < VI - 1: o = np.roll(o, HOP, axis=0); y = np.roll(y, HOP, axis=0)
    yc = np.sum((cl + 1) * (row + 1), axis=2)
    return {"yc": yc.astype(np.float32), "yr": r.astype(np.float32), "yo": o.reshape(N, 128, L).astype(np.float32), "yz": y.reshape(N, 128, L).astype(np.float32)}

@@ -1,0 +1,925 @@
+from concourse.bass import DstId, RemoteDMATransfer
+from concourse.mybir import dt, AluOpType, AxisListType, ActivationFunctionType
+
+W, L, VI, NR = 4096, 256, 5, 4
+F32, BF, F16, I32, U16 = "float32", "bfloat16", "float16", "int32", "uint16"
+SCRATCH = {}
+
+
+def _sb(dtype, cols, names):
+    for n in names.split():
+        SCRATCH[n] = ("sbuf", [128, cols], dtype)
+
+
+_sb(BF, 256 + 2 * W, "XW")
+_sb(I32, W, "MI")
+_sb(F32, W, "PG")
+_sb(F32, W + 256, "CT YT")
+_sb(F32, W + 2048, "IOT")
+_sb(BF, W, "OH XG AB TT PB")
+_sb(F16, W, "AO")
+_sb(BF, 2048, "EQ")
+_sb(F16, 768, "ST")
+_sb(F16, 512, "P4H")
+_sb(F32, 256, "RT NT MT MX MV SV DD A1 MP M1V DL KM YV DC MASK RMM MCOL")
+_sb(I32, 256, "PR PR2 QQ QQ2 NN O0 O1 O2 O3 O4 N0 N1 N2 N3 N4")
+_sb(U16, 256, "REPU R0U NU MU SU U0 U1 U2 U3 U4 V0 V1 V2 V3")
+_sb(F16, 256, "CREP OC OT NF SL SL2 SL3 Z0 Z1 Z2 Z3 Z4 Y0 Y1 Y2 Y3 Y4")
+_sb(BF, 256, "ZIN KT CM HIT FL EMP EQ0 EQD DC2 LB")
+_sb(BF, 1280, "RC")
+_sb(BF, 128, "GG")
+_sb(BF, 384, "CK")
+_sb(F32, 160, "J32 B32 B32N")
+_sb(BF, 160, "B16 BN16 BQ")
+_sb(F16, 160, "B1H")
+_sb(F32, 128, "BO32 WB32 G8")
+_sb(F32, 512, "P4")
+_sb(BF, 128, "BO1 BOK IP IK IKN IQ IR IL")
+_sb(F16, 128, "INH BOH")
+_sb(F32, 128, "TY")
+_sb(F32, 64, "AL")
+_sb(F32, 16, "CB COL")
+_sb(BF, 16, "WINB")
+_sb(I32, 16, "CI MI16")
+_sb(U16, 112, "LI")
+for _i in range(8):
+    SCRATCH["p%d" % _i] = ("psum", [128, 512], F32)
+
+DSEMS = ["d%d" % i for i in range(24)]
+SEMAPHORES = ["sV", "sS", "sP", "sG", "sent"] + DSEMS + ["ao%d" % v for v in range(1, VI)] + ["az%d" % v for v in range(1, VI)]
+
+SHAPES = {"feat": 4096, "memb": 4096, "rep": 4096, "fact": 256, "z": 256, "thr": 2, "yc": 4096, "yr": 4096, "yo": 256, "yz": 256}
+SIZE = {F32: 4, I32: 4, BF: 2, F16: 2, U16: 2}
+Op, Act = AluOpType, ActivationFunctionType
+
+LATX, LATS, DBW = 0.12, 0.07, 190000.0
+MODELS = [(0.00104, 0.00052, 1.56, 3.8), (0.0009, 0.00045, 1.2, 2.5), (0.0012, 0.0006, 1.9, 5.0), (0.0009, 0.0006, 1.2, 5.0)]
+WEIGHT = [200.0, 150.0, 260.0, 180.0]
+PARAM = {"nch": 4, "look": 0.6, "waw": False, "seed": 1, "iters": 1100, "mu": False, "ramp": "GS", "ahead": [1, 2], "split": False, "strict": False, "slots": False, "dmas": "0132ab456cde7",
+         "pg": ["VSSV"] + ["SSSS"] * 4, "xg": ["SSVS"] + ["SSSV"] * 4, "xm": ["SSSS"] * 5}
+BOOST = {'mm p60 BOH': 40, 'ts QQ0 PR': 50, 'tt PR0 O': 16, 'ts p60 QQ': 20, 'ts N0 NN': 15, 'ts R0U0 p3': 40, 'ts PR0 p3': 45,
+         'tt NF0 p7': 6, 'tt p7256 p7': 7, 'tt DD0 CT': 8, 'cp LB0 QQ': 9, 'tt AO2048 CT': 10, 'tt SL0 MT': 6, 'mm p5128 B16': 5,
+         'mm p5384 BN16': 20, 'tt DC0 XW': 4.5, 'cp V0 N': 5.4, 'tt NN0 p6': 7.5, 'tt p60 p6': 10, 'tt TY64 TY': 10,
+         'lin PB3072 TT': 20, 'mm p5256 IK': 15, 'ts TY0 LI': 20, 'mm p20 GG': -30, 'tt DL0 IOT': 9, 'mm p40 B1H': 10,
+         'mm p464 B1H': 10, 'mm p4128 B1H': 10, 'mm p4192 B1H': 10}
+SLOT = {"pb": 30, "pb+": 0.1, "lb": 34.5, "lb1": 42.85, "lb2": 44.7, "lb3": 47.2, "r0": 34.4, "r01": 41.75, "r02": 42.82, "r03": 44.65,
+        "ne": -10, "rt": 9.7, "oh": 1, "oh+": 2.6, "oc": 12.2, "u": 5, "ao": 0, "ao1": 2.9, "ao2": 5.4, "ao3": 7.9, "nu": 2.8, "nu+": 2.5,
+        "xg": 2.85, "xg+": 2.52, "d1": 3, "d1+": 2.5, "pr": 7.2, "s1": 15, "s1b": 15.5, "c": 15.2, "c2": 17, "mask": 15,
+        "fact": 15.7, "crep": 17.1, "hit": 17.2, "mt": 26.3, "eq": 23, "eqd": 26, "alt": 26.2, "xm": 15.6, "xm+": 1.8, "xs": 16,
+        "xs1": 18.5, "xs2": 21.5, "xs3": 25, "d3": 16, "d3+": 2.8, "s2": 33, "s2a": 34, "s2b": 34.6, "z": 41.7, "a": 52.3,
+        "km": 44.8, "yt": 52.4, "kml": 34.7, "ytl": 36.5, "zl": 37.5, "end": 30, "fin": 36, "fin+": 1, "out": 39.5, "out+": 0.1,
+        "nm": 8, "nm+": 0.5, "tt": 12.5, "tt+": 2.0, "y0": 12, "y0+": 0.3}
+ZO = 1536.0
+
+
+def R(name, lo=0, hi=None, st=1, p=None):
+    if hi is None:
+        hi = SCRATCH[name][1][1] if name in SCRATCH else SHAPES[name]
+    return ("R", name, lo, hi, st, p)
+
+
+def X(win, off):
+    return ("X", win, off)
+
+
+def cnt(a):
+    return 16 * cnt(a[2]) if a[0] == "X" else (a[3] - a[2] + a[4] - 1) // a[4]
+
+
+def isap(a):
+    return isinstance(a, tuple)
+
+
+def regs(a):
+    return [a[1], a[2]] if a[0] == "X" else [a]
+
+
+def inps(a):
+    return a[0] == "R" and a[1] in SCRATCH and SCRATCH[a[1]][0] == "psum"
+
+
+def width(a):
+    return SIZE[SCRATCH[(a[1] if a[0] == "X" else a)[1]][2]]
+
+
+def ap(T, a):
+    if not isap(a):
+        return a
+    if a[0] == "X":
+        return ap(T, a[1]).indirect(ap(T, a[2]))
+    t = T[a[1]]
+    ps = slice(None) if a[5] is None else slice(*a[5])
+    return t[ps, a[2]:a[3]] if a[4] == 1 else t[ps, a[2]:a[3]:a[4]]
+
+
+def build(CY, PCY, GA, SC):
+    ops = []
+    nd, cur = [0], [None]
+
+    def add(cost, kind, args, wr, rd, acc=None, lat=0.0, sem=None):
+        rr = []
+        for a in rd:
+            if isap(a):
+                rr += regs(a)
+        ww = []
+        for a in wr:
+            ww.append(regs(a)[0])
+            rr += regs(a)[1:]
+        ops.append({"cost": cost, "kind": kind, "args": args, "wr": ww, "rd": rr, "acc": acc, "lat": lat, "sem": sem, "prev": [], "slot": cur[0]})
+
+    def at(v, name, c=0):
+        cur[0] = (v, name, c)
+
+    def chain(lst):
+        for a, b in zip(lst, lst[1:]):
+            ops[b]["prev"].append(a)
+
+    def weave(gs, ab, ahead):
+        seq = []
+        for c in range(len(gs) + 1):
+            if c < len(gs) and list(ops[gs[c]]["cost"]) == ["S"]:
+                seq.append(gs[c])
+            if c >= ahead:
+                seq += ab[c - ahead]
+        for c in range(len(gs) + 1 - ahead, len(gs)):
+            seq += ab[c]
+        chain(seq)
+
+    def vcost(out, ins, two=False):
+        if out[0] == "X":
+            return 0.05 + SC * cnt(out) * CY
+        if ins[0][0] == "X":
+            return 0.05 + GA * cnt(out) * CY
+        n = cnt(out)
+        if two:
+            c = 1.0 if (inps(ins[0]) or inps(ins[1])) else 2.0
+        else:
+            c = 0.5 if max([width(a) for a in [out] + ins]) == 2 else 1.0
+        return max(64, c * n) * CY
+
+    def scost(out, a):
+        return 0.065 + GA * cnt(out) * CY if a[0] == "X" else max(64, cnt(out)) * CY + 0.03
+
+    def tt(out, a, b, op):
+        add({"V": vcost(out, [a, b], True)}, "tt", (out, a, b, op), [out], [a, b])
+
+    def ts(out, a, s1, op0, s2=None, op1=None):
+        add({"V": vcost(out, [a])}, "ts", (out, a, s1, s2, op0, op1), [out], [a, s1, s2])
+
+    def cp(out, a):
+        add({"V": vcost(out, [a])}, "cp", (out, a), [out], [a])
+
+    def lin(out, a, scale, bias, eng="VS"):
+        c = {}
+        if "V" in eng:
+            c["V"] = vcost(out, [a])
+        if "S" in eng:
+            c["S"] = scost(out, a)
+        add(c, "lin", (out, a, scale, bias), [out], [a])
+
+    def act(out, a, fn, scale=1.0, bias=0.0):
+        add({"S": scost(out, a)}, "act", (out, a, fn, scale, bias), [out], [a, bias])
+
+    def scan(out, d0, d1, init, op0, op1):
+        add({"V": vcost(out, [d0, d1])}, "scan", (out, d0, d1, init, op0, op1), [out], [d0, d1])
+
+    def tr(out, a):
+        add({"V": vcost(out, [a])}, "tr", (out, a), [out], [a])
+
+    def red(out, a):
+        add({"V": max(64, cnt(a)) * CY}, "red", (out, a), [out], [a])
+
+    def ms(out, val):
+        add({"V": vcost(out, [out])}, "ms", (out, val), [out], [])
+
+    def mm(lst, acc=None):
+        c = sum([max(64, cnt(m[2])) * (4 if width(m[2]) == 4 else 1) for m in lst]) * PCY + 0.03
+        add({"P": c}, "mm", lst, [m[0] for m in lst], [m[1] for m in lst] + [m[2] for m in lst] + ([R("p5")] if acc and acc[0] == "open" else []), acc)
+
+    def iota(out, pat, base, ch):
+        add({"G": 0.13 + 2 * cnt(out) * CY}, "iota", (out, pat, base, ch), [out], [])
+
+    def ramp(out, a, shift, pat, base):
+        c = {"G": 0.13 + 2 * cnt(out) * CY, "S": scost(out, a), "V": vcost(out, [a])}
+        add({e: c[e] for e in PARAM["ramp"]}, "ramp", (out, a, 1.0, float(shift), pat, base), [out], [a])
+
+    def asel(out, pat, cmp, base, ch):
+        add({"G": 0.17 + 2 * cnt(out) * CY}, "asel", (out, pat, cmp, base, ch), [out], [out])
+
+    def dma(out, a, nbytes, q="Y"):
+        add({q: 0.06}, "dma", (out, a), [out], [a], lat=nbytes, sem=(DSEMS[nd[0]], 16))
+        nd[0] += 1
+
+    def rdma(pairs, sem):
+        add({"G": 0.3 * len(pairs)}, "rdma", pairs, [x[0] for x in pairs], [x[1] for x in pairs], lat=2.0, sem=(sem, len(pairs)))
+
+    NCH = PARAM["nch"]
+    CL = L // NCH
+    CE = 16 * CL
+    KB = 512 // CL
+    col = lambda i: R("COL", i, i + 1)
+    PM, PAR0, PAR1, NPM, K37, KP1, T1X, TKX, TWX, AC, AI = [col(i) for i in range(11)]
+    ty = lambda i: R("TY", 16 * i, 16 * i + 16)
+    li = lambda i: R("LI", 16 * i, 16 * i + 16)
+    XA, XD, XZ = R("XW", 256, 256 + W), R("XW", 256, 256 + 2 * W), R("XW", 0, 256 + W)
+    IOA, IOB = R("IOT", 0, W), R("IOT", 2048, 2048 + W)
+    CG, IJ = R("CT", 0, W), R("YT", 256, 256 + W)
+    bview = lambda n, k: R(n, 15 - k, 143 - k)
+    sub, NSUB = [0], 2
+
+    dma(R("NN"), R("rep"), 131072)
+    dma(R("O0"), R("fact"), 131072)
+    dma(R("CI", 8, 10, 1, (0, 8)), R("thr"), 64)
+    dma(R("ZIN"), R("z"), 65536)
+    dma(XA, R("feat"), 1048576)
+    for c in range(2):
+        dma(R("MI", 2048 * c, 2048 * c + 2048), R("memb", 2048 * c, 2048 * c + 2048), 1048576)
+    dma(R("XW", 256 + W, 256 + 2 * W), R("feat"), 1048576)
+
+    iota(R("CI", 0, 1), [[0, 1]], 0, 1)
+    ts(R("CI", 1, 2), R("CI", 0, 1), 15, Op.bitwise_and)
+    ts(R("CI", 2, 3), R("CI", 0, 1), 16, Op.bitwise_and)
+    cp(PM, R("CI", 1, 2))
+    ts(PAR0, R("CI", 2, 3), 0.0, Op.is_equal)
+    ts(PAR1, R("CI", 2, 3), 16.0, Op.is_equal)
+    ts(NPM, R("CI", 1, 2), -1.0, Op.mult)
+    ts(K37, R("CI", 1, 2), 37.0, Op.mult)
+    ts(KP1, R("CI", 1, 2), 1.0, Op.add)
+    ms(R("BO32"), 1.0)
+    asel(R("BO32"), [[-16, 8], [0, 16]], Op.is_ge, 0, 1)
+    asel(R("BO32"), [[16, 8], [0, 16]], Op.is_ge, 15, -1)
+    iota(R("AL", 48, 64), [[1, 16]], 0, 0)
+    cp(li(6), R("AL", 48, 64))
+    ts(R("AL", 0, 16), R("AL", 48, 64), 16.0, Op.mult, PM, Op.add)
+    ts(R("CI", 5, 6), R("CI", 0, 1), 7, Op.bitwise_and)
+    ts(R("CI", 6, 7), R("CI", 0, 1), 8, Op.bitwise_and)
+    cp(col(13), R("CI", 5, 6))
+    ts(col(14), R("CI", 6, 7), 0.125, Op.mult)
+    ts(col(15), R("CI", 0, 1), 16.0, Op.is_ge)
+    iota(R("G8"), [[1, 8], [0, 16]], 0, 0)
+    iota(R("WB32"), [[0, 64], [1, 2]], 0, 0)
+    ts(R("G8"), R("G8"), col(13), Op.is_equal)
+    ts(R("WB32"), R("WB32"), col(14), Op.is_equal, col(15), Op.max)
+    tt(R("GG"), R("G8"), R("WB32"), Op.mult)
+    ms(R("B32"), 0.0)
+    cp(R("B32", 15, 143, 16), R("BO32", 0, 128, 16))
+    ts(R("B32N"), R("B32"), -1.0, Op.mult)
+    ts(R("B16"), R("B32"), 16.0, Op.mult)
+    ts(R("BN16"), R("B32"), -16.0, Op.mult)
+    cp(R("B1H"), R("B32"))
+    ms(R("J32"), 1.0)
+    asel(R("J32"), [[-1, 160]], Op.is_equal, 16, 1)
+    for n, s in (("IP", 1.0), ("INH", -1.0), ("IK", 65536.0), ("IKN", -65536.0), ("IQ", -0.25), ("IR", -8192.0), ("IL", -240.0)):
+        ts(R(n), R("J32", 16, 144), s, Op.mult)
+    for b in range(2):
+        for e in range(2):
+            o = 16 + 16 * (b - e)
+            ts(R("P4", 128 * (2 * b + e), 128 * (2 * b + e) + 128), R("J32", o, o + 128), PAR1 if b else PAR0, Op.mult)
+    cp(R("P4H"), R("P4"))
+    ms(R("CK", 0, 128), -2048.0)
+    ms(R("CK", 128, 256), -30720.0)
+    ms(R("CK", 256, 384), -256.0)
+    ts(R("BQ"), R("B32"), -0.0625, Op.mult)
+    for n, s in (("BO1", 1.0), ("BOH", 1.0), ("BOK", 65536.0)):
+        ts(R(n), R("BO32"), s, Op.mult)
+    ts(R("WB32"), R("BO32"), KP1, Op.mult)
+    cp(R("TY", 0, 2, 1, (0, 8)), R("CI", 8, 10, 1, (0, 8)))
+    mm([(R("p6", 0, 2), R("G8", 0, 128, 1, (0, 8)), R("TY", 0, 2, 1, (0, 8)), True, True)])
+    ts(T1X, R("p6", 0, 1), 16.0, Op.mult, 0.5, Op.add)
+    ts(col(12), R("p6", 0, 1), -262144.0, Op.mult, -8192.0, Op.add)
+    ts(TWX, R("p6", 0, 1), 16.0, Op.mult, 0.5, Op.add)
+    ts(TKX, R("p6", 1, 2), -16.0, Op.mult, 131072 - 15.5, Op.add)
+    ms(AC, 0.0)
+    iota(R("DL"), [[0, 16], [1, 16]], 0, 0)
+    ts(R("KM"), R("DL"), 0.0, Op.is_gt)
+    ts(R("RMM"), R("KM"), 2e9, Op.mult, -1e9, Op.add)
+    ts(R("YV"), R("DL"), PM, Op.is_gt)
+    ts(R("DC"), R("DL"), PM, Op.is_equal)
+    tt(R("p6", 256, 512), R("DC"), R("YV"), Op.subtract)
+    ts(R("KT"), R("DL"), 0.0, Op.mult, NPM, Op.add)
+    ms(R("CM"), -ZO)
+    ts(R("AL", 16, 32), R("AL", 0, 16), -2304.0, Op.add)
+    ts(R("AL", 32, 48), R("AL", 0, 16), 4096.0, Op.add)
+    ts(R("AL", 48, 64), R("AL", 0, 16), 2048.0, Op.add)
+    iota(R("MCOL"), [[1, 256]], 0, 0)
+    ts(col(11), PM, 256.0, Op.mult)
+    ts(R("MCOL"), R("MCOL"), col(11), Op.add)
+    iota(R("YT", 256, 768), [[1, 32], [256, 16]], 0, 0)
+    iota(R("IOT", 0, 512), [[1, 512]], -2048, 0)
+    for h in range(1, 8):
+        ramp(R("YT", 256 + 512 * h, 768 + 512 * h), R("YT", 256, 768), 32 * h, [[1, 32], [256, 16]], 32 * h)
+    for h in range(1, 12):
+        ramp(R("IOT", 512 * h, 512 * h + 512), R("IOT", 0, 512), 512 * h, [[1, 512]], 512 * h - 2048)
+
+
+    cp(R("U0"), R("O0"))
+    ts(R("Z0"), R("ZIN"), ZO, Op.add)
+    cp(R("REPU"), R("NN"))
+    ts(R("PR"), R("NN"), 4032, Op.bitwise_and)
+    rc = lambda i: R("RC", 256 * i, 256 * i + 256)
+    cp(rc(0), R("PR"))
+    ts(R("QQ"), R("NN"), 63, Op.bitwise_and)
+    cp(rc(1), R("QQ"))
+
+    ts(R("PR2"), R("NN"), 17.0, Op.mult)
+    ts(R("QQ2"), R("PR2"), 31, Op.bitwise_and)
+    ts(rc(2), R("QQ2"), 16.0, Op.mult, 2048.0, Op.add)
+    ts(rc(4), R("QQ2"), -16.0, Op.mult)
+    ts(R("SV"), R("QQ2"), 15.0, Op.mult, 256.0, Op.add)
+    tt(R("SV"), R("SV"), R("NN"), Op.add)
+    ts(rc(3), R("SV"), -16.0, Op.mult)
+    for i, p in enumerate((0, 8, 32, 64, 72)):
+        dma(R("PB", 0, W, 1, (p, p + 8)), rc(i), 65536)
+    n = len(ops)
+    chain([{"a": n - 5, "b": n - 4, "c": n - 3, "d": n - 2, "e": n - 1}.get(x) or int(x) for x in PARAM["dmas"]])
+
+    def spread(r2, p, k, banks):
+        bank = banks[sub[0] % 2]
+        sub[0] += 1
+        mm([(R(bank), R("GG", 0, 128, 1, (p, p + k)), R("PB", 512 * r2, 512 * r2 + 512, 1, (p, p + k)), True, True)])
+        return bank
+
+    for r2 in range(8):
+        lin(R("TT", 512 * r2, 512 * r2 + 512), R(spread(r2, 0, 16, ["p0", "p1"])), 1.0, 0.0)
+    for h in range(8):
+        ramp(R("CT", 512 * h, 512 * h + 512), R("IOT", 0, 512), 512 * h, [[1, 512]], 512 * h - 2048)
+
+    def tables():
+        for c in range(4):
+            at(0, "oh", c)
+            tt(R("OH", 1024 * c, 1024 * c + 1024), X(R("MI"), R("REPU", 64 * c, 64 * c + 64)),
+               R("YT", 256 + 1024 * c, 256 + 1024 * c + 1024), Op.is_equal)
+
+    def tables2():
+        for r2 in range(8):
+            at(0, "nm", r2)
+            lin(R("TT", 512 * r2, 512 * r2 + 512), R(spread(r2, 32, 8, ["p2", "p4"])), 1.0, 0.0, "S")
+        for r2 in range(8):
+            at(0, "tt", r2)
+            bank = spread(r2, 64, 16, ["p2", "p4"])
+            for r in (2 * r2, 2 * r2 + 1):
+                o = R(bank, 256 * (r & 1), 256 * (r & 1) + 256)
+                tt(o, R("OH", r, W, 16), o, Op.mult)
+            tt(R("TT", 512 * r2, 512 * r2 + 512), R("TT", 512 * r2, 512 * r2 + 512), R(bank), Op.add)
+        for c in range(8):
+            bank = "p2"
+            at(0, "y0", c)
+            ts(R("PG", 512 * c, 512 * c + 512), R("MI", 512 * c, 512 * c + 512), 1.0, Op.add)
+            mm([(R(bank), R("WB32"), R("PG", 512 * c, 512 * c + 512), True, True)])
+            lin(R("YT", 256 + 512 * c, 768 + 512 * c), R(bank), 1.0, 0.0, "S")
+
+    def extract(out, lhs, src, c, acc=None):
+        mm([(out, bview(lhs, k), R(src, CE * c + CL * k, CE * c + CL * k + CL), False, False) for k in range(16)], acc)
+
+    def extract_s(out, lhs, src, c, ck=None, more=[]):
+        mm([(out, bview(lhs, k), R(src, CE * c + k, CE * c + CE, 16), k == 0, k == 15 and ck is None) for k in range(16)]
+           + more + ([] if ck is None else [(out, R("IP"), R("CK", ck, ck + CL), False, True)]))
+
+    def dist(src, z, c, out, lhs, acc):
+        made = []
+        for h in range(16 // KB):
+            bank = "p%d" % (sub[0] % (2 if z == "Z0" else 3))
+            sub[0] += 1
+            lst = []
+            for k in range(KB):
+                o = R(bank, CL * k, CL * k + CL)
+                lst += [(o, R("IP"), R(src, CE * c + KB * h + k, CE * c + CE, 16), True, False),
+                        (o, R("INH"), R(z, CL * c, CL * c + CL), False, True)]
+            mm(lst)
+            act(R("AB", CE * c + 512 * h, CE * c + 512 * h + 512), R(bank), Act.Abs, 1.0, ZO)
+            made.append(len(ops) - 1)
+        extract(out, lhs, "AB", c, acc)
+        return made
+
+    def best(key, pay):
+        tr(R("p7", 0, 256), key)
+        scan(R("MX"), R("RMM"), R("p7", 0, 256), 0.0, Op.min, Op.max)
+        tolist("MX", "P4", 0, 1, 304)
+        tt(R("p7", 256, 512), R("p7", 0, 256), R("MX"), Op.is_equal)
+        tt(R("NF"), R("p7", 0, 256), R("MX"), Op.is_lt)
+        for src, tmp, at in pay:
+            tt(R(tmp), R(src), R("p7", 256, 512), Op.mult)
+            scan(R("ST", at, at + 256), R("NF"), R(tmp), 0.0, Op.mult, Op.add)
+
+    def tolist(src, lhs, at, n, o):
+        lst = []
+        for b in range(2):
+            for e in range(2):
+                lst.append((R("p3", o + b, o + 16 * n, 2), R(lhs, 128 * (2 * b + e), 128 * (2 * b + e) + 128),
+                            R(src, at + 16 * e + 15, at + 256 * n, 32), e == 0, e == 1))
+        mm(lst)
+
+    def pre(v):
+        gs = []
+        for c in range(NCH):
+            o, u = R("p3", CL * c, CL * c + CL), R("U%d" % v, CL * c, CL * c + CL)
+            at(v - 1, "pb", c)
+            if v:
+                lin(R("PB", CE * c, CE * c + CE), X(R("TT"), u), 1.0, 0.0, PARAM["pg"][v][c])
+            else:
+                lin(R("AB", CE * c, CE * c + CE), X(R("TT"), u), -2.0, 0.0, PARAM["pg"][v][c])
+            if PARAM["pg"][v][c] == "S":
+                gs.append(len(ops) - 1)
+                chain(gs[-2:])
+            if v:
+                extract_s(o, "BQ", "PB", c, 256)
+                at(v - 1, "lb", c)
+                ts(R("PR2", CL * c, CL * c + CL), o, 17.0, Op.mult)
+                ts(R("QQ2", CL * c, CL * c + CL), R("PR2", CL * c, CL * c + CL), 31, Op.bitwise_and)
+                cp(R("LB", CL * c, CL * c + CL), R("QQ2", CL * c, CL * c + CL))
+            else:
+                extract_s(o, "BQ", "AB", c, 0)
+            at(v - 1, "r0", c)
+            ts(R("R0U", CL * c, CL * c + CL), o, 2048.0, Op.add)
+            at(v, "rt")
+            tr(R("RT", CL * c, CL * c + CL), o)
+
+    pre(0)
+    for v in range(VI):
+        O, Z, last = "O%d" % v, "Z%d" % v, v == VI - 1
+        kd, ke = R("p5", 0, 256), R("p5", 256, 512)
+        if v == 0:
+            at(v, "oh")
+            tables()
+        at(v, "oc")
+        ts(R("OC"), R("U%d" % v), -2048.0, Op.add)
+        tr(R("OT"), R("OC"))
+        at(v, "u")
+        mm([(R("p6", 0, 256), R("BOH"), R(Z), True, False), (R("p6", 0, 256), R("BO1"), R("CM"), False, True)])
+        mm([(kd, R("IP"), R("KT"), True, False)], ("open", "d%d" % v))
+        a1, gs, ab = [], [], []
+        for c in range(NCH):
+            two = v and c == 0 and PARAM["split"]
+            for a, n in ([(0, CL // 2), (CL // 2, CL // 2)] if two else [(CL * c, CL)]):
+                if v:
+                    at(v, "ao2" if two and a else "ao", c)
+                    tt(R("AO", 16 * a, 16 * (a + n)), X(CG, R("R0U", a, a + n)), R("PB", 16 * a, 16 * (a + n)), Op.max)
+                    a1.append(len(ops) - 1)
+                    o = R("p4", a, a + n)
+                    at(v, "ne", c)
+                    mm([(o, bview("B1H", k), R("AO", 16 * a + k, 16 * (a + n), 16), k == 0, False) for k in range(16)]
+                       + [(o, R("IL"), R("LB", a, a + n), False, False), (o, R("IP"), R("CK", 128, 128 + n), False, True)])
+                    at(v, "nu", c)
+                    ts(R("NU", a, a + n), o, 2048.0, Op.add)
+                    at(v, "rt")
+                    tr(R("NT", a, a + n), o)
+                at(v, "xg", c)
+                lin(R("XG", 16 * a, 16 * (a + n)), X(XA, R("NU" if v else "R0U", a, a + n)), 1.0, 0.0, PARAM["xg"][v][c])
+            gs.append(len(ops) - 1)
+            at(v, "d1", c)
+            ab.append(dist("XG", Z, c, R("p5", CL * c, CL * c + CL), "B16", ("acc", "d%d" % v)))
+        chain(a1)
+        weave(gs, ab, PARAM["ahead"][0])
+        if v == 0:
+            tables2()
+        at(v, "pr")
+        tt(R("PR"), R(O), R("p6", 0, 256), Op.mult)
+        ts(R("QQ"), R("PR"), 5, Op.arith_shift_right, 4095, Op.bitwise_and)
+        ts(R("p6", 0, 256), R("QQ"), K37, Op.add)
+        at(v, "s1")
+        best(kd, [("RT", "SL", 0), ("OT", "SL2", 256)])
+        tolist("ST", "P4H", 0, 2, 256)
+        at(v, "s1b")
+        ts(R("LI", 0, 32), R("p3", 256, 288), 2048.0, Op.add)
+        cp(R("MV"), X(R("MI"), li(0)))
+        cp(R("MU"), X(R("MI"), li(0)) if PARAM["mu"] else R("MV"))
+        tt(R("PR2"), X(IOB, li(1)), R("MV"), Op.mult)
+        ts(R("QQ2"), R("PR2"), 5, Op.arith_shift_right, 4095, Op.bitwise_and)
+        tt(R("SV"), R("QQ2"), R("MV"), Op.add)
+        cp(R("SU"), R("SV"))
+        at(v, "c")
+        tt(R("SL3"), R("NT" if v else "RT"), R("p7", 256, 512), Op.mult)
+        scan(R("ST", 512, 768), R("NF"), R("SL3"), 0.0, Op.mult, Op.add)
+        tolist("ST", "P4H", 512, 1, 288)
+        at(v, "c2")
+        tt(ty(5), R("p3", 256, 272), R("AL", 48, 64), Op.subtract)
+        ts(li(2), R("p3", 288, 304), 2048.0, Op.add)
+        ts(ty(0), li(2), -2048.0, Op.add)
+        ts(ty(1), R("p3", 304, 320), TWX, Op.is_le, 8192.0, Op.mult)
+        tt(R("CB"), ty(0), ty(1), Op.add)
+        at(v, "mask")
+        act(R("MASK"), kd, Act.Relu, 16384.0, col(12))
+        at(v, "fact")
+        tt(R("p6", 0, 256), R("p6", 0, 256), R("MASK"), Op.min)
+        tt(R("NN"), R("p6", 0, 256), R(O), Op.add)
+        ts(R("N%d" % v), R("NN"), 4095, Op.bitwise_and)
+        if last:
+            cp(R("MASK"), R("N%d" % v))
+            dma(R("yo"), R("MASK"), 131072)
+        else:
+            cp(R("V%d" % v), R("N%d" % v))
+            rdma([(R("U%d" % (v + 1)), R("V%d" % v)), (R("O%d" % (v + 1)), R("N%d" % v))], "ao%d" % (v + 1))
+        mm([(ke, R("IP"), R("KT"), True, False)], ("open", "e%d" % v))
+        at(v, "crep")
+        cp(R("CREP"), X(IOA, li(2)))
+        tt(R("DD"), X(CG, li(0)), R("CREP"), Op.subtract)
+        at(v, "hit")
+        act(R("A1"), R("DD"), Act.Abs, 1.0, -0.09375)
+        act(R("HIT"), R("A1"), Act.Relu, -2.0, 1.1875)
+        act(R("FL"), R("A1"), Act.Relu, -32.0, 2.0)
+        act(R("EMP"), R("MV"), Act.Relu, -1.0, 0.0)
+        lin(R("MP"), R("MV"), 1.0, -2047.875, "S")
+        lin(R("M1V"), R("MV"), 1.0, 1.0, "S")
+        at(v, "mt")
+        tr(R("MT"), R("MP"))
+        at(v, "hit")
+        mm([(ke, R(a), R(b), False, False) for a, b in (("IK", "HIT"), ("IKN", "EMP"), ("IQ", "FL"), ("IR", "FL"))], ("acc", "e%d" % v))
+        at(v, "eq")
+        x, eqs = 0, []
+        for b in range(15):
+            n = 240 - 16 * b
+            ts(R("EQ", x, x + n), R("CREP", 256 - n, 256), R("CB", b, b + 1), Op.is_equal, -1.0, Op.mult)
+            eqs.append((n, R("EQ", x, x + n)))
+            x += n
+        mm([(R("p5", 512 - n, 512), R("BOK"), e, False, False) for n, e in eqs], ("acc", "e%d" % v))
+        at(v, "eqd")
+        tt(R("EQ0"), X(R("CB"), li(6)), R("CREP"), Op.is_equal)
+        tt(R("EQD"), R("EQ0"), R("p6", 256, 512), Op.mult)
+        mm([(ke, R("BOK"), R("EQD"), False, False)], ("acc", "e%d" % v))
+        at(v, "alt")
+        tt(R("DC"), X(XA, li(2)), R(Z), Op.subtract)
+        act(R("DC2"), R("DC"), Act.Abs, 2.0, 2 * ZO)
+        mm([(R("p4", 256, 512), R("IP"), R("DC2"), True, False), (R("p4", 256, 512), R("INH"), R(Z), False, True)])
+        lin(R("XW", 0, 256), R("p4", 256, 512), 1.0, ZO + 0.5, "S")
+        a1, gs, ab = [], [], []
+        for c in range(NCH):
+            xg = R("XG", CE * c, CE * c + CE)
+            at(v, "xm", c)
+            lin(xg, X(XA, R("MU", CL * c, CL * c + CL)), 1.0, 0.0, PARAM["xm"][v][c])
+            gs.append(len(ops) - 1)
+            at(v, "xs", c)
+            tt(xg, X(XD, R("SU", CL * c, CL * c + CL)), xg, Op.min)
+            a1.append(len(ops) - 1)
+            at(v, "d3", c)
+            ab.append(dist("XG", Z, c, R("p5", 256 + CL * c, 256 + CL * c + CL), "BN16", ("acc", "e%d" % v)))
+        chain(a1)
+        weave(gs, ab, PARAM["ahead"][1])
+        at(v, "s2")
+        best(ke, [("MT", "SL", 512)])
+        ts(R("p6", 0, 256), ke, TKX, Op.is_gt)
+        tolist("ST", "P4H", 512, 1, 288)
+        mx = R("p3", 304, 320)
+        at(v, "s2a")
+        cp(R("MI16"), mx)
+        ts(R("WINB"), mx, 65600.0, Op.is_gt)
+        tt(ty(2), mx, R("MI16"), Op.is_equal)
+        tt(ty(5), ty(5), R("WINB"), Op.mult)
+        tt(ty(2), ty(2), ty(5), Op.mult)
+        tt(ty(2), ty(2), R("AL", 32, 48), Op.add)
+        cp(li(3), ty(2))
+        at(v, "s2b")
+        ts(li(4), R("p3", 288, 304), 2048.0, Op.add)
+        tt(R("DL"), X(IOA, li(4)), R("MP"), Op.subtract)
+        tt(R("DL"), R("DL"), R("p6", 0, 256), Op.mult)
+        tt(X(R("CT"), li(3)), R("DL"), R("MP"), Op.add)
+        at(v, "s2b" if last else "z")
+        ts(ty(3), mx, TKX, Op.is_gt)
+        tt(ty(4), R("p3", 288, 304), R("AL", 16, 32), Op.subtract)
+        tt(ty(4), ty(4), ty(3), Op.mult)
+        tt(ty(4), ty(4), R("AL", 0, 16), Op.add)
+        cp(li(5), ty(4))
+        tt(R("DC"), X(XZ, li(5)), R(Z), Op.add)
+        ts(R("Y%d" % v), R("DC"), 0.5, Op.mult, ZO / 2 - 0.25, Op.add)
+        if last:
+            ops[-1]["slot"] = ops[-2]["slot"] = cur[0] = (v, "zl", 0)
+            ts(R("SV"), R("Y%d" % v), -ZO, Op.add)
+            dma(R("yz"), R("SV"), 131072)
+        else:
+            rdma([(R("Z%d" % (v + 1)), R("Y%d" % v))], "az%d" % (v + 1))
+            at(v, "a")
+            mm([(R("p4", 256, 272), R("BO1"), R("WINB"), True, True)])
+            red(AI, R("p4", 256, 272))
+            tt(AC, AC, AI, Op.add)
+            cp(R("CI", 3, 4), AC)
+            ts(R("CI", 4, 5), R("CI", 3, 4), 127, Op.bitwise_and)
+            ts(TWX, R("CI", 4, 5), 16.0, Op.mult, T1X, Op.add)
+        at(v, "kml" if last else "km")
+        tt(R("KM"), R("M1V"), R("p6", 0, 256), Op.mult)
+        mm([(R("p4", 256, 512), R("WB32"), R("KM"), True, True)])
+        lin(R("YV"), R("p4", 256, 512), 1.0, 0.0, "S")
+        at(v, "ytl" if last else "yt")
+        cp(X(R("YT"), li(5)), R("YV"))
+        if not last:
+            pre(v + 1)
+
+    at(VI - 1, "end")
+    dma(R("RT"), R("YT", 256, 256 + W, 1, (0, 128, 16)), 131072)
+    ts(R("NT"), R("MCOL"), -1.0, Op.mult, 2048.0, Op.add)
+    ts(R("MCOL"), R("MCOL"), 1.0, Op.add)
+    for c in range(NCH):
+        at(VI - 1, "fin", c)
+        tt(R("PG", CE * c, CE * c + CE), X(CG, R("REPU", CL * c, CL * c + CL)), R("OH", CE * c, CE * c + CE), Op.mult)
+        o = R("p%d" % c, 0, CL)
+        extract_s(o, "B32N", "PG", c)
+        s = lambda n: R(n, CL * c, CL * c + CL)
+        at(VI - 1, "out", c)
+        tt(s("DD"), o, s("NT"), Op.subtract)
+        ts(s("A1"), o, -1.0, Op.mult, 12582912.0 + 2048.0, Op.add)
+    lin(R("MT"), R("A1"), 1.0, -12582912.0, "S")
+    dma(R("yr"), R("MT"), 131072, "S")
+    ts(R("p7", 0, 256), R("DD"), 0.0, Op.is_equal)
+    ts(R("p7", 256, 512), R("DD"), -0.125, Op.is_equal)
+    tt(R("DL"), R("RT"), R("p7", 0, 256), Op.mult)
+    tt(R("p7", 256, 512), R("MCOL"), R("p7", 256, 512), Op.mult)
+    tt(R("KM"), R("DL"), R("p7", 256, 512), Op.add)
+    dma(R("yc"), R("KM"), 131072)
+    return ops
+
+
+def depend(ops):
+    seen = {}
+    for i, o in enumerate(ops):
+        dep = {}
+        for k in o["prev"]:
+            dep[k] = None
+        for w, lst in ((True, o["wr"]), (False, o["rd"])):
+            for a in lst:
+                pl, ph = (a[5] or (0, 128))[:2]
+                for j, w2, lo, hi, ql, qh in seen.get(a[1], []):
+                    if ph <= ql or qh <= pl:
+                        continue
+                    p = ops[j]
+                    if o["acc"] and p["acc"] and o["acc"][1] == p["acc"][1] and p["acc"][0] == "acc":
+                        continue
+                    if lo < a[3] and a[2] < hi and (w or w2):
+                        dep[j] = bool(dep.get(j)) or (w2 and not w)
+        o["dep"] = dep
+        o["banks"] = sorted(set([a[1] for a in o["wr"] + o["rd"] if inps(a)]))
+        for w, lst in ((True, o["wr"]), (False, o["rd"])):
+            for a in set(lst):
+                s = seen.setdefault(a[1], [])
+                if w and a[4] == 1 and a[5] is None and not o["acc"]:
+                    s[:] = [x for x in s if not (a[2] <= x[2] and x[3] <= a[3] and x[0] != i)]
+                s.append((i, w, a[2], a[3]) + (a[5] or (0, 128))[:2])
+
+
+def tag(o):
+    w, r = o["wr"][0], o["rd"][0] if o["rd"] else ("", "", 0)
+    s = lambda a: a[1].rstrip("01234") if a[1][0] != "p" else a[1]
+    return "%s %s%d %s" % (o["kind"], s(w), w[2], s(r) if r[1] else "")
+
+
+def lat(o):
+    return 1.6 + o["lat"] / DBW if o["kind"] == "dma" else o["lat"]
+
+
+def rank_of_op(ops, succ, pr, i):
+    if PARAM["slots"] and ops[i]["slot"] is not None:
+        v, name, c = ops[i]["slot"]
+        return -(40.0 * v + SLOT.get("%s%d" % (name, c), SLOT[name] + c * SLOT.get(name + "+", 0.0))) - 1e-4 * i
+    c = min(ops[i]["cost"].values())
+    if succ[i] and PARAM["slots"]:
+        return c + max([pr[j] + (0.0 if ops[j]["dep"][i] is None else lat(ops[i]) + LATX) for j in succ[i]])
+    return c + max([pr[j] + (0.0 if ops[j]["dep"][i] is None else lat(ops[i]) + LATX) for j in succ[i]] + [lat(ops[i])])
+
+
+def after(ops, o, e, eng, end):
+    t = 0.0
+    for j, raw in o["dep"].items():
+        if raw is None and eng[j] == e:
+            continue
+        if eng[j] != e or ops[j]["sem"]:
+            t = max(t, end[j] + LATX)
+        elif raw:
+            t = max(t, end[j] + LATS)
+    return t
+
+
+def finish(o, t, c, pipe):
+    if o["kind"] == "dma":
+        pipe[0] = max(pipe[0], t + 1.6) + o["lat"] / DBW
+        return pipe[0]
+    return t + c + o["lat"]
+
+
+def schedule(ops, succ, pr, look):
+    n = len(ops)
+    left, todo, vq = [len(o["dep"]) for o in ops], [i for i in range(n) if not ops[i]["dep"]], []
+    while todo and PARAM["strict"]:
+        i = max(todo, key=lambda x: pr[x])
+        todo.remove(i)
+        if PARAM["strict"] and ops[i]["slot"] is not None and list(ops[i]["cost"]) == ["V"]:
+            vq.append(i)
+        for j in succ[i]:
+            left[j] -= 1
+            if not left[j]:
+                todo.append(j)
+    turn, fixed = [0], set(vq)
+    eng, start, end = [None] * n, [0.0] * n, [0.0] * n
+    left = [len(o["dep"]) for o in ops]
+    ready = {}
+    for i in range(n):
+        if not left[i]:
+            ready[i] = [(0.0, e, c) for e, c in ops[i]["cost"].items()]
+    free = {e: 0.0 for e in "VSPGY"}
+    pipe, order = [0.0], []
+    last, extra = {}, [[] for _ in ops]
+    while ready:
+        cand = []
+        for i, l in ready.items():
+            if i in fixed and i != vq[turn[0]]:
+                continue
+            for t, e, c in l:
+                t = max(t, free[e])
+                for b in ops[i]["banks"]:
+                    for e2, j in last.get(b, {}).items():
+                        if e2 != e and end[j] + LATX > t:
+                            t = end[j] + LATX
+                cand.append((t, -pr[i], i, e, c))
+        t, _, i, e, c = min(cand)
+        for _ in range(3):
+            better = [x for x in cand if x[3] == e and x[1] < -pr[i] - 1e-9 and x[0] < t + look * c]
+            if not better:
+                break
+            t, _, i, e, c = min(better, key=lambda x: x[1])
+        if len(ready[i]) > 1:
+            t, _, i, e, c = min([x for x in cand if x[2] == i], key=lambda x: x[0] + x[4])
+        eng[i], start[i], end[i] = e, t, finish(ops[i], t, c, pipe)
+        free[e] = t + c
+        for b in ops[i]["banks"]:
+            extra[i] += [j for e2, j in last.setdefault(b, {}).items() if e2 != e]
+            last[b][e] = i
+        order.append(i)
+        turn[0] += i in fixed
+        del ready[i]
+        for j in succ[i]:
+            left[j] -= 1
+            if not left[j]:
+                ready[j] = [(after(ops, ops[j], e2, eng, end), e2, c2) for e2, c2 in ops[j]["cost"].items()]
+    return order, eng, start, end, extra
+
+
+def replay(ops, costs, order, eng, extra):
+    end, free, pipe = [0.0] * len(ops), {e: 0.0 for e in "VSPGY"}, [0.0]
+    for i in order:
+        e = eng[i]
+        t = max([free[e], after(ops, ops[i], e, eng, end)] + [end[j] + LATX for j in extra[i]])
+        free[e] = t + costs[i][e]
+        end[i] = finish(ops[i], t, costs[i][e], pipe)
+    return max(end)
+
+
+def plan():
+    ops = build(*MODELS[0])
+    costs = [[o["cost"] for o in build(*m)] for m in MODELS]
+    depend(ops)
+    n = len(ops)
+    succ = [[] for _ in ops]
+    for i, o in enumerate(ops):
+        for j in o["dep"]:
+            succ[j].append(i)
+    pr, topo_order, left = [0.0] * n, [i for i in range(n) if not ops[i]["dep"]], [len(o["dep"]) for o in ops]
+    for i in topo_order:
+        for j in succ[i]:
+            left[j] -= 1
+            if not left[j]:
+                topo_order.append(j)
+    assert len(topo_order) == n
+    for i in reversed(topo_order):
+        pr[i] = rank_of_op(ops, succ, pr, i)
+    tags = [tag(o) for o in ops]
+    pool = sorted(set(tags)) + 3 * sorted(set([t for t in tags if tags.count(t) >= 4]))
+    x, best, boost = [PARAM["seed"]], None, dict(BOOST)
+
+    def draw():
+        x[0] = (x[0] * 1103515245 + 12345) % 2147483648
+        return x[0] / 2147483648.0
+
+    for it in range(PARAM["iters"]):
+        trial = dict(boost)
+        for _ in range((1, 1, 2, 3, 5)[int(5 * draw())] if it else 0):
+            t = pool[int(len(pool) * draw())]
+            trial[t] = round(trial.get(t, 0.0) + (draw() + draw() - 1.0) * (1.5, 5.0, 15.0, 35.0)[int(4 * draw())], 1)
+        order, eng, start, end, extra = schedule(ops, succ, [p + trial.get(t, 0.0) for p, t in zip(pr, tags)], PARAM["look"])
+        ts = [replay(ops, c, order, eng, extra) for c in costs]
+        val = sum([a / b for a, b in zip(ts, WEIGHT)])
+        if best is None or val <= best[0]:
+            best, boost = (val, order, eng, start, end, ts, extra), trial
+    ops[0]["boost"] = boost
+    _, order, eng, start, end, ts, extra = best
+    for i in range(n):
+        for j in extra[i]:
+            ops[i]["dep"].setdefault(j, False)
+        ops[i]["eng"], ops[i]["start"], ops[i]["end"], ops[i]["ts"] = eng[i], start[i], end[i], ts
+    close = {}
+    for i in order:
+        if ops[i]["acc"]:
+            close[ops[i]["acc"][1]] = i
+    for i in close.values():
+        ops[i]["args"] = ops[i]["args"][:-1] + [ops[i]["args"][-1][:4] + (True,)]
+    pos, at = {}, {e: 0 for e in "VSPGY"}
+    for i in order:
+        if not ops[i]["sem"]:
+            at[ops[i]["eng"]] += 1
+            pos[i] = at[ops[i]["eng"]]
+    know = {e: {} for e in "VSPGY"}
+    for i in order:
+        o = ops[i]
+        e, k, need = o["eng"], know[o["eng"]], []
+        for j in sorted(o["dep"], key=lambda j: -ops[j]["end"]):
+            p = ops[j]
+            if o["dep"][j] is None and p["eng"] == e:
+                continue
+            if p["sem"]:
+                key, val = ("D", j), 1
+            elif p["eng"] != e or o["dep"][j] or o["sem"] or (PARAM["waw"] and e != "P"):
+                key, val = p["eng"], pos[j]
+            else:
+                continue
+            if k.get(key, 0) >= val:
+                continue
+            need.append(j)
+            k[key] = val
+            if p["kind"] != "rdma":
+                for kk, vv in p["know"].items():
+                    k[kk] = max(k.get(kk, 0), vv)
+            p["inc"] = True
+        o["need"], o["know"] = need, dict(k)
+    at = {e: 0 for e in "VSPGY"}
+    for i in order:
+        if ops[i].get("inc") and not ops[i]["sem"]:
+            at[ops[i]["eng"]] += 1
+            ops[i]["val"] = at[ops[i]["eng"]]
+    return [ops[i] for i in order], ops, at
+
+
+PLAN = []
+
+
+def rank_program(g, core, T, topo):
+    rank = T.rank_of(core)
+    if rank is None:
+        return
+    if not PLAN:
+        PLAN.append(plan())
+    order, ops, total = PLAN[0]
+    nxt = T.cores[(rank + 1) % NR]
+    rid, pid = topo.addr(nxt)[0], topo.addr(nxt)[1]
+    mask = topo.mask(core, nxt)
+    ne = len(topo.engines(core, nxt))
+    Q = {"V": g.vector, "S": g.scalar, "P": g.tensor, "G": g, "Y": g.sync}
+    sent, outs = 0, []
+    for o in order:
+        e, a, k = o["eng"], o["args"], o["kind"]
+        q = Q[e]
+        for j in o["need"]:
+            p = ops[j]
+            if p["kind"] == "rdma":
+                q.wait_ge(T.sem[p["sem"][0]], ne * p["sem"][1])
+            elif p["sem"]:
+                q.wait_ge(T.sem[p["sem"][0]], 16)
+            else:
+                q.wait_ge(T.sem["s" + p["eng"]], p["val"])
+        if k == "rdma":
+            for dst, src in a:
+                g.remote_dma(ap(T, dst), ap(T, src), T.sem[o["sem"][0]], T.sem.sent, pid, rid, mask)
+                sent += ne
+            continue
+        if k == "dma":
+            q.dma_start(ap(T, a[0]), ap(T, a[1])).then_inc(T.sem[o["sem"][0]], 16)
+            if not o.get("inc"):
+                outs.append(o["sem"][0])
+            continue
+        if k == "mm":
+            for m in a:
+                ins = q.matmul(ap(T, m[0]), ap(T, m[1]), ap(T, m[2]), m[3], m[4])
+        elif k == "tt":
+            ins = q.tensor_tensor(ap(T, a[0]), ap(T, a[1]), ap(T, a[2]), a[3])
+        elif k == "ts":
+            if a[5] is None:
+                ins = q.tensor_scalar(ap(T, a[0]), ap(T, a[1]), ap(T, a[2]), None, a[4])
+            else:
+                ins = q.tensor_scalar(ap(T, a[0]), ap(T, a[1]), ap(T, a[2]), ap(T, a[3]), a[4], a[5])
+        elif k == "cp":
+            ins = q.tensor_copy(ap(T, a[0]), ap(T, a[1]))
+        elif k == "ramp" and e == "G":
+            ins = g.iota(ap(T, a[0]), a[4], a[5], 0, allow_small_or_imprecise_dtypes=True)
+        elif k == "lin" or k == "ramp":
+            if e == "S":
+                ins = q.activation(ap(T, a[0]), ap(T, a[1]), Act.Identity, bias=a[3], scale=a[2])
+            elif a[2] == 1.0 and a[3] == 0.0:
+                ins = q.tensor_copy(ap(T, a[0]), ap(T, a[1]))
+            else:
+                ins = q.tensor_scalar(ap(T, a[0]), ap(T, a[1]), a[2], a[3], Op.mult, Op.add)
+        elif k == "act":
+            ins = q.activation(ap(T, a[0]), ap(T, a[1]), a[2], bias=ap(T, a[4]), scale=a[3])
+        elif k == "scan":
+            ins = q.tensor_tensor_scan(ap(T, a[0]), ap(T, a[1]), ap(T, a[2]), a[3], a[4], a[5])
+        elif k == "tr":
+            ins = q.transpose(ap(T, a[0]), ap(T, a[1]))
+        elif k == "red":
+            ins = q.tensor_reduce(ap(T, a[0]), ap(T, a[1]), AxisListType.X, Op.add)
+        elif k == "ms":
+            ins = q.memset(ap(T, a[0]), a[1])
+        elif k == "iota":
+            if SCRATCH[a[0][1]][2] == I32:
+                ins = g.iota(ap(T, a[0]), a[1], a[2], a[3])
+            else:
+                ins = g.iota(ap(T, a[0]), a[1], a[2], a[3], allow_small_or_imprecise_dtypes=True)
+        else:
+            ins = g.affine_select(ap(T, a[0]), ap(T, a[0]), a[1], a[2], 0.0, a[3], a[4])
+        if o.get("inc"):
+            ins.then_inc(T.sem["s" + e], 1)
+    g.wait_ge(T.sem.sent, sent)
+    for s in outs:
+        g.sync.wait_ge(T.sem[s], 16)

@@ -13,63 +13,54 @@ def _sb(dtype, cols, names):
 
 _sb(BF, 256 + 2 * W, "XW")
 _sb(I32, W, "MI")
-_sb(F32, W, "PG")
+_sb(F32, W, "PG TT")
 _sb(F32, W + 256, "CT YT")
-_sb(F32, W + 2048, "IOT")
-_sb(BF, W, "OH XG AB TT PB")
-_sb(F16, W, "AO")
-_sb(BF, 2048, "EQ")
-_sb(F16, 768, "ST")
+_sb(BF, W, "OH XG AB EQ")
+_sb(F16, W, "PB AO")
+_sb(F16, 2048, "RB")
+_sb(BF, 2048, "TRI")
+_sb(BF, 1024, "SEL")
+_sb(BF, 1104, "CK")
+_sb(F32, 768, "ST BB")
 _sb(F16, 512, "P4H")
-_sb(F32, 256, "RT NT MT MX MV SV DD A1 MP M1V DL KM YV DC MASK RMM MCOL")
-_sb(I32, 256, "PR PR2 QQ QQ2 NN O0 O1 O2 O3 O4 N0 N1 N2 N3 N4")
+_sb(F32, 256, "MX AA MV SV DD MP DL YV DC MASK RMM KET MX2 EQT I6 I7 Y0 RT MC MC8 C1 FA FB")
+_sb(I32, 256, "RP PR PR2 QQ QQ2 NN O0 O1 O2 O3 O4 N0 N1 N2 N3 N4")
 _sb(U16, 256, "REPU R0U NU MU SU U0 U1 U2 U3 U4 V0 V1 V2 V3")
-_sb(F16, 256, "CREP OC OT NF SL SL2 SL3 Z0 Z1 Z2 Z3 Z4 Y0 Y1 Y2 Y3 Y4")
-_sb(BF, 256, "ZIN KT CM HIT FL EMP EQ0 EQD DC2 LB")
-_sb(BF, 1280, "RC")
-_sb(BF, 128, "GG")
-_sb(BF, 384, "CK")
-_sb(F32, 160, "J32 B32 B32N")
-_sb(BF, 160, "B16 BN16 BQ")
-_sb(F16, 160, "B1H")
-_sb(F32, 128, "BO32 WB32 G8")
-_sb(F32, 512, "P4")
-_sb(BF, 128, "BO1 BOK IP IK IKN IQ IR IL")
-_sb(F16, 128, "INH BOH")
-_sb(F32, 128, "TY")
-_sb(F32, 64, "AL")
+_sb(F16, 256, "CREP FLH MH SL KP KM H1 H2 RH0 FL0 OWN Z0 Z1 Z2 Z3 Z4 Y0H Y1H Y2H Y3H Y4H")
+_sb(BF, 256, "ZIN ZT KT1 HC HF EMP DC2")
+_sb(F32, 160, "J32 B32")
+_sb(BF, 3 * 160, "BB16")
+_sb(F16, 4 * 160, "BH16")
+_sb(BF, 6 * 128, "IB")
+_sb(F16, 6 * 128, "IH")
+_sb(F32, 128, "BO32 G8 BOA KT3")
+_sb(F32, 64, "TY")
+_sb(F32, 80, "AL")
 _sb(F32, 16, "CB COL")
-_sb(BF, 16, "WINB")
-_sb(I32, 16, "CI MI16")
-_sb(U16, 112, "LI")
+_sb(F16, 80, "LH")
+_sb(I32, 16, "CI TH")
+_sb(U16, 80, "LI")
 for _i in range(8):
     SCRATCH["p%d" % _i] = ("psum", [128, 512], F32)
 
-DSEMS = ["d%d" % i for i in range(24)]
+DSEMS = ["d%d" % i for i in range(16)]
 SEMAPHORES = ["sV", "sS", "sP", "sG", "sent"] + DSEMS + ["ao%d" % v for v in range(1, VI)] + ["az%d" % v for v in range(1, VI)]
 
 SHAPES = {"feat": 4096, "memb": 4096, "rep": 4096, "fact": 256, "z": 256, "thr": 2, "yc": 4096, "yr": 4096, "yo": 256, "yz": 256}
 SIZE = {F32: 4, I32: 4, BF: 2, F16: 2, U16: 2}
 Op, Act = AluOpType, ActivationFunctionType
 
-LATX, LATS, DBW = 0.12, 0.07, 190000.0
-MODELS = [(0.00104, 0.00052, 1.56, 3.8), (0.0009, 0.00045, 1.2, 2.5), (0.0012, 0.0006, 1.9, 5.0), (0.0009, 0.0006, 1.2, 5.0)]
-WEIGHT = [200.0, 150.0, 260.0, 180.0]
-PARAM = {"nch": 4, "look": 0.6, "waw": False, "seed": 1, "iters": 1100, "mu": False, "ramp": "GS", "ahead": [1, 2], "split": False, "strict": False, "slots": False, "dmas": "0132ab456cde7",
-         "pg": ["VSSV"] + ["SSSS"] * 4, "xg": ["SSVS"] + ["SSSV"] * 4, "xm": ["SSSS"] * 5}
-BOOST = {'mm p60 BOH': 40, 'ts QQ0 PR': 50, 'tt PR0 O': 16, 'ts p60 QQ': 20, 'ts N0 NN': 15, 'ts R0U0 p3': 40, 'ts PR0 p3': 45,
-         'tt NF0 p7': 6, 'tt p7256 p7': 7, 'tt DD0 CT': 8, 'cp LB0 QQ': 9, 'tt AO2048 CT': 10, 'tt SL0 MT': 6, 'mm p5128 B16': 5,
-         'mm p5384 BN16': 20, 'tt DC0 XW': 4.5, 'cp V0 N': 5.4, 'tt NN0 p6': 7.5, 'tt p60 p6': 10, 'tt TY64 TY': 10,
-         'lin PB3072 TT': 20, 'mm p5256 IK': 15, 'ts TY0 LI': 20, 'mm p20 GG': -30, 'tt DL0 IOT': 9, 'mm p40 B1H': 10,
-         'mm p464 B1H': 10, 'mm p4128 B1H': 10, 'mm p4192 B1H': 10}
-SLOT = {"pb": 30, "pb+": 0.1, "lb": 34.5, "lb1": 42.85, "lb2": 44.7, "lb3": 47.2, "r0": 34.4, "r01": 41.75, "r02": 42.82, "r03": 44.65,
-        "ne": -10, "rt": 9.7, "oh": 1, "oh+": 2.6, "oc": 12.2, "u": 5, "ao": 0, "ao1": 2.9, "ao2": 5.4, "ao3": 7.9, "nu": 2.8, "nu+": 2.5,
-        "xg": 2.85, "xg+": 2.52, "d1": 3, "d1+": 2.5, "pr": 7.2, "s1": 15, "s1b": 15.5, "c": 15.2, "c2": 17, "mask": 15,
-        "fact": 15.7, "crep": 17.1, "hit": 17.2, "mt": 26.3, "eq": 23, "eqd": 26, "alt": 26.2, "xm": 15.6, "xm+": 1.8, "xs": 16,
-        "xs1": 18.5, "xs2": 21.5, "xs3": 25, "d3": 16, "d3+": 2.8, "s2": 33, "s2a": 34, "s2b": 34.6, "z": 41.7, "a": 52.3,
-        "km": 44.8, "yt": 52.4, "kml": 34.7, "ytl": 36.5, "zl": 37.5, "end": 30, "fin": 36, "fin+": 1, "out": 39.5, "out+": 0.1,
-        "nm": 8, "nm+": 0.5, "tt": 12.5, "tt+": 2.0, "y0": 12, "y0+": 0.3}
+MODELS = [(0.00083, 0.00042, 1.56, 3.8, 0.2), (0.00104, 0.00052, 1.3, 3.0, 0.2), (0.00115, 0.00058, 1.9, 5.0, 0.2), (0.0009, 0.00045, 1.2, 2.5, 0.3)]
+WEIGHT = [160.0, 180.0, 240.0, 165.0]
+DBW = 190000.0
+PARAM = {"rot": 3, "look": 0.6, "seed": 1, "iters": 800,
+         "a": ["VSVS"] + ["SSSS"] * 4, "c": ["SVSV"] + ["SSVS"] * 4, "d": ["SSSS"] * 5}
+BOOST = {t: 8.0 for t in ("f tt NN0", "f ts N0", "f lin V0", "f tt p40", "f tt p4128", "f rdma U0", "f tt PR0", "f ts QQ0",
+                          "f act MASK0", "f act MASK128", "z mm p40", "z lin L32", "z mm p30")}
 ZO = 1536.0
+KS = 8192.0
+BAND = 131072.0
+RND = 12582912.0
 
 
 def R(name, lo=0, hi=None, st=1, p=None):
@@ -112,9 +103,9 @@ def ap(T, a):
     return t[ps, a[2]:a[3]] if a[4] == 1 else t[ps, a[2]:a[3]:a[4]]
 
 
-def build(CY, PCY, GA, SC):
+def build(CY, PCY, GA, SC, LAT=0.0):
     ops = []
-    nd, cur = [0], [None]
+    nd, cur, turns, starts = [0], ["s", "0", 0], [0], []
 
     def add(cost, kind, args, wr, rd, acc=None, lat=0.0, sem=None):
         rr = []
@@ -125,25 +116,11 @@ def build(CY, PCY, GA, SC):
         for a in wr:
             ww.append(regs(a)[0])
             rr += regs(a)[1:]
-        ops.append({"cost": cost, "kind": kind, "args": args, "wr": ww, "rd": rr, "acc": acc, "lat": lat, "sem": sem, "prev": [], "slot": cur[0]})
-
-    def at(v, name, c=0):
-        cur[0] = (v, name, c)
+        ops.append({"cost": cost, "kind": kind, "args": args, "wr": ww, "rd": rr, "acc": acc, "lat": lat, "sem": sem, "prev": [], "part": cur[0] + cur[1], "vis": cur[2]})
 
     def chain(lst):
         for a, b in zip(lst, lst[1:]):
             ops[b]["prev"].append(a)
-
-    def weave(gs, ab, ahead):
-        seq = []
-        for c in range(len(gs) + 1):
-            if c < len(gs) and list(ops[gs[c]]["cost"]) == ["S"]:
-                seq.append(gs[c])
-            if c >= ahead:
-                seq += ab[c - ahead]
-        for c in range(len(gs) + 1 - ahead, len(gs)):
-            seq += ab[c]
-        chain(seq)
 
     def vcost(out, ins, two=False):
         if out[0] == "X":
@@ -166,22 +143,19 @@ def build(CY, PCY, GA, SC):
     def ts(out, a, s1, op0, s2=None, op1=None):
         add({"V": vcost(out, [a])}, "ts", (out, a, s1, s2, op0, op1), [out], [a, s1, s2])
 
-    def cp(out, a):
-        add({"V": vcost(out, [a])}, "cp", (out, a), [out], [a])
-
-    def lin(out, a, scale, bias, eng="VS"):
+    def lin(out, a, scale=1.0, bias=0.0, eng="VS", fn=Act.Identity):
         c = {}
         if "V" in eng:
             c["V"] = vcost(out, [a])
         if "S" in eng:
             c["S"] = scost(out, a)
-        add(c, "lin", (out, a, scale, bias), [out], [a])
+        add(c, "lin", (out, a, scale, bias, fn), [out], [a, scale])
 
     def act(out, a, fn, scale=1.0, bias=0.0):
         add({"S": scost(out, a)}, "act", (out, a, fn, scale, bias), [out], [a, bias])
 
-    def scan(out, d0, d1, init, op0, op1):
-        add({"V": vcost(out, [d0, d1])}, "scan", (out, d0, d1, init, op0, op1), [out], [d0, d1])
+    def scan(out, d0, d1, op0, op1):
+        add({"V": vcost(out, [d0, d1])}, "scan", (out, d0, d1, 0.0, op0, op1), [out], [d0, d1])
 
     def tr(out, a):
         add({"V": vcost(out, [a])}, "tr", (out, a), [out], [a])
@@ -193,18 +167,13 @@ def build(CY, PCY, GA, SC):
         add({"V": vcost(out, [out])}, "ms", (out, val), [out], [])
 
     def mm(lst, acc=None):
+        if len(lst[0]) == 3:
+            lst = [m + (i == 0 and not (acc and acc[0] == "acc"), i == len(lst) - 1 and not acc) for i, m in enumerate(lst)]
         c = sum([max(64, cnt(m[2])) * (4 if width(m[2]) == 4 else 1) for m in lst]) * PCY + 0.03
-        add({"P": c}, "mm", lst, [m[0] for m in lst], [m[1] for m in lst] + [m[2] for m in lst] + ([R("p5")] if acc and acc[0] == "open" else []), acc)
+        add({"P": c}, "mm", lst, [m[0] for m in lst], [m[1] for m in lst] + [m[2] for m in lst], acc)
 
-    def iota(out, pat, base, ch):
+    def iota(out, pat, base, ch=0):
         add({"G": 0.13 + 2 * cnt(out) * CY}, "iota", (out, pat, base, ch), [out], [])
-
-    def ramp(out, a, shift, pat, base):
-        c = {"G": 0.13 + 2 * cnt(out) * CY, "S": scost(out, a), "V": vcost(out, [a])}
-        add({e: c[e] for e in PARAM["ramp"]}, "ramp", (out, a, 1.0, float(shift), pat, base), [out], [a])
-
-    def asel(out, pat, cmp, base, ch):
-        add({"G": 0.17 + 2 * cnt(out) * CY}, "asel", (out, pat, cmp, base, ch), [out], [out])
 
     def dma(out, a, nbytes, q="Y"):
         add({q: 0.06}, "dma", (out, a), [out], [a], lat=nbytes, sem=(DSEMS[nd[0]], 16))
@@ -213,416 +182,356 @@ def build(CY, PCY, GA, SC):
     def rdma(pairs, sem):
         add({"G": 0.3 * len(pairs)}, "rdma", pairs, [x[0] for x in pairs], [x[1] for x in pairs], lat=2.0, sem=(sem, len(pairs)))
 
-    NCH = PARAM["nch"]
-    CL = L // NCH
-    CE = 16 * CL
-    KB = 512 // CL
+    CL, CE, HL = 64, 1024, 128
     col = lambda i: R("COL", i, i + 1)
-    PM, PAR0, PAR1, NPM, K37, KP1, T1X, TKX, TWX, AC, AI = [col(i) for i in range(11)]
+    PF, PM, PG8, P32, P32B, PAR0, PAR1, NPM, KP1, T1X, TMX, TKX, TWX, AI, P256 = [col(i) for i in range(15)]
+    ci = lambda i: R("CI", i, i + 1)
     ty = lambda i: R("TY", 16 * i, 16 * i + 16)
-    li = lambda i: R("LI", 16 * i, 16 * i + 16)
+    li = lambda i, h=None: R("LI", 16 * i, 16 * i + 16) if h is None else R("LI", 16 * i + 8 * h, 16 * i + 8 * h + 8)
+    al = lambda i: R("AL", 16 * i, 16 * i + 16)
     XA, XD, XZ = R("XW", 256, 256 + W), R("XW", 256, 256 + 2 * W), R("XW", 0, 256 + W)
-    IOA, IOB = R("IOT", 0, W), R("IOT", 2048, 2048 + W)
-    CG, IJ = R("CT", 0, W), R("YT", 256, 256 + W)
-    bview = lambda n, k: R(n, 15 - k, 143 - k)
-    sub, NSUB = [0], 2
+    CG = R("CT", 0, W)
+    names = {"BKD": 0, "BN16": 1, "BN1": 2, "BHF": 0, "B16": 1, "B1H": 2, "BK1": 3}
+    ids = {"IP": 0, "IK": 1, "IKN": 2, "IBG": 3, "BOK": 4, "BO1": 5, "I1": 0, "IN1": 1, "I30": 2, "BOH": 3, "WBH": 4, "WB2": 5}
 
-    dma(R("NN"), R("rep"), 131072)
-    dma(R("O0"), R("fact"), 131072)
-    dma(R("CI", 8, 10, 1, (0, 8)), R("thr"), 64)
-    dma(R("ZIN"), R("z"), 65536)
+    def bv(n, k):
+        if n == "B32":
+            return R(n, 15 - k, 143 - k)
+        o = 160 * names[n]
+        return R("BB16" if n[1] in "KN" and n != "BK1" else "BH16", o + 15 - k, o + 143 - k)
+
+    def im(n):
+        return R("IB" if n in ("IP", "IK", "IKN", "IBG", "BOK", "BO1") else "IH", 128 * ids[n], 128 * ids[n] + 128)
+
+    C8192, C2048, CN8, CR0, CGOT = [lambda n, o=o: R("CK", o, o + n) for o in (0, 512, 768, 1024, 1088)]
+    rb = lambda r: R("RB", 128 * r, 128 * r + 128)
+
+    dma(R("RP"), R("rep"), 131072)
+    dma(R("NN"), R("fact"), 131072)
+    dma(R("ZIN"), R("z"), 65536, "S")
+    dma(R("TH", 0, 2, 1, (0, 8)), R("thr"), 64, "S")
     dma(XA, R("feat"), 1048576)
     for c in range(2):
         dma(R("MI", 2048 * c, 2048 * c + 2048), R("memb", 2048 * c, 2048 * c + 2048), 1048576)
-    dma(R("XW", 256 + W, 256 + 2 * W), R("feat"), 1048576)
+    chain([0, 1, 4, 5, 6])
 
-    iota(R("CI", 0, 1), [[0, 1]], 0, 1)
-    ts(R("CI", 1, 2), R("CI", 0, 1), 15, Op.bitwise_and)
-    ts(R("CI", 2, 3), R("CI", 0, 1), 16, Op.bitwise_and)
-    cp(PM, R("CI", 1, 2))
-    ts(PAR0, R("CI", 2, 3), 0.0, Op.is_equal)
-    ts(PAR1, R("CI", 2, 3), 16.0, Op.is_equal)
-    ts(NPM, R("CI", 1, 2), -1.0, Op.mult)
-    ts(K37, R("CI", 1, 2), 37.0, Op.mult)
-    ts(KP1, R("CI", 1, 2), 1.0, Op.add)
-    ms(R("BO32"), 1.0)
-    asel(R("BO32"), [[-16, 8], [0, 16]], Op.is_ge, 0, 1)
-    asel(R("BO32"), [[16, 8], [0, 16]], Op.is_ge, 15, -1)
-    iota(R("AL", 48, 64), [[1, 16]], 0, 0)
-    cp(li(6), R("AL", 48, 64))
-    ts(R("AL", 0, 16), R("AL", 48, 64), 16.0, Op.mult, PM, Op.add)
-    ts(R("CI", 5, 6), R("CI", 0, 1), 7, Op.bitwise_and)
-    ts(R("CI", 6, 7), R("CI", 0, 1), 8, Op.bitwise_and)
-    cp(col(13), R("CI", 5, 6))
-    ts(col(14), R("CI", 6, 7), 0.125, Op.mult)
-    ts(col(15), R("CI", 0, 1), 16.0, Op.is_ge)
-    iota(R("G8"), [[1, 8], [0, 16]], 0, 0)
-    iota(R("WB32"), [[0, 64], [1, 2]], 0, 0)
-    ts(R("G8"), R("G8"), col(13), Op.is_equal)
-    ts(R("WB32"), R("WB32"), col(14), Op.is_equal, col(15), Op.max)
-    tt(R("GG"), R("G8"), R("WB32"), Op.mult)
-    ms(R("B32"), 0.0)
-    cp(R("B32", 15, 143, 16), R("BO32", 0, 128, 16))
-    ts(R("B32N"), R("B32"), -1.0, Op.mult)
-    ts(R("B16"), R("B32"), 16.0, Op.mult)
-    ts(R("BN16"), R("B32"), -16.0, Op.mult)
-    cp(R("B1H"), R("B32"))
-    ms(R("J32"), 1.0)
-    asel(R("J32"), [[-1, 160]], Op.is_equal, 16, 1)
-    for n, s in (("IP", 1.0), ("INH", -1.0), ("IK", 65536.0), ("IKN", -65536.0), ("IQ", -0.25), ("IR", -8192.0), ("IL", -240.0)):
-        ts(R(n), R("J32", 16, 144), s, Op.mult)
+    iota(ci(0), [[0, 1]], 0, 1)
+    iota(R("J32"), [[1, 160]], -16, -1)
+    iota(R("G8"), [[1, 8], [0, 16]], 0)
+    iota(al(0), [[1, 16]], 0)
+    iota(R("I6"), [[0, 16], [1, 16]], 0)
+    iota(R("I7"), [[1, 16], [0, 16]], 0)
+    for i, (s, op) in enumerate(((15, Op.bitwise_and), (4, Op.arith_shift_right), (31, Op.bitwise_and), (16, Op.bitwise_and))):
+        ts(ci(1 + i), ci(0), s, op)
+    lin(R("COL", 0, 4), R("CI", 0, 4), eng="V")
+    ts(P32B, ci(3), -16.0, Op.add)
+    ts(PAR0, ci(4), 0.0, Op.is_equal)
+    ts(PAR1, ci(4), 16.0, Op.is_equal)
+    ts(NPM, ci(1), -1.0, Op.mult)
+    ts(KP1, ci(1), 1.0, Op.add)
+    ts(P256, ci(1), 256.0, Op.mult)
+    ts(R("J32"), R("J32"), 0.0, Op.is_equal)
+    ts(R("BO32"), R("G8"), PG8, Op.is_equal)
+    ts(R("G8"), R("G8"), PF, Op.is_equal)
     for b in range(2):
         for e in range(2):
-            o = 16 + 16 * (b - e)
-            ts(R("P4", 128 * (2 * b + e), 128 * (2 * b + e) + 128), R("J32", o, o + 128), PAR1 if b else PAR0, Op.mult)
-    cp(R("P4H"), R("P4"))
-    ms(R("CK", 0, 128), -2048.0)
-    ms(R("CK", 128, 256), -30720.0)
-    ms(R("CK", 256, 384), -256.0)
-    ts(R("BQ"), R("B32"), -0.0625, Op.mult)
-    for n, s in (("BO1", 1.0), ("BOH", 1.0), ("BOK", 65536.0)):
-        ts(R(n), R("BO32"), s, Op.mult)
-    ts(R("WB32"), R("BO32"), KP1, Op.mult)
-    cp(R("TY", 0, 2, 1, (0, 8)), R("CI", 8, 10, 1, (0, 8)))
-    mm([(R("p6", 0, 2), R("G8", 0, 128, 1, (0, 8)), R("TY", 0, 2, 1, (0, 8)), True, True)])
-    ts(T1X, R("p6", 0, 1), 16.0, Op.mult, 0.5, Op.add)
-    ts(col(12), R("p6", 0, 1), -262144.0, Op.mult, -8192.0, Op.add)
-    ts(TWX, R("p6", 0, 1), 16.0, Op.mult, 0.5, Op.add)
-    ts(TKX, R("p6", 1, 2), -16.0, Op.mult, 131072 - 15.5, Op.add)
-    ms(AC, 0.0)
-    iota(R("DL"), [[0, 16], [1, 16]], 0, 0)
-    ts(R("KM"), R("DL"), 0.0, Op.is_gt)
-    ts(R("RMM"), R("KM"), 2e9, Op.mult, -1e9, Op.add)
-    ts(R("YV"), R("DL"), PM, Op.is_gt)
-    ts(R("DC"), R("DL"), PM, Op.is_equal)
-    tt(R("p6", 256, 512), R("DC"), R("YV"), Op.subtract)
-    ts(R("KT"), R("DL"), 0.0, Op.mult, NPM, Op.add)
-    ms(R("CM"), -ZO)
-    ts(R("AL", 16, 32), R("AL", 0, 16), -2304.0, Op.add)
-    ts(R("AL", 32, 48), R("AL", 0, 16), 4096.0, Op.add)
-    ts(R("AL", 48, 64), R("AL", 0, 16), 2048.0, Op.add)
-    iota(R("MCOL"), [[1, 256]], 0, 0)
-    ts(col(11), PM, 256.0, Op.mult)
-    ts(R("MCOL"), R("MCOL"), col(11), Op.add)
-    iota(R("YT", 256, 768), [[1, 32], [256, 16]], 0, 0)
-    iota(R("IOT", 0, 512), [[1, 512]], -2048, 0)
-    for h in range(1, 8):
-        ramp(R("YT", 256 + 512 * h, 768 + 512 * h), R("YT", 256, 768), 32 * h, [[1, 32], [256, 16]], 32 * h)
-    for h in range(1, 12):
-        ramp(R("IOT", 512 * h, 512 * h + 512), R("IOT", 0, 512), 512 * h, [[1, 512]], 512 * h - 2048)
+            o, q = 16 + 16 * (b - e), 128 * (2 * b + e)
+            ts(R("P4H", q, q + 128), R("J32", o, o + 128), PAR1 if b else PAR0, Op.mult)
+    for n, s in (("IP", 1.0), ("I1", 1.0), ("IK", BAND), ("IKN", -BAND), ("IBG", -8192.0), ("IN1", -1.0), ("I30", -30.0)):
+        lin(im(n), R("J32", 16, 144), s)
+    lin(im("BOH"), R("BO32"))
+    lin(im("BOK"), R("BO32"), BAND)
+    lin(R("BOA"), R("BO32"), -1.0 / 8192)
+    ts(im("WBH"), R("BO32"), KP1, Op.mult)
+    ts(im("WB2"), R("BO32"), KP1, Op.mult, 2048.0, Op.mult)
+    ms(R("B32"), 0.0)
+    lin(R("B32", 15, 143, 16), R("BO32", 0, 128, 16), eng="V")
+    for n, s in (("B16", 0.0625), ("BKD", 16 * KS), ("B1H", 1.0), ("BN16", -16.0), ("BN1", 8192.0), ("BHF", 0.5), ("BK1", KP1)):
+        a = bv(n, 15)
+        lin(R(a[1], a[2], a[2] + 160), R("B32"), s)
+    ts(al(1), al(0), PM, Op.is_equal)
+    ts(al(2), al(0), PM, Op.is_gt)
+    tt(al(2), al(2), al(1), Op.subtract)
+    for r in range(16):
+        lin(rb(r), im("BOH"), R("AL", 16 + r, 17 + r))
+    for r in range(16):
+        lin(R("TRI", 128 * r, 128 * r + 128), im("BOK"), R("AL", 32 + r, 33 + r))
+    ts(li(4), al(0), 16.0, Op.mult, 15.0, Op.add)
+    ts(al(3), al(0), 16.0, Op.mult, PM, Op.add)
+    ts(al(4), al(3), 4096.0, Op.add)
+    ts(al(3), al(3), -255.0, Op.add)
+    for o, n, val in ((512, 256, 2048.0), (0, 512, 8192.0), (768, 256, -0.125), (1024, 64, -14336.0), (1088, 16, -47104.0)):
+        ms(R("CK", o, o + n), val)
+    for i, (src, p) in enumerate((("I6", P32), ("I6", P32B), ("I7", P32), ("I7", P32B))):
+        ts(R("SEL", 256 * i, 256 * i + 256), R(src), p, Op.is_equal, -1.0, Op.mult)
+    lin(R("KT1"), R("I6"), -KS)
+    ts(R("RMM"), R("I6"), 0.0, Op.is_gt, 8e9, Op.mult)
+    ts(R("RMM"), R("RMM"), -4e9, Op.add)
+    for h in range(2):
+        lin(R("p%d" % (5 + h), 384, 512), R("I6", 0, 128), 37.0)
+    lin(R("TY", 0, 2, 1, (0, 8)), R("TH", 0, 2, 1, (0, 8)), eng="V")
+    mm([(R("p7", 0, 2), R("G8", 0, 128, 1, (0, 8)), R("TY", 0, 2, 1, (0, 8)))])
+    ts(T1X, R("p7", 0, 1), 16 * KS, Op.mult, KS / 2, Op.add)
+    ts(TWX, R("p7", 0, 1), 16 * KS, Op.mult, KS / 2, Op.add)
+    ts(TMX, R("p7", 0, 1), -32 * KS, Op.mult, -KS, Op.add)
+    ts(TKX, R("p7", 1, 2), 16.0, Op.mult, NPM, Op.add)
+    ts(R("KT3"), R("I6", 0, 128), 0.0, Op.mult, TKX, Op.add)
+    ms(ci(8), 0)
+    ramps = []
+    for name, o, pat, base, step in (("PG", 0, [[1, 32], [256, 16]], 0, 32), ("CT", 0, [[1, 512]], -2048, 512), ("YT", 256, [[0, 512]], 8388608, 0)):
+        for h in range(8):
+            iota(R(name, o + 512 * h, o + 512 * h + 512), pat, base + step * h)
+            ramps.append(len(ops) - 1)
+    iota(R("MC"), [[1, 256]], -2048)
+    chain([7, 8, 9, 10, 11, 12] + ramps + [len(ops) - 1])
 
+    def turn(src, out):
+        tr(R("H2"), src)
+        mm([(R(out, 32 * b + 16 * x, 32 * b + 16 * x + 16), R("P4H", 128 * (2 * x + y), 128 * (2 * x + y) + 128),
+             R("H2", 32 * b + 16 * y, 32 * b + 16 * y + 16), y == 0, y == 1) for b in range(8) for x in range(2) for y in range(2)])
 
-    cp(R("U0"), R("O0"))
-    ts(R("Z0"), R("ZIN"), ZO, Op.add)
-    cp(R("REPU"), R("NN"))
-    ts(R("PR"), R("NN"), 4032, Op.bitwise_and)
-    rc = lambda i: R("RC", 256 * i, 256 * i + 256)
-    cp(rc(0), R("PR"))
-    ts(R("QQ"), R("NN"), 63, Op.bitwise_and)
-    cp(rc(1), R("QQ"))
+    def spread(bank, src, t, more=[]):
+        mm(more + [(R(bank, 256 * i, 256 * i + 256), rb(2 * t + i), R(src)) + (() if more else (True, True)) for i in range(2)])
 
-    ts(R("PR2"), R("NN"), 17.0, Op.mult)
-    ts(R("QQ2"), R("PR2"), 31, Op.bitwise_and)
-    ts(rc(2), R("QQ2"), 16.0, Op.mult, 2048.0, Op.add)
-    ts(rc(4), R("QQ2"), -16.0, Op.mult)
-    ts(R("SV"), R("QQ2"), 15.0, Op.mult, 256.0, Op.add)
-    tt(R("SV"), R("SV"), R("NN"), Op.add)
-    ts(rc(3), R("SV"), -16.0, Op.mult)
-    for i, p in enumerate((0, 8, 32, 64, 72)):
-        dma(R("PB", 0, W, 1, (p, p + 8)), rc(i), 65536)
-    n = len(ops)
-    chain([{"a": n - 5, "b": n - 4, "c": n - 3, "d": n - 2, "e": n - 1}.get(x) or int(x) for x in PARAM["dmas"]])
-
-    def spread(r2, p, k, banks):
-        bank = banks[sub[0] % 2]
-        sub[0] += 1
-        mm([(R(bank), R("GG", 0, 128, 1, (p, p + k)), R("PB", 512 * r2, 512 * r2 + 512, 1, (p, p + k)), True, True)])
-        return bank
-
-    for r2 in range(8):
-        lin(R("TT", 512 * r2, 512 * r2 + 512), R(spread(r2, 0, 16, ["p0", "p1"])), 1.0, 0.0)
-    for h in range(8):
-        ramp(R("CT", 512 * h, 512 * h + 512), R("IOT", 0, 512), 512 * h, [[1, 512]], 512 * h - 2048)
+    lin(R("RH0"), R("RP"), 1.0, -2048.0)
+    lin(R("H1"), R("NN"), 1.0, -2048.0)
+    turn(R("H1"), "p4")
+    lin(R("U0"), R("p4", 0, 256), 1.0, 2048.125)
+    lin(R("O0"), R("p4", 0, 256), 1.0, 2048.125)
+    lin(R("Z0"), R("ZIN"), 1.0, ZO)
+    for t in range(8):
+        bank = "p%d" % (t % 2)
+        spread(bank, "RH0", t)
+        lin(R("TT", 512 * t, 512 * t + 512), R(bank))
+    cur[0] = "t"
+    lin(R("REPU"), R("RP"))
+    lin(R("FL0"), R("RP"), 1.0 / 15, 1025 - 7.0 / 15)
+    lin(R("FA"), R("FL0"), -30.0, 28672.0)
+    lin(R("FB"), R("RP"), 2.0)
+    tt(R("OWN"), R("FA"), R("FB"), Op.add)
+    for t in range(8):
+        bank = "p%d" % (6 + t % 2)
+        bank = "p7" if t % 2 else "p3"
+        spread(bank, "FL0", t)
+        lin(R("AO", 512 * t, 512 * t + 512), R(bank), 2.0)
+    for c in range(2):
+        lin(R("XW", 256 + W + 2048 * c, 256 + W + 2048 * c + 2048), R("XW", 256 + 2048 * c, 256 + 2048 * c + 2048), eng="V")
+    for c in range(4):
+        tt(R("OH", CE * c, CE * c + CE), X(R("MI"), R("REPU", CL * c, CL * c + CL)), R("PG", CE * c, CE * c + CE), Op.is_equal)
 
     def tables():
-        for c in range(4):
-            at(0, "oh", c)
-            tt(R("OH", 1024 * c, 1024 * c + 1024), X(R("MI"), R("REPU", 64 * c, 64 * c + 64)),
-               R("YT", 256 + 1024 * c, 256 + 1024 * c + 1024), Op.is_equal)
+        cur[0] = "t"
+        for t in range(8):
+            bank = "p%d" % (t % 2)
+            spread(bank, "OWN", t, [(R(bank), im("IP"), C8192(512))]
+                   + [(R(bank, 256 * i, 256 * i + 256), im("IBG"), R("OH", 2 * t + i, W, 16)) for i in range(2)])
+            tt(R("TT", 512 * t, 512 * t + 512), R(bank), R("AO", 512 * t, 512 * t + 512), Op.min)
 
-    def tables2():
-        for r2 in range(8):
-            at(0, "nm", r2)
-            lin(R("TT", 512 * r2, 512 * r2 + 512), R(spread(r2, 32, 8, ["p2", "p4"])), 1.0, 0.0, "S")
-        for r2 in range(8):
-            at(0, "tt", r2)
-            bank = spread(r2, 64, 16, ["p2", "p4"])
-            for r in (2 * r2, 2 * r2 + 1):
-                o = R(bank, 256 * (r & 1), 256 * (r & 1) + 256)
-                tt(o, R("OH", r, W, 16), o, Op.mult)
-            tt(R("TT", 512 * r2, 512 * r2 + 512), R("TT", 512 * r2, 512 * r2 + 512), R(bank), Op.add)
-        for c in range(8):
-            bank = "p2"
-            at(0, "y0", c)
-            ts(R("PG", 512 * c, 512 * c + 512), R("MI", 512 * c, 512 * c + 512), 1.0, Op.add)
-            mm([(R(bank), R("WB32"), R("PG", 512 * c, 512 * c + 512), True, True)])
-            lin(R("YT", 256 + 512 * c, 768 + 512 * c), R(bank), 1.0, 0.0, "S")
+    def extract(out, lhs, src, c):
+        return [(out, bv(lhs, k), R(src, CE * c + k, CE * c + CE, 16)) for k in range(16)]
 
-    def extract(out, lhs, src, c, acc=None):
-        mm([(out, bview(lhs, k), R(src, CE * c + CL * k, CE * c + CL * k + CL), False, False) for k in range(16)], acc)
+    def dist(c, sel, out, lhs, first, acc):
+        for t in (2 * c, 2 * c + 1):
+            bank, rows = ("p0", "p1", "p7")[turns[0] % PARAM["rot"]], (32 * (t % 4), 32 * (t % 4) + 32)
+            turns[0] += 1
+            mm([(R(bank), im("IP"), R("XG", 512 * t, 512 * t + 512)),
+                (R(bank), R("ZT", 128 * (t // 4), 128 * (t // 4) + 128, 1, rows), R("SEL", 512 * sel, 512 * sel + 512, 1, rows))])
+            act(R("AB", 512 * t, 512 * t + 512), R(bank), Act.Abs)
+        mm(first + extract(out, lhs, "AB", c), acc)
 
-    def extract_s(out, lhs, src, c, ck=None, more=[]):
-        mm([(out, bview(lhs, k), R(src, CE * c + k, CE * c + CE, 16), k == 0, k == 15 and ck is None) for k in range(16)]
-           + more + ([] if ck is None else [(out, R("IP"), R("CK", ck, ck + CL), False, True)]))
-
-    def dist(src, z, c, out, lhs, acc):
-        made = []
-        for h in range(16 // KB):
-            bank = "p%d" % (sub[0] % (2 if z == "Z0" else 3))
-            sub[0] += 1
-            lst = []
-            for k in range(KB):
-                o = R(bank, CL * k, CL * k + CL)
-                lst += [(o, R("IP"), R(src, CE * c + KB * h + k, CE * c + CE, 16), True, False),
-                        (o, R("INH"), R(z, CL * c, CL * c + CL), False, True)]
-            mm(lst)
-            act(R("AB", CE * c + 512 * h, CE * c + 512 * h + 512), R(bank), Act.Abs, 1.0, ZO)
-            made.append(len(ops) - 1)
-        extract(out, lhs, "AB", c, acc)
-        return made
-
-    def best(key, pay):
-        tr(R("p7", 0, 256), key)
-        scan(R("MX"), R("RMM"), R("p7", 0, 256), 0.0, Op.min, Op.max)
-        tolist("MX", "P4", 0, 1, 304)
-        tt(R("p7", 256, 512), R("p7", 0, 256), R("MX"), Op.is_equal)
-        tt(R("NF"), R("p7", 0, 256), R("MX"), Op.is_lt)
-        for src, tmp, at in pay:
-            tt(R(tmp), R(src), R("p7", 256, 512), Op.mult)
-            scan(R("ST", at, at + 256), R("NF"), R(tmp), 0.0, Op.mult, Op.add)
-
-    def tolist(src, lhs, at, n, o):
-        lst = []
-        for b in range(2):
-            for e in range(2):
-                lst.append((R("p3", o + b, o + 16 * n, 2), R(lhs, 128 * (2 * b + e), 128 * (2 * b + e) + 128),
-                            R(src, at + 16 * e + 15, at + 256 * n, 32), e == 0, e == 1))
-        mm(lst)
+    def tolist(o, src, n):
+        return [(R("p3", o + b, o + n, 2), R("P4H", 128 * (2 * b + e), 128 * (2 * b + e) + 128), R("LH", src + e, src + n, 2))
+                for b in range(2) for e in range(2)]
 
     def pre(v):
-        gs = []
-        for c in range(NCH):
-            o, u = R("p3", CL * c, CL * c + CL), R("U%d" % v, CL * c, CL * c + CL)
-            at(v - 1, "pb", c)
+        cur[:] = ["a", "0" if v == 0 else "4" if v == VI - 1 else "", v]
+        for c in range(4):
+            s = lambda n, o=0: R(n, o + CL * c, o + CL * c + CL)
+            lin(R("PB", CE * c, CE * c + CE), X(R("TT"), s("U%d" % v)), eng=PARAM["a"][v][c])
+            mm([(s("p2"), im("IP"), CR0(CL) if v else C2048(CL))] + extract(s("p2"), "BHF" if v else "B16", "PB", c))
+            lin(s("R0U"), s("p2"), 1.0, 0.125)
             if v:
-                lin(R("PB", CE * c, CE * c + CE), X(R("TT"), u), 1.0, 0.0, PARAM["pg"][v][c])
-            else:
-                lin(R("AB", CE * c, CE * c + CE), X(R("TT"), u), -2.0, 0.0, PARAM["pg"][v][c])
-            if PARAM["pg"][v][c] == "S":
-                gs.append(len(ops) - 1)
-                chain(gs[-2:])
-            if v:
-                extract_s(o, "BQ", "PB", c, 256)
-                at(v - 1, "lb", c)
-                ts(R("PR2", CL * c, CL * c + CL), o, 17.0, Op.mult)
-                ts(R("QQ2", CL * c, CL * c + CL), R("PR2", CL * c, CL * c + CL), 31, Op.bitwise_and)
-                cp(R("LB", CL * c, CL * c + CL), R("QQ2", CL * c, CL * c + CL))
-            else:
-                extract_s(o, "BQ", "AB", c, 0)
-            at(v - 1, "r0", c)
-            ts(R("R0U", CL * c, CL * c + CL), o, 2048.0, Op.add)
-            at(v, "rt")
-            tr(R("RT", CL * c, CL * c + CL), o)
+                lin(s("FLH"), s("p2"), 1.0 / 15, 1025 - 7.0 / 15)
 
     pre(0)
     for v in range(VI):
         O, Z, last = "O%d" % v, "Z%d" % v, v == VI - 1
-        kd, ke = R("p5", 0, 256), R("p5", 256, 512)
-        if v == 0:
-            at(v, "oh")
-            tables()
-        at(v, "oc")
-        ts(R("OC"), R("U%d" % v), -2048.0, Op.add)
-        tr(R("OT"), R("OC"))
-        at(v, "u")
-        mm([(R("p6", 0, 256), R("BOH"), R(Z), True, False), (R("p6", 0, 256), R("BO1"), R("CM"), False, True)])
-        mm([(kd, R("IP"), R("KT"), True, False)], ("open", "d%d" % v))
-        a1, gs, ab = [], [], []
-        for c in range(NCH):
-            two = v and c == 0 and PARAM["split"]
-            for a, n in ([(0, CL // 2), (CL // 2, CL // 2)] if two else [(CL * c, CL)]):
-                if v:
-                    at(v, "ao2" if two and a else "ao", c)
-                    tt(R("AO", 16 * a, 16 * (a + n)), X(CG, R("R0U", a, a + n)), R("PB", 16 * a, 16 * (a + n)), Op.max)
-                    a1.append(len(ops) - 1)
-                    o = R("p4", a, a + n)
-                    at(v, "ne", c)
-                    mm([(o, bview("B1H", k), R("AO", 16 * a + k, 16 * (a + n), 16), k == 0, False) for k in range(16)]
-                       + [(o, R("IL"), R("LB", a, a + n), False, False), (o, R("IP"), R("CK", 128, 128 + n), False, True)])
-                    at(v, "nu", c)
-                    ts(R("NU", a, a + n), o, 2048.0, Op.add)
-                    at(v, "rt")
-                    tr(R("NT", a, a + n), o)
-                at(v, "xg", c)
-                lin(R("XG", 16 * a, 16 * (a + n)), X(XA, R("NU" if v else "R0U", a, a + n)), 1.0, 0.0, PARAM["xg"][v][c])
-            gs.append(len(ops) - 1)
-            at(v, "d1", c)
-            ab.append(dist("XG", Z, c, R("p5", CL * c, CL * c + CL), "B16", ("acc", "d%d" % v)))
-        chain(a1)
-        weave(gs, ab, PARAM["ahead"][0])
-        if v == 0:
-            tables2()
-        at(v, "pr")
-        tt(R("PR"), R(O), R("p6", 0, 256), Op.mult)
+        acc = [("acc", "e%d%d" % (v, h)) for h in range(2)]
+        UL, FLL, CLL, WS = R("p3", 0, 16), R("p3", 16, 32), R("p3", 48, 64), R("p3", 64, 65)
+        NEW, UP4 = R("p4", 0, 256), R("p4", 256, 512)
+        cur[0] = "z"
+        mm([(R("p3", 256 + HL * h, 256 + HL * h + HL), R(Z, HL * h, HL * h + HL), im("I1"), True, True) for h in range(2)])
+        lin(R("ZT"), R("p3", 256, 512), 1.0, -ZO)
+        mm([(UL, bv("B1H", r), R(Z, r, L, 16)) for r in range(16)])
+        lin(R("LH", 32, 48), UL, 1.0, -16 * ZO - 2048)
+        mm([(NEW, im("IP"), C2048(256))] + [(R("p4", k, 256, 16), im("I1"), R("LH", 32, 48)) for k in range(16)])
+        cur[0] = "f"
+        tt(R("PR"), R(O), NEW, Op.mult)
         ts(R("QQ"), R("PR"), 5, Op.arith_shift_right, 4095, Op.bitwise_and)
-        ts(R("p6", 0, 256), R("QQ"), K37, Op.add)
-        at(v, "s1")
-        best(kd, [("RT", "SL", 0), ("OT", "SL2", 256)])
-        tolist("ST", "P4H", 0, 2, 256)
-        at(v, "s1b")
-        ts(R("LI", 0, 32), R("p3", 256, 288), 2048.0, Op.add)
-        cp(R("MV"), X(R("MI"), li(0)))
-        cp(R("MU"), X(R("MI"), li(0)) if PARAM["mu"] else R("MV"))
-        tt(R("PR2"), X(IOB, li(1)), R("MV"), Op.mult)
-        ts(R("QQ2"), R("PR2"), 5, Op.arith_shift_right, 4095, Op.bitwise_and)
-        tt(R("SV"), R("QQ2"), R("MV"), Op.add)
-        cp(R("SU"), R("SV"))
-        at(v, "c")
-        tt(R("SL3"), R("NT" if v else "RT"), R("p7", 256, 512), Op.mult)
-        scan(R("ST", 512, 768), R("NF"), R("SL3"), 0.0, Op.mult, Op.add)
-        tolist("ST", "P4H", 512, 1, 288)
-        at(v, "c2")
-        tt(ty(5), R("p3", 256, 272), R("AL", 48, 64), Op.subtract)
-        ts(li(2), R("p3", 288, 304), 2048.0, Op.add)
-        ts(ty(0), li(2), -2048.0, Op.add)
-        ts(ty(1), R("p3", 304, 320), TWX, Op.is_le, 8192.0, Op.mult)
-        tt(R("CB"), ty(0), ty(1), Op.add)
-        at(v, "mask")
-        act(R("MASK"), kd, Act.Relu, 16384.0, col(12))
-        at(v, "fact")
-        tt(R("p6", 0, 256), R("p6", 0, 256), R("MASK"), Op.min)
-        tt(R("NN"), R("p6", 0, 256), R(O), Op.add)
+        for h in range(2):
+            tt(R("p4", HL * h, HL * h + HL), R("QQ", HL * h, HL * h + HL), R("p%d" % (5 + h), 384, 512), Op.add)
+        for c in range(4):
+            s = lambda n, o=0: R(n, o + CL * c, o + CL * c + CL)
+            if v:
+                cur[0] = "b"
+                tt(R("AO", CE * c, CE * c + CE), X(CG, s("R0U")), R("PB", CE * c, CE * c + CE), Op.max)
+                mm([(s("p2", 256), im("IP"), C2048(CL)), (s("p2", 256), im("I30"), s("FLH"))] + extract(s("p2", 256), "B1H", "AO", c))
+                lin(s("NU"), s("p2", 256), 1.0, 0.125)
+            cur[0] = "c"
+            lin(R("XG", CE * c, CE * c + CE), X(XA, s("NU" if v else "R0U")), eng=PARAM["c"][v][c])
+            kd = R("p%d" % (5 + c // 2), CL * (c % 2), CL * (c % 2) + CL)
+            dist(c, 0, kd, "BKD", [(kd, im("IP"), R("KT1", 0, CL))], None)
+        if v == 0:
+            tables()
+        for h in range(2):
+            s = lambda n, o=0: R(n, o + HL * h, o + HL * h + HL)
+            end = lambda n, o=0: R(n, o + HL * h + 15, o + HL * h + HL, 16)
+            bank = "p%d" % (5 + h)
+            kd, orep, crep = R(bank, 0, 128), R(bank, 128, 256), R(bank, 256, 384)
+            cur[0] = "m"
+            scan(s("MX"), s("RMM"), kd, Op.min, Op.max)
+            tt(s("AA"), s("MX"), kd, Op.subtract)
+            for j, src in ((0, s("p2")), (1, s(O)), (2, s("p2", 256))):
+                if j < 2 or v:
+                    tt(s("BB", 256 * j), src, s("AA"), Op.subtract)
+                    scan(s("ST", 256 * j), s("AA"), s("BB", 256 * j), Op.min, Op.max)
+            cl = end("ST", 512 if v else 0)
+            lin(li(0, h), end("ST"), 1.0, 0.125, "V")
+            lin(s("MV"), X(R("MI"), li(0, h)))
+            lin(s("MU"), s("MV"), fn=Act.Relu)
+            lin(R("LH", 16 * h, 16 * h + 8), end("ST", 256), 1.0, -2048.0, "V")
+            ts(R("LH", 16 * h + 8, 16 * h + 16), cl, RND, Op.add, -RND - 2048, Op.add)
+            mm([(R(bank, 128, 384), im("IP"), R("CK", 640, 896))]
+               + [(R(bank, 128 + r, 384, 16), rb(r), R("LH", 16 * h, 16 * h + 16)) for r in range(16)])
+            tt(s("PR2"), s("MV"), orep, Op.mult)
+            ts(s("QQ2"), s("PR2"), 5, Op.arith_shift_right, 4095, Op.bitwise_and)
+            tt(s("SV"), s("QQ2"), s("MV"), Op.add)
+            lin(s("SU"), s("SV"), fn=Act.Relu)
+            cur[0] = "k"
+            ts(R("TY", 8 * h, 8 * h + 8), end("MX"), TWX, Op.is_le, 8192.0, Op.mult)
+            tt(R("CB", 8 * h, 8 * h + 8), R("TY", 8 * h, 8 * h + 8), R("LH", 16 * h + 8, 16 * h + 16), Op.add)
+            lin(s("CREP"), crep, 1.0, 0.125)
+            tt(s("DD"), X(CG, li(0, h)), s("CREP"), Op.subtract)
+            ts(s("HC"), s("DD"), 0.0, Op.is_equal)
+            ts(s("HF"), s("DD"), 0.125, Op.is_equal)
+            act(s("EMP"), s("MV"), Act.Relu, -1.0)
+            lin(s("MP"), s("MV"), 1.0, -2047.875)
+            lin(s("MH"), s("MV"), 1.0, -2047.0)
+            cur[0] = "f"
+            act(s("MASK"), kd, Act.Relu, 2.0, TMX)
+            cur[0] = "k"
+            mm([(kd, R("J32", 16, 144), R("KT3"))], ("open", acc[h][1]))
+            chain([max([i for i, o in enumerate(ops) if o["kind"] == "mm" and o["part"][0] == "m"]), len(ops) - 1])
+            mm([(kd, im(a), s(b)) for a, b in (("IK", "HC"), ("IK", "HF"), ("IKN", "EMP"))], acc[h])
+        cur[0] = "f"
+        tt(NEW, NEW, R("MASK"), Op.min)
+        tt(R("NN"), NEW, R(O), Op.add)
         ts(R("N%d" % v), R("NN"), 4095, Op.bitwise_and)
         if last:
-            cp(R("MASK"), R("N%d" % v))
+            lin(R("H1"), R("N%d" % v), 1.0, -2048.0)
+            turn(R("H1"), "p4")
+            lin(R("MASK"), NEW, 1.0, 2048.0)
             dma(R("yo"), R("MASK"), 131072)
         else:
-            cp(R("V%d" % v), R("N%d" % v))
+            lin(R("V%d" % v), R("N%d" % v))
             rdma([(R("U%d" % (v + 1)), R("V%d" % v)), (R("O%d" % (v + 1)), R("N%d" % v))], "ao%d" % (v + 1))
-        mm([(ke, R("IP"), R("KT"), True, False)], ("open", "e%d" % v))
-        at(v, "crep")
-        cp(R("CREP"), X(IOA, li(2)))
-        tt(R("DD"), X(CG, li(0)), R("CREP"), Op.subtract)
-        at(v, "hit")
-        act(R("A1"), R("DD"), Act.Abs, 1.0, -0.09375)
-        act(R("HIT"), R("A1"), Act.Relu, -2.0, 1.1875)
-        act(R("FL"), R("A1"), Act.Relu, -32.0, 2.0)
-        act(R("EMP"), R("MV"), Act.Relu, -1.0, 0.0)
-        lin(R("MP"), R("MV"), 1.0, -2047.875, "S")
-        lin(R("M1V"), R("MV"), 1.0, 1.0, "S")
-        at(v, "mt")
-        tr(R("MT"), R("MP"))
-        at(v, "hit")
-        mm([(ke, R(a), R(b), False, False) for a, b in (("IK", "HIT"), ("IKN", "EMP"), ("IQ", "FL"), ("IR", "FL"))], ("acc", "e%d" % v))
-        at(v, "eq")
-        x, eqs = 0, []
-        for b in range(15):
-            n = 240 - 16 * b
-            ts(R("EQ", x, x + n), R("CREP", 256 - n, 256), R("CB", b, b + 1), Op.is_equal, -1.0, Op.mult)
-            eqs.append((n, R("EQ", x, x + n)))
-            x += n
-        mm([(R("p5", 512 - n, 512), R("BOK"), e, False, False) for n, e in eqs], ("acc", "e%d" % v))
-        at(v, "eqd")
-        tt(R("EQ0"), X(R("CB"), li(6)), R("CREP"), Op.is_equal)
-        tt(R("EQD"), R("EQ0"), R("p6", 256, 512), Op.mult)
-        mm([(ke, R("BOK"), R("EQD"), False, False)], ("acc", "e%d" % v))
-        at(v, "alt")
-        tt(R("DC"), X(XA, li(2)), R(Z), Op.subtract)
+        cur[0] = "q"
+        for b in range(16):
+            ts(R("EQ", 272 * b, 256 * b + 256), R("CREP", 16 * b, 256), R("CB", b, b + 1), Op.is_equal, -1.0, Op.mult)
+        for h in range(2):
+            bank, lo = "p%d" % (5 + h), lambda b: max(16 * b + 16, HL * h)
+            mm([(R(bank, lo(b) - HL * h, HL), im("BOK"), R("EQ", 256 * b + lo(b), 256 * b + HL * h + HL)) for b in range(8 * h + 7)], acc[h])
+            mm([(R(bank, r, HL, 16), R("TRI", 128 * r, 128 * r + 128), R("EQ", 2176 * h + r, min(W, 2176 * h + 2176), 272)) for r in range(16)], acc[h])
+        mm([(FLL, bv("BN1", r), R("HF", r, L, 16)) for r in range(16)])
+        tt(ty(1), FLL, R("ST", 15, 256, 16), Op.add)
+        cur[0] = "y"
+        lin(li(1), R("ST", (512 if v else 0) + 15, (512 if v else 0) + 256, 16), 1.0, 0.125, "V")
+        tt(R("DC"), X(XA, li(1)), R(Z), Op.subtract)
         act(R("DC2"), R("DC"), Act.Abs, 2.0, 2 * ZO)
-        mm([(R("p4", 256, 512), R("IP"), R("DC2"), True, False), (R("p4", 256, 512), R("INH"), R(Z), False, True)])
-        lin(R("XW", 0, 256), R("p4", 256, 512), 1.0, ZO + 0.5, "S")
-        a1, gs, ab = [], [], []
-        for c in range(NCH):
+        mm([(UP4, im("IP"), R("DC2")), (UP4, im("IN1"), R(Z))])
+        lin(R("XW", 0, 256), UP4, 1.0, ZO + 0.5)
+        for c in range(4):
+            s = lambda n: R(n, CL * c, CL * c + CL)
             xg = R("XG", CE * c, CE * c + CE)
-            at(v, "xm", c)
-            lin(xg, X(XA, R("MU", CL * c, CL * c + CL)), 1.0, 0.0, PARAM["xm"][v][c])
-            gs.append(len(ops) - 1)
-            at(v, "xs", c)
-            tt(xg, X(XD, R("SU", CL * c, CL * c + CL)), xg, Op.min)
-            a1.append(len(ops) - 1)
-            at(v, "d3", c)
-            ab.append(dist("XG", Z, c, R("p5", 256 + CL * c, 256 + CL * c + CL), "BN16", ("acc", "e%d" % v)))
-        chain(a1)
-        weave(gs, ab, PARAM["ahead"][1])
-        at(v, "s2")
-        best(ke, [("MT", "SL", 512)])
-        ts(R("p6", 0, 256), ke, TKX, Op.is_gt)
-        tolist("ST", "P4H", 512, 1, 288)
-        mx = R("p3", 304, 320)
-        at(v, "s2a")
-        cp(R("MI16"), mx)
-        ts(R("WINB"), mx, 65600.0, Op.is_gt)
-        tt(ty(2), mx, R("MI16"), Op.is_equal)
-        tt(ty(5), ty(5), R("WINB"), Op.mult)
-        tt(ty(2), ty(2), ty(5), Op.mult)
-        tt(ty(2), ty(2), R("AL", 32, 48), Op.add)
-        cp(li(3), ty(2))
-        at(v, "s2b")
-        ts(li(4), R("p3", 288, 304), 2048.0, Op.add)
-        tt(R("DL"), X(IOA, li(4)), R("MP"), Op.subtract)
-        tt(R("DL"), R("DL"), R("p6", 0, 256), Op.mult)
-        tt(X(R("CT"), li(3)), R("DL"), R("MP"), Op.add)
-        at(v, "s2b" if last else "z")
-        ts(ty(3), mx, TKX, Op.is_gt)
-        tt(ty(4), R("p3", 288, 304), R("AL", 16, 32), Op.subtract)
-        tt(ty(4), ty(4), ty(3), Op.mult)
-        tt(ty(4), ty(4), R("AL", 0, 16), Op.add)
-        cp(li(5), ty(4))
-        tt(R("DC"), X(XZ, li(5)), R(Z), Op.add)
-        ts(R("Y%d" % v), R("DC"), 0.5, Op.mult, ZO / 2 - 0.25, Op.add)
+            cur[0] = "d"
+            lin(xg, X(XA, s("MU")), eng=PARAM["d"][v][c])
+            cur[0] = "e"
+            tt(xg, X(XD, s("SU")), xg, Op.min)
+            dist(c, 1, R("p%d" % (5 + c // 2), CL * (c % 2), CL * (c % 2) + CL), "BN16", [], acc[c // 2])
+        for h in range(2):
+            s = lambda n: R(n, HL * h, HL * h + HL)
+            e8 = lambda n, o: R(n, o + 8 * h, o + 8 * h + 8)
+            bank = "p%d" % (5 + h)
+            ke, new, best = R(bank, 0, 128), R(bank, 128, 256), R(bank, 256, 384)
+            cur[0] = "w"
+            tr(s("KET"), ke)
+            scan(s("MX2"), s("RMM"), s("KET"), Op.min, Op.max)
+            ts(s("KP"), ke, 2 * BAND - 15.5, Op.is_gt)
+            tt(s("EQT"), X(s("MX2"), li(4, 0)), s("KET"), Op.is_equal)
+            tr(best, s("EQT"))
+            tt(s("SL"), best, s("MH"), Op.mult)
+            mm([(new, im("IP"), CN8(HL)), (new, im("IN1"), s("MH")), (new, im("BOH"), s("SL"))])
+            tt(s("DL"), new, s("KP"), Op.mult)
+            top = R("MX2", HL * h + 15, HL * h + HL, 16)
+            ts(e8("LH", 48), top, 1.5 * BAND, Op.is_le, 8192.0, Op.mult)
+            mm([m + (i % 2 == 0, i % 2 == 1) for i, m in enumerate(tolist(32 + 8 * h, 48 + 8 * h, 8))])
+            tt(e8("TY", 32), e8("p3", 32), e8("TY", 16), Op.add)
+            tt(e8("TY", 32), e8("TY", 32), e8("AL", 64), Op.min)
+            lin(li(2, h), e8("TY", 32), 1.0, 0.125, "V")
+            tt(X(R("CT"), li(2, h)), s("DL"), s("MP"), Op.add)
+        cur[0] = "x"
+        ts(R("LH", 64, 80), R("MX2", 15, 256, 16), 2 * BAND - 15.5, Op.is_gt, 49152.0, Op.mult)
+        mm([(CLL, im("IP"), CGOT(16))] + tolist(48, 64, 16) + [(CLL, bv("B1H", r), R("SL", r, L, 16)) for r in range(16)])
+        tt(ty(3), CLL, al(3), Op.max)
+        lin(li(3), ty(3), 1.0, 255.125, "V")
+        tt(R("DC"), X(XZ, li(3)), R(Z), Op.add)
+        lin(R("Y%dH" % v), R("DC"), 0.5, ZO / 2 - 0.25)
         if last:
-            ops[-1]["slot"] = ops[-2]["slot"] = cur[0] = (v, "zl", 0)
-            ts(R("SV"), R("Y%d" % v), -ZO, Op.add)
+            lin(R("SV"), R("Y%dH" % v), 1.0, -ZO)
             dma(R("yz"), R("SV"), 131072)
         else:
-            rdma([(R("Z%d" % (v + 1)), R("Y%d" % v))], "az%d" % (v + 1))
-            at(v, "a")
-            mm([(R("p4", 256, 272), R("BO1"), R("WINB"), True, True)])
-            red(AI, R("p4", 256, 272))
-            tt(AC, AC, AI, Op.add)
-            cp(R("CI", 3, 4), AC)
-            ts(R("CI", 4, 5), R("CI", 3, 4), 127, Op.bitwise_and)
-            ts(TWX, R("CI", 4, 5), 16.0, Op.mult, T1X, Op.add)
-        at(v, "kml" if last else "km")
-        tt(R("KM"), R("M1V"), R("p6", 0, 256), Op.mult)
-        mm([(R("p4", 256, 512), R("WB32"), R("KM"), True, True)])
-        lin(R("YV"), R("p4", 256, 512), 1.0, 0.0, "S")
-        at(v, "ytl" if last else "yt")
-        cp(X(R("YT"), li(5)), R("YV"))
+            rdma([(R("Z%d" % (v + 1)), R("Y%dH" % v))], "az%d" % (v + 1))
+            cur[0] = "n"
+            red(AI, R("p3", 32, 48))
+            mm([(WS, R("BOA"), AI)])
+            tt(ci(9), WS, ci(8), Op.add)
+            ts(ci(8), ci(9), 127, Op.bitwise_and)
+            ts(TWX, ci(8), 16 * KS, Op.mult, T1X, Op.add)
+        cur[0] = "s"
+        tt(R("KM"), R("MH"), R("KP"), Op.mult)
+        mm([(UP4, im("WBH"), R("KM")), (UP4, im("WB2"), R("KP"))])
+        lin(R("YV"), UP4)
+        lin(X(R("YT"), li(3)), R("YV"), eng="V")
         if not last:
             pre(v + 1)
 
-    at(VI - 1, "end")
+    cur[0] = "i"
+    for c in range(8):
+        lin(R("PB", 512 * c, 512 * c + 512), R("MI", 512 * c, 512 * c + 512), 1.0, -2047.0)
+    mm([(R("p2", 0, 256), bv("BK1", x), R("PB", 256 * x, 256 * x + 256)) for x in range(16)])
+    lin(R("Y0"), R("p2", 0, 256), 1.0, 136 * 2048.0)
+    ts(R("FA"), R("Y0"), 0.0, Op.is_equal, 8388608.0, Op.mult)
+    tt(R("Y0"), R("Y0"), R("FA"), Op.add)
+    ts(R("MC"), R("MC"), P256, Op.add)
+    lin(R("MC8"), R("MC"), 1.0, 0.125)
+    lin(R("C1"), R("MC"), 1.0, 2049.0)
+    cur[0] = "o"
     dma(R("RT"), R("YT", 256, 256 + W, 1, (0, 128, 16)), 131072)
-    ts(R("NT"), R("MCOL"), -1.0, Op.mult, 2048.0, Op.add)
-    ts(R("MCOL"), R("MCOL"), 1.0, Op.add)
-    for c in range(NCH):
-        at(VI - 1, "fin", c)
+    tt(R("RT"), R("RT"), R("Y0"), Op.min)
+    for c in range(4):
         tt(R("PG", CE * c, CE * c + CE), X(CG, R("REPU", CL * c, CL * c + CL)), R("OH", CE * c, CE * c + CE), Op.mult)
-        o = R("p%d" % c, 0, CL)
-        extract_s(o, "B32N", "PG", c)
-        s = lambda n: R(n, CL * c, CL * c + CL)
-        at(VI - 1, "out", c)
-        tt(s("DD"), o, s("NT"), Op.subtract)
-        ts(s("A1"), o, -1.0, Op.mult, 12582912.0 + 2048.0, Op.add)
-    lin(R("MT"), R("A1"), 1.0, -12582912.0, "S")
-    dma(R("yr"), R("MT"), 131072, "S")
-    ts(R("p7", 0, 256), R("DD"), 0.0, Op.is_equal)
-    ts(R("p7", 256, 512), R("DD"), -0.125, Op.is_equal)
-    tt(R("DL"), R("RT"), R("p7", 0, 256), Op.mult)
-    tt(R("p7", 256, 512), R("MCOL"), R("p7", 256, 512), Op.mult)
-    tt(R("KM"), R("DL"), R("p7", 256, 512), Op.add)
-    dma(R("yc"), R("KM"), 131072)
+        mm(extract(R("p%d" % (c // 2), CL * (c % 2), CL * (c % 2) + CL), "B32", "PG", c))
+    for h in range(2):
+        s = lambda n: R(n, HL * h, HL * h + HL)
+        o, f0, f1 = R("p%d" % h, 0, HL), R("p3", 256 * h, 256 * h + HL), R("p3", 256 * h + HL, 256 * h + 256)
+        ts(s("DD"), o, RND + 2048, Op.add, -RND, Op.add)
+        tt(f0, o, s("MC"), Op.is_equal)
+        tt(f1, o, s("MC8"), Op.is_equal)
+        tt(s("FA"), f0, s("RT"), Op.mult)
+        tt(f1, f1, s("C1"), Op.mult)
+        tt(s("FB"), f1, s("FA"), Op.add)
+    dma(R("yr"), R("DD"), 131072, "S")
+    dma(R("yc"), R("FB"), 131072)
     return ops
 
 
@@ -633,7 +542,7 @@ def depend(ops):
         for k in o["prev"]:
             dep[k] = None
         for w, lst in ((True, o["wr"]), (False, o["rd"])):
-            for a in lst:
+            for a in set(lst):
                 pl, ph = (a[5] or (0, 128))[:2]
                 for j, w2, lo, hi, ql, qh in seen.get(a[1], []):
                     if ph <= ql or qh <= pl:
@@ -642,11 +551,11 @@ def depend(ops):
                     if o["acc"] and p["acc"] and o["acc"][1] == p["acc"][1] and p["acc"][0] == "acc":
                         continue
                     if lo < a[3] and a[2] < hi and (w or w2):
-                        dep[j] = bool(dep.get(j)) or (w2 and not w)
-        o["dep"] = dep
+                        dep[j] = bool(dep.get(j)) or o["kind"] != "mm" or p["kind"] != "mm"
+        o["dep"] = dict(sorted(dep.items()))
         o["banks"] = sorted(set([a[1] for a in o["wr"] + o["rd"] if inps(a)]))
         for w, lst in ((True, o["wr"]), (False, o["rd"])):
-            for a in set(lst):
+            for a in sorted(set(lst), key=str):
                 s = seen.setdefault(a[1], [])
                 if w and a[4] == 1 and a[5] is None and not o["acc"]:
                     s[:] = [x for x in s if not (a[2] <= x[2] and x[3] <= a[3] and x[0] != i)]
@@ -654,34 +563,22 @@ def depend(ops):
 
 
 def tag(o):
-    w, r = o["wr"][0], o["rd"][0] if o["rd"] else ("", "", 0)
-    s = lambda a: a[1].rstrip("01234") if a[1][0] != "p" else a[1]
-    return "%s %s%d %s" % (o["kind"], s(w), w[2], s(r) if r[1] else "")
+    w = o["wr"][0]
+    s = w[1].rstrip("01234H") if w[1][0] != "p" else w[1]
+    return "%s %s %s%d" % (o["part"], o["kind"], s, w[2])
 
 
 def lat(o):
     return 1.6 + o["lat"] / DBW if o["kind"] == "dma" else o["lat"]
 
 
-def rank_of_op(ops, succ, pr, i):
-    if PARAM["slots"] and ops[i]["slot"] is not None:
-        v, name, c = ops[i]["slot"]
-        return -(40.0 * v + SLOT.get("%s%d" % (name, c), SLOT[name] + c * SLOT.get(name + "+", 0.0))) - 1e-4 * i
-    c = min(ops[i]["cost"].values())
-    if succ[i] and PARAM["slots"]:
-        return c + max([pr[j] + (0.0 if ops[j]["dep"][i] is None else lat(ops[i]) + LATX) for j in succ[i]])
-    return c + max([pr[j] + (0.0 if ops[j]["dep"][i] is None else lat(ops[i]) + LATX) for j in succ[i]] + [lat(ops[i])])
-
-
-def after(ops, o, e, eng, end):
+def after(ops, o, e, eng, end, wait):
     t = 0.0
     for j, raw in o["dep"].items():
         if raw is None and eng[j] == e:
             continue
-        if eng[j] != e or ops[j]["sem"]:
-            t = max(t, end[j] + LATX)
-        elif raw:
-            t = max(t, end[j] + LATS)
+        if eng[j] != e or ops[j]["sem"] or raw:
+            t = max(t, end[j] + wait)
     return t
 
 
@@ -692,19 +589,8 @@ def finish(o, t, c, pipe):
     return t + c + o["lat"]
 
 
-def schedule(ops, succ, pr, look):
+def schedule(ops, succ, pr, look, wait):
     n = len(ops)
-    left, todo, vq = [len(o["dep"]) for o in ops], [i for i in range(n) if not ops[i]["dep"]], []
-    while todo and PARAM["strict"]:
-        i = max(todo, key=lambda x: pr[x])
-        todo.remove(i)
-        if PARAM["strict"] and ops[i]["slot"] is not None and list(ops[i]["cost"]) == ["V"]:
-            vq.append(i)
-        for j in succ[i]:
-            left[j] -= 1
-            if not left[j]:
-                todo.append(j)
-    turn, fixed = [0], set(vq)
     eng, start, end = [None] * n, [0.0] * n, [0.0] * n
     left = [len(o["dep"]) for o in ops]
     ready = {}
@@ -717,14 +603,12 @@ def schedule(ops, succ, pr, look):
     while ready:
         cand = []
         for i, l in ready.items():
-            if i in fixed and i != vq[turn[0]]:
-                continue
             for t, e, c in l:
                 t = max(t, free[e])
                 for b in ops[i]["banks"]:
                     for e2, j in last.get(b, {}).items():
-                        if e2 != e and end[j] + LATX > t:
-                            t = end[j] + LATX
+                        if e2 != e and end[j] + wait > t:
+                            t = end[j] + wait
                 cand.append((t, -pr[i], i, e, c))
         t, _, i, e, c = min(cand)
         for _ in range(3):
@@ -740,20 +624,19 @@ def schedule(ops, succ, pr, look):
             extra[i] += [j for e2, j in last.setdefault(b, {}).items() if e2 != e]
             last[b][e] = i
         order.append(i)
-        turn[0] += i in fixed
         del ready[i]
         for j in succ[i]:
             left[j] -= 1
             if not left[j]:
-                ready[j] = [(after(ops, ops[j], e2, eng, end), e2, c2) for e2, c2 in ops[j]["cost"].items()]
+                ready[j] = [(after(ops, ops[j], e2, eng, end, wait), e2, c2) for e2, c2 in ops[j]["cost"].items()]
     return order, eng, start, end, extra
 
 
-def replay(ops, costs, order, eng, extra):
+def replay(ops, costs, wait, order, eng, extra):
     end, free, pipe = [0.0] * len(ops), {e: 0.0 for e in "VSPGY"}, [0.0]
     for i in order:
         e = eng[i]
-        t = max([free[e], after(ops, ops[i], e, eng, end)] + [end[j] + LATX for j in extra[i]])
+        t = max([free[e], after(ops, ops[i], e, eng, end, wait)] + [end[j] + wait for j in extra[i]])
         free[e] = t + costs[i][e]
         end[i] = finish(ops[i], t, costs[i][e], pipe)
     return max(end)
@@ -762,21 +645,17 @@ def replay(ops, costs, order, eng, extra):
 def plan():
     ops = build(*MODELS[0])
     costs = [[o["cost"] for o in build(*m)] for m in MODELS]
+    wait = MODELS[0][4]
     depend(ops)
     n = len(ops)
     succ = [[] for _ in ops]
     for i, o in enumerate(ops):
         for j in o["dep"]:
             succ[j].append(i)
-    pr, topo_order, left = [0.0] * n, [i for i in range(n) if not ops[i]["dep"]], [len(o["dep"]) for o in ops]
-    for i in topo_order:
-        for j in succ[i]:
-            left[j] -= 1
-            if not left[j]:
-                topo_order.append(j)
-    assert len(topo_order) == n
-    for i in reversed(topo_order):
-        pr[i] = rank_of_op(ops, succ, pr, i)
+    pr = [0.0] * n
+    for i in reversed(range(n)):
+        o = ops[i]
+        pr[i] = min(o["cost"].values()) + max([pr[j] + (0.0 if ops[j]["dep"][i] is None else lat(o) + wait) for j in succ[i]] + [lat(o)])
     tags = [tag(o) for o in ops]
     pool = sorted(set(tags)) + 3 * sorted(set([t for t in tags if tags.count(t) >= 4]))
     x, best, boost = [PARAM["seed"]], None, dict(BOOST)
@@ -790,8 +669,8 @@ def plan():
         for _ in range((1, 1, 2, 3, 5)[int(5 * draw())] if it else 0):
             t = pool[int(len(pool) * draw())]
             trial[t] = round(trial.get(t, 0.0) + (draw() + draw() - 1.0) * (1.5, 5.0, 15.0, 35.0)[int(4 * draw())], 1)
-        order, eng, start, end, extra = schedule(ops, succ, [p + trial.get(t, 0.0) for p, t in zip(pr, tags)], PARAM["look"])
-        ts = [replay(ops, c, order, eng, extra) for c in costs]
+        order, eng, start, end, extra = schedule(ops, succ, [p + trial.get(t, 0.0) for p, t in zip(pr, tags)], PARAM["look"], wait)
+        ts = [replay(ops, c, m[4], order, eng, extra) for c, m in zip(costs, MODELS)]
         val = sum([a / b for a, b in zip(ts, WEIGHT)])
         if best is None or val <= best[0]:
             best, boost = (val, order, eng, start, end, ts, extra), trial
@@ -822,7 +701,7 @@ def plan():
                 continue
             if p["sem"]:
                 key, val = ("D", j), 1
-            elif p["eng"] != e or o["dep"][j] or o["sem"] or (PARAM["waw"] and e != "P"):
+            elif p["eng"] != e or o["dep"][j] or o["sem"]:
                 key, val = p["eng"], pos[j]
             else:
                 continue
@@ -890,17 +769,13 @@ def rank_program(g, core, T, topo):
                 ins = q.tensor_scalar(ap(T, a[0]), ap(T, a[1]), ap(T, a[2]), None, a[4])
             else:
                 ins = q.tensor_scalar(ap(T, a[0]), ap(T, a[1]), ap(T, a[2]), ap(T, a[3]), a[4], a[5])
-        elif k == "cp":
-            ins = q.tensor_copy(ap(T, a[0]), ap(T, a[1]))
-        elif k == "ramp" and e == "G":
-            ins = g.iota(ap(T, a[0]), a[4], a[5], 0, allow_small_or_imprecise_dtypes=True)
-        elif k == "lin" or k == "ramp":
+        elif k == "lin":
             if e == "S":
-                ins = q.activation(ap(T, a[0]), ap(T, a[1]), Act.Identity, bias=a[3], scale=a[2])
+                ins = q.activation(ap(T, a[0]), ap(T, a[1]), a[4], bias=a[3], scale=ap(T, a[2]))
             elif a[2] == 1.0 and a[3] == 0.0:
                 ins = q.tensor_copy(ap(T, a[0]), ap(T, a[1]))
             else:
-                ins = q.tensor_scalar(ap(T, a[0]), ap(T, a[1]), a[2], a[3], Op.mult, Op.add)
+                ins = q.tensor_scalar(ap(T, a[0]), ap(T, a[1]), ap(T, a[2]), a[3], Op.mult, Op.add)
         elif k == "act":
             ins = q.activation(ap(T, a[0]), ap(T, a[1]), a[2], bias=ap(T, a[4]), scale=a[3])
         elif k == "scan":
@@ -911,13 +786,10 @@ def rank_program(g, core, T, topo):
             ins = q.tensor_reduce(ap(T, a[0]), ap(T, a[1]), AxisListType.X, Op.add)
         elif k == "ms":
             ins = q.memset(ap(T, a[0]), a[1])
-        elif k == "iota":
-            if SCRATCH[a[0][1]][2] == I32:
-                ins = g.iota(ap(T, a[0]), a[1], a[2], a[3])
-            else:
-                ins = g.iota(ap(T, a[0]), a[1], a[2], a[3], allow_small_or_imprecise_dtypes=True)
+        elif SCRATCH[a[0][1]][2] == I32:
+            ins = g.iota(ap(T, a[0]), a[1], a[2], a[3])
         else:
-            ins = g.affine_select(ap(T, a[0]), ap(T, a[0]), a[1], a[2], 0.0, a[3], a[4])
+            ins = g.iota(ap(T, a[0]), a[1], a[2], a[3], allow_small_or_imprecise_dtypes=True)
         if o.get("inc"):
             ins.then_inc(T.sem["s" + e], 1)
     g.wait_ge(T.sem.sent, sent)

@@ -20,31 +20,32 @@ _sb(F16, W, "PB AO")
 _sb(F16, 2048, "RB")
 _sb(BF, 2048, "TRI")
 _sb(BF, 1024, "SEL")
-_sb(BF, 1104, "CK")
+_sb(BF, 480, "CK")
 _sb(F32, 768, "ST BB")
 _sb(F16, 512, "P4H")
-_sb(F32, 256, "MX AA MV SV DD MP DL YV DC MASK RMM KET MX2 EQT I6 I7 Y0 RT MC MC8 C1 FA FB")
+_sb(F32, 256, "MX AA MV SV DD MP DL YV DC MASK KM KET MX2 EQT I6 I7 Y0 RT MC MC8 C1 FA FB")
 _sb(I32, 256, "RP PR PR2 QQ QQ2 NN O0 O1 O2 O3 O4 N0 N1 N2 N3 N4")
 _sb(U16, 256, "REPU R0U NU MU SU U0 U1 U2 U3 U4 V0 V1 V2 V3")
-_sb(F16, 256, "CREP FLH MH SL KP KM H1 H2 RH0 FL0 OWN Z0 Z1 Z2 Z3 Z4 Y0H Y1H Y2H Y3H Y4H")
-_sb(BF, 256, "ZIN ZT KT1 HC HF EMP DC2")
+_sb(F16, 256, "CREP FLH MH SL KP H1 H2 RH0 FL0 OWN Z0 Z1 Z2 Z3 Z4 Y0H Y1H Y2H Y3H Y4H")
+_sb(BF, 256, "ZIN ZT HC HF EMP DC2")
 _sb(F32, 160, "J32 B32")
 _sb(BF, 3 * 160, "BB16")
 _sb(F16, 4 * 160, "BH16")
-_sb(BF, 6 * 128, "IB")
-_sb(F16, 6 * 128, "IH")
-_sb(F32, 128, "BO32 G8 BOA KT3")
+_sb(BF, 5 * 128, "IB")
+_sb(F16, 5 * 128, "IH")
+_sb(F32, 128, "BO32 G8 BOA KT3 RMM WB32")
+_sb(BF, 64, "KT1")
 _sb(F32, 64, "TY")
 _sb(F32, 80, "AL")
 _sb(F32, 16, "CB COL")
-_sb(F16, 80, "LH")
+_sb(F16, 96, "LH")
 _sb(I32, 16, "CI TH")
 _sb(U16, 80, "LI")
 for _i in range(8):
     SCRATCH["p%d" % _i] = ("psum", [128, 512], F32)
 
 DSEMS = ["d%d" % i for i in range(16)]
-SEMAPHORES = ["sV", "sS", "sP", "sG", "sent"] + DSEMS + ["ao%d" % v for v in range(1, VI)] + ["az%d" % v for v in range(1, VI)]
+SEMAPHORES = ["sV", "sS", "sP", "sG", "sent"] + DSEMS + ["ao%d" % v for v in range(1, VI)] + ["az%d%d" % (v, h) for v in range(1, VI) for h in range(2)]
 
 SHAPES = {"feat": 4096, "memb": 4096, "rep": 4096, "fact": 256, "z": 256, "thr": 2, "yc": 4096, "yr": 4096, "yo": 256, "yz": 256}
 SIZE = {F32: 4, I32: 4, BF: 2, F16: 2, U16: 2}
@@ -53,13 +54,44 @@ Op, Act = AluOpType, ActivationFunctionType
 MODELS = [(0.00083, 0.00042, 1.56, 3.8, 0.2), (0.00104, 0.00052, 1.3, 3.0, 0.2), (0.00115, 0.00058, 1.9, 5.0, 0.2), (0.0009, 0.00045, 1.2, 2.5, 0.3)]
 WEIGHT = [160.0, 180.0, 240.0, 165.0]
 DBW = 190000.0
-PARAM = {"rot": 3, "look": 0.6, "seed": 1, "iters": 800,
-         "a": ["VSVS"] + ["SSSS"] * 4, "c": ["SVSV"] + ["SSVS"] * 4, "d": ["SSSS"] * 5}
-BOOST = {t: 8.0 for t in ("f tt NN0", "f ts N0", "f lin V0", "f tt p40", "f tt p4128", "f rdma U0", "f tt PR0", "f ts QQ0",
-                          "f act MASK0", "f act MASK128", "z mm p40", "z lin L32", "z mm p30")}
+PARAM = {"rot": 3, "look": 0.6, "seed": 1, "rounds": 4, "iters": 1800, "models": (0, 2), "slack": 0.0012,
+         "a": [["VS"] * 4] * 5, "c": [["VS"] * 4] * 5, "d": [["VS"] * 4] * 5}
+
+V_END = """ y.DC0 w.KET0 q.L80 w.MX0 w.KP0 w.EQT0 x.L64 w.L48 w.p5256 k.MP128 w.SL0 k.M128 w.TY32 w.DL0 w.LI32 w.KET128 w.CT0 w.MX128
+    w.KP128 x.TY48 w.L56 w.EQT128 x.L72 x.LI48 w.p6256 x.DC0 w.SL128 w.TY40 n.COL13 w.LI40 w.DL128 w.CT0 """
+V_HEAD = """ b.AO0 <x.DC128 b.AO1024 <n.CI9 b.AO2048 b.AO3072 <s.YT0 c.XG2048 f.PR0 <n.CI8 m.MX0 <n.COL12 m.AA0 f.QQ0 m.BB0 m.BB256
+    m.ST0 m.BB512 k.TY0 m.LI0 m.ST256 m.ST512 f.MASK0 m.MV0 m.L0 m.L8 m.MU0 f.p40 k.CB0 m.PR0 k.CREP0 m.QQ0 m.MX128 m.SV0 m.AA128
+    f.MASK128 m.SU0 m.BB128 m.BB384 f.p40 m.BB640 m.ST128 m.ST384 f.NN0 m.LI8 m.ST640 k.TY8 m.L16 f.N0 m.L24 e.XG0 k.DD0 m.PR128
+    k.CB8 e.XG1024 k.HF0 m.QQ128 k.HC0 k.DD128 m.SV128 q.EQ* m.SU128 k.HF128 y.LI16 k.HC128 e.XG2048 e.XG3072 """
+V_MID = V_HEAD + V_END + " x.TY56 x.LI56 "
+V_FIRST = """ r.* g.TT0 u.turn j.COL8 g.TT1024 l.COL4 l.COL7 l.G80 l.TY0 g.TT2048 l.SEL0 g.TT3072 l.SEL256 l.COL9 l.COL12 l.COL10 l.COL11
+    l.RMM0 l.AL32 l.SEL512 l.RMM0 l.AL32 l.SEL768 a.PB0 a.PB2048 a.R0U0 a.R0U64 c.XG1024 a.R0U128 a.R0U192 z.L32 c.XG3072 l.* h.FL0
+    f.PR0 h.FB0 f.QQ0 h.FA0 h.REPU0 f.p40 h.OWN0 m.MX0 k.TY0 m.AA0 f.MASK0 m.BB0 m.BB256 m.ST0 m.ST256 m.LI0 m.L0 m.L8 k.CB0 t.O0
+    m.MX128 k.CREP0 m.AA128 f.MASK128 m.BB128 m.BB384 f.p40 m.ST128 m.ST384 f.NN0 m.LI8 m.L16 f.N0 m.L24 m.MV0 k.TY8 m.MV128 m.MU0
+    m.PR0 f.V0 m.MU128 m.QQ0 k.CB8 m.PR128 m.SV0 m.QQ128 k.CREP128 m.SV128 t.O1024 t.O2048 t.O3072 q.EQ* t.TT0 k.DD0 t.TT512
+    k.DD128 t.TT1024 k.HC0 k.HF0 t.TT1536 k.HC128 k.HF128 t.TT* e.XG0 y.LI16 e.XG1024 e.XG2048 e.XG3072 """ + V_END + " x.TY56 x.LI56 "
+V_LAST = V_HEAD + " i.MC0 " + V_END.replace("k.MP128", "f.turn").replace("k.M128", "").replace("n.COL13", "") + """ o.PG0 x.TY56 o.PG1024
+    x.LI56 o.PG2048 s.YT0 o.PG3072 i.FA0 x.DC128 i.Y1 o.DD0 o.p30 o.p3128 o.RT0 o.p3128 o.FA0 o.FB0 o.p3256 o.p3384 o.DD128 o.FA128
+    o.p3384 o.FB128 """
+S_HEAD = """ a.R0U128 a.FL128 <s.KM0 a.R0U192 a.FL192 <s.YV0 z.ZT0 <x.Y128 b.NU0 c.XG0 b.NU64 c.XG1024 b.NU128 c.AB0 c.AB512 z.L32
+    c.AB1024 z.ZT128 b.NU192 c.AB1536 c.XG3072 c.AB2048 c.AB2560 c.AB3072 c.AB3584 k.EMP0 d.XG0 d.XG1024 m.MV128 k.MP0 m.MU128 """
+S_MID = S_HEAD + """ f.V0 d.XG2048 k.CREP128 e.AB0 e.AB512 d.XG3072 k.EMP128 k.M0 >a.PB0 e.AB1024 e.AB1536 >a.PB1024 e.AB2048 e.AB2560
+    e.AB3072 e.AB3584 y.DC0 >a.R0U0 >a.FL0 >a.PB2048 y.XW0 >a.R0U64 >a.FL64 x.Y0 >a.PB3072 """
+S_FIRST = """ u.R0 j.IB0 j.I0 u.0 j.BH16160 j.BH16320 g.TT512 u.Z0 g.TT1536 u.U0 g.TT2560 g.TT3584 u.O0 a.PB1024 a.PB3072 z.ZT0 z.ZT128
+    j.BB160 j.KT0 c.XG0 j.p30 j.IB512 c.AB0 c.AB512 c.AB1024 c.AB1536 c.XG2048 c.AB* j.* h.AO0 h.AO512 h.AO1024 d.XG0 h.AO1536
+    h.AO2048 d.XG1024 m.SU0 m.SU128 h.AO* k.EMP0 k.EMP128 d.XG2048 d.XG3072 k.M0 k.MP0 e.AB0 e.AB512 >a.PB0 e.AB1024 e.AB1536
+    >a.PB1024 e.AB2048 e.AB2560 e.AB3072 e.AB3584 y.DC0 >a.R0U0 >a.FL0 >a.PB2048 y.XW0 >a.R0U64 >a.FL64 x.Y0 >a.PB3072 """
+S_LAST = S_HEAD + """ d.XG2048 k.CREP128 e.AB0 e.AB512 d.XG3072 k.EMP128 k.M0 k.M128 k.MP128 f.0 e.AB1024 e.AB1536 i.PB0 i.PB512
+    i.PB1024 e.AB2048 e.AB2560 i.PB1536 e.AB3072 e.AB3584 y.DC0 f.MASK0 i.PB2048 y.XW0 i.PB* x.Y0 s.KM0 i.Y0 s.YV0 i.MC80 i.C0
+    x.Y128 x.SV0 o.yr0 """
+P_ALL = """ g u l a.p2192 z.p3256 b.p2256 c.z0 c.z1 c.z2 b.p2320 c.x0 c.x1 b.p2384 c.x2 b.p2448 c.z3 c.x3 z.p3384 c.p50 c.p564 z.p4256
+    c.z4 c.x4 z.p40 c.z5 c.x5 c.z6 c.x6 c.z7 c.x7 m.p5128 c.p60 c.p664 h m.p6128 k.p50 k.p60 t e.z0 e.z1 e.z2 e.x0 e.x1 e.z3 k.p50
+    e.p50 e.z4 e.x2 e.x3 q.p516 q.p50 k.p60 e.z5 e.p564 e.x4 e.x5 q.p60 q.p60 q.p4272 e.z6 e.z7 e.x6 e.x7 w.p40 w.p5128 e.p60
+    e.p664 y.p3256 x.c0 >a.p20 f.p40 w.p48 w.p6128 x.c1 >a.p264 >a.p2128 s.p5128 s.p6128 n.p4288 i.p20 o """
 ZO = 1536.0
 KS = 8192.0
 BAND = 131072.0
+LOW = 5120.0
 RND = 12582912.0
 
 
@@ -154,6 +186,9 @@ def build(CY, PCY, GA, SC, LAT=0.0):
     def act(out, a, fn, scale=1.0, bias=0.0):
         add({"S": scost(out, a)}, "act", (out, a, fn, scale, bias), [out], [a, bias])
 
+    def step(out, a, t, t2):
+        add({"V": vcost(out, [a]), "S": scost(out, a)}, "step", (out, a, t, t2), [out], [a, t, t2])
+
     def scan(out, d0, d1, op0, op1):
         add({"V": vcost(out, [d0, d1])}, "scan", (out, d0, d1, 0.0, op0, op1), [out], [d0, d1])
 
@@ -185,6 +220,7 @@ def build(CY, PCY, GA, SC, LAT=0.0):
     CL, CE, HL = 64, 1024, 128
     col = lambda i: R("COL", i, i + 1)
     PF, PM, PG8, P32, P32B, PAR0, PAR1, NPM, KP1, T1X, TMX, TKX, TWX, AI, P256 = [col(i) for i in range(15)]
+    CKM = 2048.0 - 8192.0
     ci = lambda i: R("CI", i, i + 1)
     ty = lambda i: R("TY", 16 * i, 16 * i + 16)
     li = lambda i, h=None: R("LI", 16 * i, 16 * i + 16) if h is None else R("LI", 16 * i + 8 * h, 16 * i + 8 * h + 8)
@@ -192,7 +228,7 @@ def build(CY, PCY, GA, SC, LAT=0.0):
     XA, XD, XZ = R("XW", 256, 256 + W), R("XW", 256, 256 + 2 * W), R("XW", 0, 256 + W)
     CG = R("CT", 0, W)
     names = {"BKD": 0, "BN16": 1, "BN1": 2, "BHF": 0, "B16": 1, "B1H": 2, "BK1": 3}
-    ids = {"IP": 0, "IK": 1, "IKN": 2, "IBG": 3, "BOK": 4, "BO1": 5, "I1": 0, "IN1": 1, "I30": 2, "BOH": 3, "WBH": 4, "WB2": 5}
+    ids = {"IP": 0, "IK": 1, "IKN": 2, "IBG": 3, "BOK": 4, "I1": 0, "IN1": 1, "I30": 2, "BOH": 3, "I8K": 4}
 
     def bv(n, k):
         if n == "B32":
@@ -203,7 +239,7 @@ def build(CY, PCY, GA, SC, LAT=0.0):
     def im(n):
         return R("IB" if n in ("IP", "IK", "IKN", "IBG", "BOK", "BO1") else "IH", 128 * ids[n], 128 * ids[n] + 128)
 
-    C8192, C2048, CN8, CR0, CGOT = [lambda n, o=o: R("CK", o, o + n) for o in (0, 512, 768, 1024, 1088)]
+    C2048, CN8, CR0, CGOT, CM2048 = [lambda n, o=o: R("CK", o, o + n) for o in (0, 256, 384, 448, 464)]
     rb = lambda r: R("RB", 128 * r, 128 * r + 128)
 
     dma(R("RP"), R("rep"), 131072)
@@ -213,118 +249,122 @@ def build(CY, PCY, GA, SC, LAT=0.0):
     dma(XA, R("feat"), 1048576)
     for c in range(2):
         dma(R("MI", 2048 * c, 2048 * c + 2048), R("memb", 2048 * c, 2048 * c + 2048), 1048576)
-    chain([0, 1, 4, 5, 6])
+    dma(R("XW", 256 + W, 256 + 2 * W), R("feat"), 1048576)
+    chain([0, 1, 4, 5, 6, 7])
 
+    cur[0] = "r"
     iota(ci(0), [[0, 1]], 0, 1)
-    iota(R("J32"), [[1, 160]], -16, -1)
     iota(R("G8"), [[1, 8], [0, 16]], 0)
     iota(al(0), [[1, 16]], 0)
+    iota(R("J32"), [[1, 160]], -16, -1)
     iota(R("I6"), [[0, 16], [1, 16]], 0)
     iota(R("I7"), [[1, 16], [0, 16]], 0)
+    for o, n, val in ((0, 256, 2048.0), (256, 128, -0.125), (384, 64, -14336.0), (448, 16, -47104.0), (464, 16, -2048.0)):
+        ms(R("CK", o, o + n), val)
+    ms(R("B32"), 0.0)
+    ms(ci(8), 0)
     for i, (s, op) in enumerate(((15, Op.bitwise_and), (4, Op.arith_shift_right), (31, Op.bitwise_and), (16, Op.bitwise_and))):
         ts(ci(1 + i), ci(0), s, op)
     lin(R("COL", 0, 4), R("CI", 0, 4), eng="V")
-    ts(P32B, ci(3), -16.0, Op.add)
     ts(PAR0, ci(4), 0.0, Op.is_equal)
     ts(PAR1, ci(4), 16.0, Op.is_equal)
-    ts(NPM, ci(1), -1.0, Op.mult)
-    ts(KP1, ci(1), 1.0, Op.add)
-    ts(P256, ci(1), 256.0, Op.mult)
-    ts(R("J32"), R("J32"), 0.0, Op.is_equal)
+    ts(im("BOH"), R("G8"), PG8, Op.is_equal)
+    ts(al(1), al(0), PM, Op.is_equal)
     ts(R("BO32"), R("G8"), PG8, Op.is_equal)
-    ts(R("G8"), R("G8"), PF, Op.is_equal)
+    ts(R("J32"), R("J32"), 0.0, Op.is_equal)
+    for r in range(16):
+        lin(rb(r), im("BOH"), R("AL", 16 + r, 17 + r), eng="V")
     for b in range(2):
         for e in range(2):
             o, q = 16 + 16 * (b - e), 128 * (2 * b + e)
             ts(R("P4H", q, q + 128), R("J32", o, o + 128), PAR1 if b else PAR0, Op.mult)
-    for n, s in (("IP", 1.0), ("I1", 1.0), ("IK", BAND), ("IKN", -BAND), ("IBG", -8192.0), ("IN1", -1.0), ("I30", -30.0)):
-        lin(im(n), R("J32", 16, 144), s)
-    lin(im("BOH"), R("BO32"))
-    lin(im("BOK"), R("BO32"), BAND)
-    lin(R("BOA"), R("BO32"), -1.0 / 8192)
-    ts(im("WBH"), R("BO32"), KP1, Op.mult)
-    ts(im("WB2"), R("BO32"), KP1, Op.mult, 2048.0, Op.mult)
-    ms(R("B32"), 0.0)
     lin(R("B32", 15, 143, 16), R("BO32", 0, 128, 16), eng="V")
-    for n, s in (("B16", 0.0625), ("BKD", 16 * KS), ("B1H", 1.0), ("BN16", -16.0), ("BN1", 8192.0), ("BHF", 0.5), ("BK1", KP1)):
+    cur[0] = "j"
+    for n, s in (("IP", 1.0), ("I1", 1.0), ("IK", BAND), ("IKN", -BAND), ("IBG", -LOW), ("IN1", -1.0), ("I30", -30.0), ("I8K", 8192.0)):
+        lin(im(n), R("J32", 16, 144), s)
+    ts(KP1, ci(1), 1.0, Op.add)
+    for n, s in (("B16", 0.0625), ("B1H", 1.0), ("BKD", 16 * KS), ("BN16", -16.0), ("BN1", 8192.0), ("BHF", 0.5), ("BK1", KP1)):
         a = bv(n, 15)
         lin(R(a[1], a[2], a[2] + 160), R("B32"), s)
-    ts(al(1), al(0), PM, Op.is_equal)
-    ts(al(2), al(0), PM, Op.is_gt)
-    tt(al(2), al(2), al(1), Op.subtract)
-    for r in range(16):
-        lin(rb(r), im("BOH"), R("AL", 16 + r, 17 + r))
-    for r in range(16):
-        lin(R("TRI", 128 * r, 128 * r + 128), im("BOK"), R("AL", 32 + r, 33 + r))
-    ts(li(4), al(0), 16.0, Op.mult, 15.0, Op.add)
-    ts(al(3), al(0), 16.0, Op.mult, PM, Op.add)
-    ts(al(4), al(3), 4096.0, Op.add)
-    ts(al(3), al(3), -255.0, Op.add)
-    for o, n, val in ((512, 256, 2048.0), (0, 512, 8192.0), (768, 256, -0.125), (1024, 64, -14336.0), (1088, 16, -47104.0)):
-        ms(R("CK", o, o + n), val)
+    lin(R("KT1"), R("I6", 0, 64), -KS)
+    lin(R("p3", 0, 256), R("I6"), 37.0)
+    lin(im("BOK"), R("BO32"), BAND)
+    lin(R("BOA"), R("BO32"), -1.0 / 8192)
+    lin(R("WB32"), R("BO32"), KP1)
+    cur[0] = "l"
+    ts(P32B, ci(3), -16.0, Op.add)
+    ts(NPM, ci(1), -1.0, Op.mult)
+    ts(R("G8"), R("G8"), PF, Op.is_equal)
+    lin(R("TY", 0, 2, 1, (0, 8)), R("TH", 0, 2, 1, (0, 8)), eng="V")
     for i, (src, p) in enumerate((("I6", P32), ("I6", P32B), ("I7", P32), ("I7", P32B))):
         ts(R("SEL", 256 * i, 256 * i + 256), R(src), p, Op.is_equal, -1.0, Op.mult)
-    lin(R("KT1"), R("I6"), -KS)
-    ts(R("RMM"), R("I6"), 0.0, Op.is_gt, 8e9, Op.mult)
-    ts(R("RMM"), R("RMM"), -4e9, Op.add)
-    for h in range(2):
-        lin(R("p%d" % (5 + h), 384, 512), R("I6", 0, 128), 37.0)
-    lin(R("TY", 0, 2, 1, (0, 8)), R("TH", 0, 2, 1, (0, 8)), eng="V")
     mm([(R("p7", 0, 2), R("G8", 0, 128, 1, (0, 8)), R("TY", 0, 2, 1, (0, 8)))])
+    ts(R("RMM"), R("I6", 0, 128), 0.0, Op.is_gt, 8e9, Op.mult)
+    ts(al(2), al(0), PM, Op.is_gt)
     ts(T1X, R("p7", 0, 1), 16 * KS, Op.mult, KS / 2, Op.add)
     ts(TWX, R("p7", 0, 1), 16 * KS, Op.mult, KS / 2, Op.add)
     ts(TMX, R("p7", 0, 1), -32 * KS, Op.mult, -KS, Op.add)
     ts(TKX, R("p7", 1, 2), 16.0, Op.mult, NPM, Op.add)
+    ts(R("RMM"), R("RMM"), -4e9, Op.add)
+    tt(al(2), al(2), al(1), Op.subtract)
+    ts(li(4), al(0), 16.0, Op.mult, 15.0, Op.add)
+    ts(al(3), al(0), 16.0, Op.mult, PM, Op.add)
     ts(R("KT3"), R("I6", 0, 128), 0.0, Op.mult, TKX, Op.add)
-    ms(ci(8), 0)
+    ts(P256, ci(1), 256.0, Op.mult)
+    ts(al(4), al(3), 2048.0, Op.add)
+    for r in range(16):
+        lin(R("TRI", 128 * r, 128 * r + 128), im("BOK"), R("AL", 32 + r, 33 + r), eng="V")
+    ts(al(3), al(3), -255.0, Op.add)
     ramps = []
-    for name, o, pat, base, step in (("PG", 0, [[1, 32], [256, 16]], 0, 32), ("CT", 0, [[1, 512]], -2048, 512), ("YT", 256, [[0, 512]], 8388608, 0)):
+    for name, o, pat, base, inc in (("PG", 0, [[1, 32], [256, 16]], 0, 32), ("CT", 0, [[1, 512]], -2048, 512), ("YT", 256, [[0, 512]], 8388608, 0)):
         for h in range(8):
-            iota(R(name, o + 512 * h, o + 512 * h + 512), pat, base + step * h)
+            iota(R(name, o + 512 * h, o + 512 * h + 512), pat, base + inc * h)
             ramps.append(len(ops) - 1)
     iota(R("MC"), [[1, 256]], -2048)
-    chain([7, 8, 9, 10, 11, 12] + ramps + [len(ops) - 1])
+    chain([8, 9, 10, 11, 12, 13] + ramps + [len(ops) - 1])
 
     def turn(src, out):
         tr(R("H2"), src)
+        ops[-1]["name"] = "turn"
         mm([(R(out, 32 * b + 16 * x, 32 * b + 16 * x + 16), R("P4H", 128 * (2 * x + y), 128 * (2 * x + y) + 128),
              R("H2", 32 * b + 16 * y, 32 * b + 16 * y + 16), y == 0, y == 1) for b in range(8) for x in range(2) for y in range(2)])
 
-    def spread(bank, src, t, more=[]):
-        mm(more + [(R(bank, 256 * i, 256 * i + 256), rb(2 * t + i), R(src)) + (() if more else (True, True)) for i in range(2)])
+    def spread(bank, src, t):
+        mm([(R(bank, 256 * i, 256 * i + 256), rb(2 * t + i), R(src), True, True) for i in range(2)])
 
+    cur[0] = "u"
     lin(R("RH0"), R("RP"), 1.0, -2048.0)
     lin(R("H1"), R("NN"), 1.0, -2048.0)
     turn(R("H1"), "p4")
     lin(R("U0"), R("p4", 0, 256), 1.0, 2048.125)
     lin(R("O0"), R("p4", 0, 256), 1.0, 2048.125)
     lin(R("Z0"), R("ZIN"), 1.0, ZO)
+    cur[0] = "g"
     for t in range(8):
-        bank = "p%d" % (t % 2)
+        bank = ("p0", "p1", "p5", "p6")[t % 4]
         spread(bank, "RH0", t)
         lin(R("TT", 512 * t, 512 * t + 512), R(bank))
-    cur[0] = "t"
+    cur[0] = "h"
     lin(R("REPU"), R("RP"))
     lin(R("FL0"), R("RP"), 1.0 / 15, 1025 - 7.0 / 15)
     lin(R("FA"), R("FL0"), -30.0, 28672.0)
     lin(R("FB"), R("RP"), 2.0)
     tt(R("OWN"), R("FA"), R("FB"), Op.add)
-    for t in range(8):
-        bank = "p%d" % (6 + t % 2)
-        bank = "p7" if t % 2 else "p3"
-        spread(bank, "FL0", t)
-        lin(R("AO", 512 * t, 512 * t + 512), R(bank), 2.0)
-    for c in range(2):
-        lin(R("XW", 256 + W + 2048 * c, 256 + W + 2048 * c + 2048), R("XW", 256 + 2048 * c, 256 + 2048 * c + 2048), eng="V")
+    cur[0] = "t"
     for c in range(4):
         tt(R("OH", CE * c, CE * c + CE), X(R("MI"), R("REPU", CL * c, CL * c + CL)), R("PG", CE * c, CE * c + CE), Op.is_equal)
 
     def tables():
+        cur[0] = "h"
+        for t in range(8):
+            bank = ("p0", "p1", "p7")[t % 3]
+            spread(bank, "FL0", t)
+            lin(R("AO", 512 * t, 512 * t + 512), R(bank), 2.0, -LOW)
         cur[0] = "t"
         for t in range(8):
-            bank = "p%d" % (t % 2)
-            spread(bank, "OWN", t, [(R(bank), im("IP"), C8192(512))]
-                   + [(R(bank, 256 * i, 256 * i + 256), im("IBG"), R("OH", 2 * t + i, W, 16)) for i in range(2)])
+            bank = ("p7", "p0", "p1")[t % 3]
+            mm([(R(bank, 256 * i, 256 * i + 256), a, b, j == 0, j == 1) for i in range(2)
+                for j, (a, b) in enumerate(((rb(2 * t + i), R("OWN")), (im("IBG"), R("OH", 2 * t + i, W, 16))))])
             tt(R("TT", 512 * t, 512 * t + 512), R(bank), R("AO", 512 * t, 512 * t + 512), Op.min)
 
     def extract(out, lhs, src, c):
@@ -334,20 +374,21 @@ def build(CY, PCY, GA, SC, LAT=0.0):
         for t in (2 * c, 2 * c + 1):
             bank, rows = ("p0", "p1", "p7")[turns[0] % PARAM["rot"]], (32 * (t % 4), 32 * (t % 4) + 32)
             turns[0] += 1
-            mm([(R(bank), im("IP"), R("XG", 512 * t, 512 * t + 512)),
-                (R(bank), R("ZT", 128 * (t // 4), 128 * (t // 4) + 128, 1, rows), R("SEL", 512 * sel, 512 * sel + 512, 1, rows))])
+            mm([(R(bank), R("ZT", 128 * (t // 4), 128 * (t // 4) + 128, 1, rows), R("SEL", 512 * sel, 512 * sel + 512, 1, rows))], ("open", turns[0]))
+            mm([(R(bank), im("IP"), R("XG", 512 * t, 512 * t + 512))], ("acc", turns[0]))
+            ops[-2]["name"], ops[-1]["name"] = "z%d" % t, "x%d" % t
             act(R("AB", 512 * t, 512 * t + 512), R(bank), Act.Abs)
         mm(first + extract(out, lhs, "AB", c), acc)
 
-    def tolist(o, src, n):
-        return [(R("p3", o + b, o + n, 2), R("P4H", 128 * (2 * b + e), 128 * (2 * b + e) + 128), R("LH", src + e, src + n, 2))
+    def tolist(bank, o, src, n):
+        return [(R(bank, o + b, o + n, 2), R("P4H", 128 * (2 * b + e), 128 * (2 * b + e) + 128), R("LH", src + e, src + n, 2))
                 for b in range(2) for e in range(2)]
 
     def pre(v):
         cur[:] = ["a", "0" if v == 0 else "4" if v == VI - 1 else "", v]
         for c in range(4):
             s = lambda n, o=0: R(n, o + CL * c, o + CL * c + CL)
-            lin(R("PB", CE * c, CE * c + CE), X(R("TT"), s("U%d" % v)), eng=PARAM["a"][v][c])
+            lin(R("PB", CE * c, CE * c + CE), X(R("TT"), s("U%d" % v)), 1.0, LOW if v else 0.0, eng=PARAM["a"][v][c])
             mm([(s("p2"), im("IP"), CR0(CL) if v else C2048(CL))] + extract(s("p2"), "BHF" if v else "B16", "PB", c))
             lin(s("R0U"), s("p2"), 1.0, 0.125)
             if v:
@@ -357,19 +398,20 @@ def build(CY, PCY, GA, SC, LAT=0.0):
     for v in range(VI):
         O, Z, last = "O%d" % v, "Z%d" % v, v == VI - 1
         acc = [("acc", "e%d%d" % (v, h)) for h in range(2)]
-        UL, FLL, CLL, WS = R("p3", 0, 16), R("p3", 16, 32), R("p3", 48, 64), R("p3", 64, 65)
-        NEW, UP4 = R("p4", 0, 256), R("p4", 256, 512)
+        UL, FLL, WS = R("p4", 256, 272), R("p4", 272, 288), R("p4", 288, 289)
+        NEW, UP4 = R("p4", 0, 256), R("p3", 256, 512)
+        idle = ("p0", "p1", "p7")[(turns[0] + 13) % PARAM["rot"]]
         cur[0] = "z"
-        mm([(R("p3", 256 + HL * h, 256 + HL * h + HL), R(Z, HL * h, HL * h + HL), im("I1"), True, True) for h in range(2)])
-        lin(R("ZT"), R("p3", 256, 512), 1.0, -ZO)
+        for h in range(2):
+            mm([(R("p3", 256 + HL * h, 256 + HL * h + HL), R(Z, HL * h, HL * h + HL), im("I1"))])
+            lin(R("ZT", HL * h, HL * h + HL), R("p3", 256 + HL * h, 256 + HL * h + HL), 1.0, -ZO)
         mm([(UL, bv("B1H", r), R(Z, r, L, 16)) for r in range(16)])
         lin(R("LH", 32, 48), UL, 1.0, -16 * ZO - 2048)
         mm([(NEW, im("IP"), C2048(256))] + [(R("p4", k, 256, 16), im("I1"), R("LH", 32, 48)) for k in range(16)])
         cur[0] = "f"
         tt(R("PR"), R(O), NEW, Op.mult)
         ts(R("QQ"), R("PR"), 5, Op.arith_shift_right, 4095, Op.bitwise_and)
-        for h in range(2):
-            tt(R("p4", HL * h, HL * h + HL), R("QQ", HL * h, HL * h + HL), R("p%d" % (5 + h), 384, 512), Op.add)
+        tt(NEW, R("QQ"), R("p3", 0, 256), Op.add)
         for c in range(4):
             s = lambda n, o=0: R(n, o + CL * c, o + CL * c + CL)
             if v:
@@ -389,7 +431,7 @@ def build(CY, PCY, GA, SC, LAT=0.0):
             bank = "p%d" % (5 + h)
             kd, orep, crep = R(bank, 0, 128), R(bank, 128, 256), R(bank, 256, 384)
             cur[0] = "m"
-            scan(s("MX"), s("RMM"), kd, Op.min, Op.max)
+            scan(s("MX"), R("RMM"), kd, Op.min, Op.max)
             tt(s("AA"), s("MX"), kd, Op.subtract)
             for j, src in ((0, s("p2")), (1, s(O)), (2, s("p2", 256))):
                 if j < 2 or v:
@@ -401,7 +443,7 @@ def build(CY, PCY, GA, SC, LAT=0.0):
             lin(s("MU"), s("MV"), fn=Act.Relu)
             lin(R("LH", 16 * h, 16 * h + 8), end("ST", 256), 1.0, -2048.0, "V")
             ts(R("LH", 16 * h + 8, 16 * h + 16), cl, RND, Op.add, -RND - 2048, Op.add)
-            mm([(R(bank, 128, 384), im("IP"), R("CK", 640, 896))]
+            mm([(R(bank, 128, 384), im("IP"), R("CK", 128, 384))]
                + [(R(bank, 128 + r, 384, 16), rb(r), R("LH", 16 * h, 16 * h + 16)) for r in range(16)])
             tt(s("PR2"), s("MV"), orep, Op.mult)
             ts(s("QQ2"), s("PR2"), 5, Op.arith_shift_right, 4095, Op.bitwise_and)
@@ -418,7 +460,7 @@ def build(CY, PCY, GA, SC, LAT=0.0):
             lin(s("MP"), s("MV"), 1.0, -2047.875)
             lin(s("MH"), s("MV"), 1.0, -2047.0)
             cur[0] = "f"
-            act(s("MASK"), kd, Act.Relu, 2.0, TMX)
+            step(s("MASK"), kd, T1X, TMX)
             cur[0] = "k"
             mm([(kd, R("J32", 16, 144), R("KT3"))], ("open", acc[h][1]))
             chain([max([i for i, o in enumerate(ops) if o["kind"] == "mm" and o["part"][0] == "m"]), len(ops) - 1])
@@ -442,8 +484,8 @@ def build(CY, PCY, GA, SC, LAT=0.0):
             bank, lo = "p%d" % (5 + h), lambda b: max(16 * b + 16, HL * h)
             mm([(R(bank, lo(b) - HL * h, HL), im("BOK"), R("EQ", 256 * b + lo(b), 256 * b + HL * h + HL)) for b in range(8 * h + 7)], acc[h])
             mm([(R(bank, r, HL, 16), R("TRI", 128 * r, 128 * r + 128), R("EQ", 2176 * h + r, min(W, 2176 * h + 2176), 272)) for r in range(16)], acc[h])
-        mm([(FLL, bv("BN1", r), R("HF", r, L, 16)) for r in range(16)])
-        tt(ty(1), FLL, R("ST", 15, 256, 16), Op.add)
+        mm([(FLL, im("IP"), CM2048(16))] + [(FLL, bv("BN1", r), R("HF", r, L, 16)) for r in range(16)])
+        tt(R("LH", 80, 96), FLL, R("ST", 15, 256, 16), Op.add)
         cur[0] = "y"
         lin(li(1), R("ST", (512 if v else 0) + 15, (512 if v else 0) + 256, 16), 1.0, 0.125, "V")
         tt(R("DC"), X(XA, li(1)), R(Z), Op.subtract)
@@ -465,7 +507,7 @@ def build(CY, PCY, GA, SC, LAT=0.0):
             ke, new, best = R(bank, 0, 128), R(bank, 128, 256), R(bank, 256, 384)
             cur[0] = "w"
             tr(s("KET"), ke)
-            scan(s("MX2"), s("RMM"), s("KET"), Op.min, Op.max)
+            scan(s("MX2"), R("RMM"), s("KET"), Op.min, Op.max)
             ts(s("KP"), ke, 2 * BAND - 15.5, Op.is_gt)
             tt(s("EQT"), X(s("MX2"), li(4, 0)), s("KET"), Op.is_equal)
             tr(best, s("EQT"))
@@ -474,33 +516,37 @@ def build(CY, PCY, GA, SC, LAT=0.0):
             tt(s("DL"), new, s("KP"), Op.mult)
             top = R("MX2", HL * h + 15, HL * h + HL, 16)
             ts(e8("LH", 48), top, 1.5 * BAND, Op.is_le, 8192.0, Op.mult)
-            mm([m + (i % 2 == 0, i % 2 == 1) for i, m in enumerate(tolist(32 + 8 * h, 48 + 8 * h, 8))])
-            tt(e8("TY", 32), e8("p3", 32), e8("TY", 16), Op.add)
-            tt(e8("TY", 32), e8("TY", 32), e8("AL", 64), Op.min)
-            lin(li(2, h), e8("TY", 32), 1.0, 0.125, "V")
+            mm([m + (i % 2 == 0, i % 2 == 1) for i, m in enumerate(tolist("p4", 8 * h, 48 + 8 * h, 8))]
+               + [(e8("p4", 16), im("I1"), e8("LH", 80), True, False)] + [m + (False, i == 3) for i, m in enumerate(tolist("p4", 16 + 8 * h, 48 + 8 * h, 8))])
+            tt(e8("TY", 32), e8("p4", 16), e8("AL", 64), Op.min)
+            lin(li(2, h), e8("TY", 32), 1.0, 2048.125, "V")
             tt(X(R("CT"), li(2, h)), s("DL"), s("MP"), Op.add)
-        cur[0] = "x"
-        ts(R("LH", 64, 80), R("MX2", 15, 256, 16), 2 * BAND - 15.5, Op.is_gt, 49152.0, Op.mult)
-        mm([(CLL, im("IP"), CGOT(16))] + tolist(48, 64, 16) + [(CLL, bv("B1H", r), R("SL", r, L, 16)) for r in range(16)])
-        tt(ty(3), CLL, al(3), Op.max)
-        lin(li(3), ty(3), 1.0, 255.125, "V")
-        tt(R("DC"), X(XZ, li(3)), R(Z), Op.add)
-        lin(R("Y%dH" % v), R("DC"), 0.5, ZO / 2 - 0.25)
+            cur[0] = "x"
+            ts(e8("LH", 64), top, 2 * BAND - 15.5, Op.is_gt, 49152.0, Op.mult)
+            mm([(e8(idle, 0), im("IP"), CGOT(8))] + tolist(idle, 8 * h, 64 + 8 * h, 8)
+               + [(e8(idle, 0), bv("B1H", r), R("SL", HL * h + r, HL * h + HL, 16)) for r in range(16)])
+            ops[-1]["name"] = "c%d" % h
+            tt(e8("TY", 48), e8(idle, 0), e8("AL", 48), Op.max)
+            lin(li(3, h), e8("TY", 48), 1.0, 255.125, "V")
+            tt(s("DC"), X(XZ, li(3, h)), s(Z), Op.add)
+            lin(s("Y%dH" % v), s("DC"), 0.5, ZO / 2 - 0.25)
+            if not last:
+                rdma([(s("Z%d" % (v + 1)), s("Y%dH" % v))], "az%d%d" % (v + 1, h))
         if last:
             lin(R("SV"), R("Y%dH" % v), 1.0, -ZO)
             dma(R("yz"), R("SV"), 131072)
         else:
-            rdma([(R("Z%d" % (v + 1)), R("Y%dH" % v))], "az%d" % (v + 1))
             cur[0] = "n"
-            red(AI, R("p3", 32, 48))
+            red(AI, R("p4", 0, 16))
             mm([(WS, R("BOA"), AI)])
             tt(ci(9), WS, ci(8), Op.add)
             ts(ci(8), ci(9), 127, Op.bitwise_and)
             ts(TWX, ci(8), 16 * KS, Op.mult, T1X, Op.add)
         cur[0] = "s"
-        tt(R("KM"), R("MH"), R("KP"), Op.mult)
-        mm([(UP4, im("WBH"), R("KM")), (UP4, im("WB2"), R("KP"))])
-        lin(R("YV"), UP4)
+        mm([(R("p5", 128, 384), im("I8K"), R("KP")), (R("p5", 128, 384), im("I1"), R("MH"))])
+        act(R("KM"), R("p5", 128, 384), Act.Relu, 1.0, CKM)
+        mm([(R("p6", 128, 384), R("WB32"), R("KM"))])
+        lin(R("YV"), R("p6", 128, 384))
         lin(X(R("YT"), li(3)), R("YV"), eng="V")
         if not last:
             pre(v + 1)
@@ -512,6 +558,7 @@ def build(CY, PCY, GA, SC, LAT=0.0):
     lin(R("Y0"), R("p2", 0, 256), 1.0, 136 * 2048.0)
     ts(R("FA"), R("Y0"), 0.0, Op.is_equal, 8388608.0, Op.mult)
     tt(R("Y0"), R("Y0"), R("FA"), Op.add)
+    ops[-1]["name"] = "Y1"
     ts(R("MC"), R("MC"), P256, Op.add)
     lin(R("MC8"), R("MC"), 1.0, 0.125)
     lin(R("C1"), R("MC"), 1.0, 2049.0)
@@ -565,7 +612,7 @@ def depend(ops):
 def tag(o):
     w = o["wr"][0]
     s = w[1].rstrip("01234H") if w[1][0] != "p" else w[1]
-    return "%s %s %s%d" % (o["part"], o["kind"], s, w[2])
+    return "%s %s %s" % (o["part"], o["kind"], o.get("name", s + str(w[2])))
 
 
 def lat(o):
@@ -642,44 +689,203 @@ def replay(ops, costs, wait, order, eng, extra):
     return max(end)
 
 
+def queues(ops):
+    pool, used, seq = {}, set(), {"V": [], "S": []}
+    for i, o in enumerate(ops):
+        p, k, w = tag(o).split()
+        pool.setdefault((o["vis"], p[0]), []).append((w, i))
+    lists = {"V": [V_FIRST] + [V_MID] * (VI - 2) + [V_LAST], "S": [S_FIRST] + [S_MID] * (VI - 2) + [S_LAST]}
+    for star in (False, True):
+        for e in "VS":
+            steps = [(v + {"<": -1, ">": 1}.get(t[0], 0), t.lstrip("<>")) for v in range(VI) for t in lists[e][v].split()]
+            for n, (v, t) in enumerate(steps):
+                p, w = t.split(".")
+                if w.endswith("*") == star:
+                    got = [i for x, i in pool[(v, p)] if e in ops[i]["cost"] and i not in used and (x.startswith(w[:-1]) if star else x == w)]
+                    got = got if star else got[:1]
+                    used.update(got)
+                    seq[e] += [(n, i) for i in got]
+    rank, seen, steps = {}, {}, P_ALL.split()
+    for i, o in enumerate(ops):
+        if o["kind"] == "mm":
+            p, k, w = tag(o).split()
+            t = p[0] + "." + w
+            c = [n for n, x in enumerate(steps) if x.lstrip(">") in (t, p[0])]
+            seen[(o["vis"], t)] = seen.get((o["vis"], t), 0) + 1
+            n = c[min(seen[(o["vis"], t)], len(c)) - 1]
+            rank[i] = 100 * (o["vis"] - (steps[n][0] == ">")) + n + i * 1e-5
+    return dict([(e, [i for _, i in sorted(seq[e])]) for e in "VS"]), rank
+
+
+def first_plan(ops, wait):
+    n, (seq, rank) = len(ops), queues(ops)
+    eng = [list(o["cost"])[0] for o in ops]
+    for e in "VS":
+        for i in seq[e]:
+            eng[i] = e
+    ramps = [i for i in range(n) if ops[i]["kind"] == "iota"]
+    sends = [i for i in range(n) if ops[i]["kind"] == "rdma"]
+    seq["G"] = ramps[:22] + sends[:1] + ramps[22:] + sends[1:]
+    seq["Y"] = sorted([i for i in range(n) if eng[i] == "Y"], key=lambda i: tag(ops[i])[-3:] in ("yz0", "yc0"))
+    seq["S"] = [i for i in range(8) if eng[i] == "S"] + seq["S"]
+    seq = dict([(e, seq[e][::-1]) for e in seq])
+    left, end, start = [len(o["pre"]) for o in ops], [0.0] * n, [0.0] * n
+    free, last, pipe, ready = dict([(e, 0.0) for e in "VSPGY"]), {}, 0.0, []
+
+    def when(i):
+        t = max([free[eng[i]]] + [end[j] + wait for j, hard in ops[i]["pre"] if hard or eng[j] != eng[i]])
+        return max([t] + [end[j] + wait for b in ops[i]["banks"] for e, j in last.get(b, {}).items() if e != eng[i]])
+
+    for _ in range(n):
+        c = [(when(seq[e][-1]), seq[e][-1]) for e in "VSGY" if seq[e] and not left[seq[e][-1]]]
+        p = [(when(i), i) for i in ready]
+        if p and (not c or min(p)[0] <= min(c)[0]):
+            t, i = min([x for x in p if x[0] <= min(p)[0] + 0.15], key=lambda x: rank[x[1]])
+            ready.remove(i)
+        else:
+            t, i = min(c)
+            seq[eng[i]].pop()
+        o = ops[i]
+        free[eng[i]] = t + o["cost"][eng[i]]
+        for b in o["banks"]:
+            last.setdefault(b, {})[eng[i]] = i
+        if o["lag"] < 0:
+            pipe = max(pipe, t + 1.6) - o["lag"]
+        start[i], end[i] = t, pipe if o["lag"] < 0 else free[eng[i]] + o["lag"]
+        for j in o["succ"]:
+            left[j] -= 1
+            if not left[j] and eng[j] == "P":
+                ready.append(j)
+    return start, eng
+
+
+def run(ops, cost, wait, order, eng):
+    n = len(ops)
+    end, why, res = [0.0] * n, [None] * n, [True] * n
+    free, prev, last, pipe = dict([(e, 0.0) for e in "VSPGY"]), {}, dict([("p%d" % b, {}) for b in range(8)]), 0.0
+    for i in order:
+        o, e = ops[i], eng[i]
+        t, w = free[e] - wait, prev.get(e)
+        for j, hard in o["pre"]:
+            if end[j] > t and (hard or eng[j] != e):
+                t, w, res[i] = end[j], j, False
+        for b in o["banks"]:
+            lb = last[b]
+            for e2, j in lb.items():
+                if end[j] > t and e2 != e:
+                    t, w, res[i] = end[j], j, True
+            lb[e] = i
+        t += wait + cost[i][e]
+        free[e], prev[e], why[i] = t, i, w
+        if o["lag"] < 0:
+            pipe = max(pipe, t + 1.54) - o["lag"]
+            end[i] = pipe
+        else:
+            end[i] = t + o["lag"]
+    return max(end), end, why, res
+
+
+def arrange(ops, costs):
+    n = len(ops)
+    seen, cls = {}, []
+    for i, o in enumerate(ops):
+        o["pre"] = [(j, bool(raw) or (bool(ops[j]["sem"]) and raw is not None)) for j, raw in o["dep"].items()]
+        o["lag"] = -o["lat"] / DBW if o["kind"] == "dma" else o["lat"]
+        o["succ"] = []
+        for j in o["dep"]:
+            ops[j]["succ"].append(i)
+        seen[(tag(o), o["vis"])] = seen.get((tag(o), o["vis"]), 0) + 1
+        cls.append((tag(o), seen[(tag(o), o["vis"])]))
+    succ = [o["succ"] for o in ops]
+    start, eng = first_plan(ops, MODELS[0][4])
+    engs = dict([(cls[i], eng[i]) for i in range(n)])
+    heads = [i for i in range(n) if cls[i][0].endswith("tt AO0")]
+    x = [PARAM["seed"]]
+
+    def draw(k=0):
+        x[0] = (x[0] * 1103515245 + 12345) % 2147483648
+        return int(k * x[0] / 2147483648.0) if k else x[0] / 2147483648.0
+
+    def value(tau, engs, vis):
+        key = [tau[c] + v for c, v in zip(cls, vis)]
+        for i in range(n - 1, -1, -1):
+            for j in succ[i]:
+                if key[j] <= key[i]:
+                    key[i] = key[j] - 1e-4
+        eng = [engs[c] for c in cls]
+        order = sorted(range(n), key=lambda i: key[i])
+        rs = [run(ops, costs[m], MODELS[m][4], order, eng) for m in PARAM["models"]]
+        return sum([r[0] / WEIGHT[m] for r, m in zip(rs, PARAM["models"])]), rs, key, eng, order
+
+    def meets(cur):
+        edges = []
+        for _, end, why, res in cur[1]:
+            i = end.index(max(end))
+            while why[i] is not None:
+                if res[i] and why[i] not in ops[i]["dep"]:
+                    edges.append((why[i], i))
+                i = why[i]
+        return edges
+
+    for rounds in range(PARAM["rounds"]):
+        per = start[heads[2]] - start[heads[1]]
+        off = {0: start[heads[0]] - per, 2: start[heads[1]], VI - 1: start[heads[3]]}
+        vis = [o["vis"] * per for o in ops]
+        tau = dict([(cls[i], start[i] - off[o["vis"]] if o["kind"] != "dma" else i * 0.01 - 100 if i < 8 else 100.0)
+                    for i, o in enumerate(ops) if o["vis"] in off])
+        best = cur = value(tau, engs, vis)
+        edges, keep = meets(cur), engs
+        for it in range(PARAM["iters"]):
+            key, eng = cur[2], cur[3]
+            j, i = edges[draw(len(edges))]
+            t2, e2, u = dict(tau), engs, draw()
+            d = (0.001, 0.001, 0.001, 0.2, 0.5, 1.0, 2.0, 4.0)[draw(8)]
+            flex = [a for a in (i, j) if len(ops[a]["cost"]) > 1]
+            if u >= 0.92:
+                i = draw(n)
+                t2[cls[i]] = key[i] - vis[i] + (draw() - 0.5) * d * 2
+                flex = [i] if len(ops[i]["cost"]) > 1 and draw() < 0.5 else []
+            if flex and (u < 0.2 or u >= 0.92):
+                a = flex[draw(len(flex))]
+                e2 = dict(engs)
+                e2[cls[a]] = "V" if eng[a] == "S" else "S"
+            elif u < 0.55:
+                t2[cls[i]] = key[j] - vis[i] - d
+            elif u < 0.92:
+                stack = [(j, key[i] + d)]
+                while stack:
+                    a, k = stack.pop()
+                    if key[a] < k and t2[cls[a]] + vis[a] < k and a != i:
+                        t2[cls[a]] = k - vis[a]
+                        stack += [(b, k + 1e-3) for b in succ[a]]
+            new = value(t2, e2, vis)
+            if new[0] <= cur[0] + PARAM["slack"] * draw() * (1 - it / PARAM["iters"]):
+                cur, tau, engs = new, t2, e2
+                edges = meets(cur)
+                if new[0] < best[0]:
+                    best, keep = new, e2
+        engs = keep
+        start = [best[1][0][1][i] - costs[PARAM["models"][0]][i][best[3][i]] - max(0.0, ops[i]["lag"]) for i in range(n)]
+    return best[4], best[3]
+
+
 def plan():
     ops = build(*MODELS[0])
     costs = [[o["cost"] for o in build(*m)] for m in MODELS]
-    wait = MODELS[0][4]
     depend(ops)
-    n = len(ops)
-    succ = [[] for _ in ops]
-    for i, o in enumerate(ops):
-        for j in o["dep"]:
-            succ[j].append(i)
-    pr = [0.0] * n
-    for i in reversed(range(n)):
+    order, eng = arrange(ops, costs)
+    ts = [run(ops, c, m[4], order, eng)[0] for c, m in zip(costs, MODELS)]
+    _, end, why, _ = run(ops, costs[0], MODELS[0][4], order, eng)
+    last = {}
+    for i in order:
         o = ops[i]
-        pr[i] = min(o["cost"].values()) + max([pr[j] + (0.0 if ops[j]["dep"][i] is None else lat(o) + wait) for j in succ[i]] + [lat(o)])
-    tags = [tag(o) for o in ops]
-    pool = sorted(set(tags)) + 3 * sorted(set([t for t in tags if tags.count(t) >= 4]))
-    x, best, boost = [PARAM["seed"]], None, dict(BOOST)
-
-    def draw():
-        x[0] = (x[0] * 1103515245 + 12345) % 2147483648
-        return x[0] / 2147483648.0
-
-    for it in range(PARAM["iters"]):
-        trial = dict(boost)
-        for _ in range((1, 1, 2, 3, 5)[int(5 * draw())] if it else 0):
-            t = pool[int(len(pool) * draw())]
-            trial[t] = round(trial.get(t, 0.0) + (draw() + draw() - 1.0) * (1.5, 5.0, 15.0, 35.0)[int(4 * draw())], 1)
-        order, eng, start, end, extra = schedule(ops, succ, [p + trial.get(t, 0.0) for p, t in zip(pr, tags)], PARAM["look"], wait)
-        ts = [replay(ops, c, m[4], order, eng, extra) for c, m in zip(costs, MODELS)]
-        val = sum([a / b for a, b in zip(ts, WEIGHT)])
-        if best is None or val <= best[0]:
-            best, boost = (val, order, eng, start, end, ts, extra), trial
-    ops[0]["boost"] = boost
-    _, order, eng, start, end, ts, extra = best
-    for i in range(n):
-        for j in extra[i]:
-            ops[i]["dep"].setdefault(j, False)
-        ops[i]["eng"], ops[i]["start"], ops[i]["end"], ops[i]["ts"] = eng[i], start[i], end[i], ts
+        for b in o["banks"]:
+            for e, j in last.setdefault(b, {}).items():
+                if e != eng[i]:
+                    o["dep"].setdefault(j, False)
+            last[b][eng[i]] = i
+        o["eng"], o["end"], o["ts"], o["why"] = eng[i], end[i], ts, why[i]
+        o["start"] = end[i] - o["cost"][eng[i]] - max(0.0, o["lag"])
     close = {}
     for i in order:
         if ops[i]["acc"]:
@@ -776,6 +982,11 @@ def rank_program(g, core, T, topo):
                 ins = q.tensor_copy(ap(T, a[0]), ap(T, a[1]))
             else:
                 ins = q.tensor_scalar(ap(T, a[0]), ap(T, a[1]), ap(T, a[2]), a[3], Op.mult, Op.add)
+        elif k == "step":
+            if e == "S":
+                ins = q.activation(ap(T, a[0]), ap(T, a[1]), Act.Relu, bias=ap(T, a[3]), scale=2.0)
+            else:
+                ins = q.tensor_scalar(ap(T, a[0]), ap(T, a[1]), ap(T, a[2]), KS, Op.is_gt, Op.mult)
         elif k == "act":
             ins = q.activation(ap(T, a[0]), ap(T, a[1]), a[2], bias=ap(T, a[4]), scale=a[3])
         elif k == "scan":

from concourse.bass import DstId, RemoteDMATransfer
from concourse.mybir import dt, AluOpType, AxisListType, ActivationFunctionType

W, L, VI, NR = 4096, 256, 5, 4
F32, BF, F16, I32, U16 = "float32", "bfloat16", "float16", "int32", "uint16"
SCRATCH = {}


def _sb(dtype, cols, names):
    for n in names.split():
        SCRATCH[n] = ("sbuf", [128, cols], dtype)


_sb(BF, 256 + 2 * W, "XW")
_sb(I32, W, "MI")
_sb(F32, W, "PG TT")
_sb(F32, W + 256, "CT YT")
_sb(BF, W, "OH XG AB EQ")
_sb(F16, W, "PB AO")
_sb(F16, 2048, "RB")
_sb(BF, 2048, "TRI")
_sb(BF, 1024, "SEL")
_sb(BF, 480, "CK")
_sb(F32, 768, "ST BB")
_sb(F16, 512, "P4H")
_sb(F32, 256, "MX AA MV SV DD MP DL YV DC MASK KM KET MX2 EQT I6 I7 Y0 RT MC MC8 C1 FA FB")
_sb(I32, 256, "RP PR PR2 QQ QQ2 NN O0 O1 O2 O3 O4 N0 N1 N2 N3 N4")
_sb(U16, 256, "REPU R0U NU MU SU U0 U1 U2 U3 U4 V0 V1 V2 V3")
_sb(F16, 256, "CREP FLH MH SL KP H1 H2 RH0 FL0 OWN Z0 Z1 Z2 Z3 Z4 Y0H Y1H Y2H Y3H Y4H")
_sb(BF, 256, "ZIN ZT HC HF EMP DC2")
_sb(F32, 160, "J32 B32")
_sb(BF, 3 * 160, "BB16")
_sb(F16, 4 * 160, "BH16")
_sb(BF, 5 * 128, "IB")
_sb(F16, 5 * 128, "IH")
_sb(F32, 128, "BO32 G8 BOA KT3 RMM WB32")
_sb(BF, 64, "KT1")
_sb(F32, 64, "TY")
_sb(F32, 80, "AL")
_sb(F32, 16, "CB COL")
_sb(F16, 96, "LH")
_sb(I32, 16, "CI TH")
_sb(U16, 80, "LI")
for _i in range(8):
    SCRATCH["p%d" % _i] = ("psum", [128, 512], F32)

DSEMS = ["d%d" % i for i in range(16)]
SEMAPHORES = ["sV", "sS", "sP", "sG", "sent"] + DSEMS + ["ao%d" % v for v in range(1, VI)] + ["az%d%d" % (v, h) for v in range(1, VI) for h in range(2)]

SHAPES = {"feat": 4096, "memb": 4096, "rep": 4096, "fact": 256, "z": 256, "thr": 2, "yc": 4096, "yr": 4096, "yo": 256, "yz": 256}
SIZE = {F32: 4, I32: 4, BF: 2, F16: 2, U16: 2}
Op, Act = AluOpType, ActivationFunctionType

MODELS = [(0.00083, 0.00042, 1.56, 3.8, 0.2), (0.00104, 0.00052, 1.3, 3.0, 0.2), (0.00115, 0.00058, 1.9, 5.0, 0.2), (0.0009, 0.00045, 1.2, 2.5, 0.3)]
WEIGHT = [160.0, 180.0, 240.0, 165.0]
DBW = 190000.0
PARAM = {"rot": 3, "look": 0.6, "seed": 1, "rounds": 4, "iters": 1800, "models": (0, 2), "slack": 0.0012,
         "a": [["VS"] * 4] * 5, "c": [["VS"] * 4] * 5, "d": [["VS"] * 4] * 5}

V_END = """ y.DC0 w.KET0 q.L80 w.MX0 w.KP0 w.EQT0 x.L64 w.L48 w.p5256 k.MP128 w.SL0 k.M128 w.TY32 w.DL0 w.LI32 w.KET128 w.CT0 w.MX128
    w.KP128 x.TY48 w.L56 w.EQT128 x.L72 x.LI48 w.p6256 x.DC0 w.SL128 w.TY40 n.COL13 w.LI40 w.DL128 w.CT0 """
V_HEAD = """ b.AO0 <x.DC128 b.AO1024 <n.CI9 b.AO2048 b.AO3072 <s.YT0 c.XG2048 f.PR0 <n.CI8 m.MX0 <n.COL12 m.AA0 f.QQ0 m.BB0 m.BB256
    m.ST0 m.BB512 k.TY0 m.LI0 m.ST256 m.ST512 f.MASK0 m.MV0 m.L0 m.L8 m.MU0 f.p40 k.CB0 m.PR0 k.CREP0 m.QQ0 m.MX128 m.SV0 m.AA128
    f.MASK128 m.SU0 m.BB128 m.BB384 f.p40 m.BB640 m.ST128 m.ST384 f.NN0 m.LI8 m.ST640 k.TY8 m.L16 f.N0 m.L24 e.XG0 k.DD0 m.PR128
    k.CB8 e.XG1024 k.HF0 m.QQ128 k.HC0 k.DD128 m.SV128 q.EQ* m.SU128 k.HF128 y.LI16 k.HC128 e.XG2048 e.XG3072 """
V_MID = V_HEAD + V_END + " x.TY56 x.LI56 "
V_FIRST = """ r.* g.TT0 u.turn j.COL8 g.TT1024 l.COL4 l.COL7 l.G80 l.TY0 g.TT2048 l.SEL0 g.TT3072 l.SEL256 l.COL9 l.COL12 l.COL10 l.COL11
    l.RMM0 l.AL32 l.SEL512 l.RMM0 l.AL32 l.SEL768 a.PB0 a.PB2048 a.R0U0 a.R0U64 c.XG1024 a.R0U128 a.R0U192 z.L32 c.XG3072 l.* h.FL0
    f.PR0 h.FB0 f.QQ0 h.FA0 h.REPU0 f.p40 h.OWN0 m.MX0 k.TY0 m.AA0 f.MASK0 m.BB0 m.BB256 m.ST0 m.ST256 m.LI0 m.L0 m.L8 k.CB0 t.O0
    m.MX128 k.CREP0 m.AA128 f.MASK128 m.BB128 m.BB384 f.p40 m.ST128 m.ST384 f.NN0 m.LI8 m.L16 f.N0 m.L24 m.MV0 k.TY8 m.MV128 m.MU0
    m.PR0 f.V0 m.MU128 m.QQ0 k.CB8 m.PR128 m.SV0 m.QQ128 k.CREP128 m.SV128 t.O1024 t.O2048 t.O3072 q.EQ* t.TT0 k.DD0 t.TT512
    k.DD128 t.TT1024 k.HC0 k.HF0 t.TT1536 k.HC128 k.HF128 t.TT* e.XG0 y.LI16 e.XG1024 e.XG2048 e.XG3072 """ + V_END + " x.TY56 x.LI56 "
V_LAST = V_HEAD + " i.MC0 " + V_END.replace("k.MP128", "f.turn").replace("k.M128", "").replace("n.COL13", "") + """ o.PG0 x.TY56 o.PG1024
    x.LI56 o.PG2048 s.YT0 o.PG3072 i.FA0 x.DC128 i.Y1 o.DD0 o.p30 o.p3128 o.RT0 o.p3128 o.FA0 o.FB0 o.p3256 o.p3384 o.DD128 o.FA128
    o.p3384 o.FB128 """
S_HEAD = """ a.R0U128 a.FL128 <s.KM0 a.R0U192 a.FL192 <s.YV0 z.ZT0 <x.Y128 b.NU0 c.XG0 b.NU64 c.XG1024 b.NU128 c.AB0 c.AB512 z.L32
    c.AB1024 z.ZT128 b.NU192 c.AB1536 c.XG3072 c.AB2048 c.AB2560 c.AB3072 c.AB3584 k.EMP0 d.XG0 d.XG1024 m.MV128 k.MP0 m.MU128 """
S_MID = S_HEAD + """ f.V0 d.XG2048 k.CREP128 e.AB0 e.AB512 d.XG3072 k.EMP128 k.M0 >a.PB0 e.AB1024 e.AB1536 >a.PB1024 e.AB2048 e.AB2560
    e.AB3072 e.AB3584 y.DC0 >a.R0U0 >a.FL0 >a.PB2048 y.XW0 >a.R0U64 >a.FL64 x.Y0 >a.PB3072 """
S_FIRST = """ u.R0 j.IB0 j.I0 u.0 j.BH16160 j.BH16320 g.TT512 u.Z0 g.TT1536 u.U0 g.TT2560 g.TT3584 u.O0 a.PB1024 a.PB3072 z.ZT0 z.ZT128
    j.BB160 j.KT0 c.XG0 j.p30 j.IB512 c.AB0 c.AB512 c.AB1024 c.AB1536 c.XG2048 c.AB* j.* h.AO0 h.AO512 h.AO1024 d.XG0 h.AO1536
    h.AO2048 d.XG1024 m.SU0 m.SU128 h.AO* k.EMP0 k.EMP128 d.XG2048 d.XG3072 k.M0 k.MP0 e.AB0 e.AB512 >a.PB0 e.AB1024 e.AB1536
    >a.PB1024 e.AB2048 e.AB2560 e.AB3072 e.AB3584 y.DC0 >a.R0U0 >a.FL0 >a.PB2048 y.XW0 >a.R0U64 >a.FL64 x.Y0 >a.PB3072 """
S_LAST = S_HEAD + """ d.XG2048 k.CREP128 e.AB0 e.AB512 d.XG3072 k.EMP128 k.M0 k.M128 k.MP128 f.0 e.AB1024 e.AB1536 i.PB0 i.PB512
    i.PB1024 e.AB2048 e.AB2560 i.PB1536 e.AB3072 e.AB3584 y.DC0 f.MASK0 i.PB2048 y.XW0 i.PB* x.Y0 s.KM0 i.Y0 s.YV0 i.MC80 i.C0
    x.Y128 x.SV0 o.yr0 """
P_ALL = """ g u l a.p2192 z.p3256 b.p2256 c.z0 c.z1 c.z2 b.p2320 c.x0 c.x1 b.p2384 c.x2 b.p2448 c.z3 c.x3 z.p3384 c.p50 c.p564 z.p4256
    c.z4 c.x4 z.p40 c.z5 c.x5 c.z6 c.x6 c.z7 c.x7 m.p5128 c.p60 c.p664 h m.p6128 k.p50 k.p60 t e.z0 e.z1 e.z2 e.x0 e.x1 e.z3 k.p50
    e.p50 e.z4 e.x2 e.x3 q.p516 q.p50 k.p60 e.z5 e.p564 e.x4 e.x5 q.p60 q.p60 q.p4272 e.z6 e.z7 e.x6 e.x7 w.p40 w.p5128 e.p60
    e.p664 y.p3256 x.c0 >a.p20 f.p40 w.p48 w.p6128 x.c1 >a.p264 >a.p2128 s.p5128 s.p6128 n.p4288 i.p20 o """
ZO = 1536.0
KS = 8192.0
BAND = 131072.0
LOW = 5120.0
RND = 12582912.0


def R(name, lo=0, hi=None, st=1, p=None):
    if hi is None:
        hi = SCRATCH[name][1][1] if name in SCRATCH else SHAPES[name]
    return ("R", name, lo, hi, st, p)


def X(win, off):
    return ("X", win, off)


def cnt(a):
    return 16 * cnt(a[2]) if a[0] == "X" else (a[3] - a[2] + a[4] - 1) // a[4]


def isap(a):
    return isinstance(a, tuple)


def regs(a):
    return [a[1], a[2]] if a[0] == "X" else [a]


def inps(a):
    return a[0] == "R" and a[1] in SCRATCH and SCRATCH[a[1]][0] == "psum"


def width(a):
    return SIZE[SCRATCH[(a[1] if a[0] == "X" else a)[1]][2]]


def ap(T, a):
    if not isap(a):
        return a
    if a[0] == "X":
        return ap(T, a[1]).indirect(ap(T, a[2]))
    t = T[a[1]]
    ps = slice(None) if a[5] is None else slice(*a[5])
    return t[ps, a[2]:a[3]] if a[4] == 1 else t[ps, a[2]:a[3]:a[4]]


def build(CY, PCY, GA, SC, LAT=0.0):
    ops = []
    nd, cur, turns, starts = [0], ["s", "0", 0], [0], []

    def add(cost, kind, args, wr, rd, acc=None, lat=0.0, sem=None):
        rr = []
        for a in rd:
            if isap(a):
                rr += regs(a)
        ww = []
        for a in wr:
            ww.append(regs(a)[0])
            rr += regs(a)[1:]
        ops.append({"cost": cost, "kind": kind, "args": args, "wr": ww, "rd": rr, "acc": acc, "lat": lat, "sem": sem, "prev": [], "part": cur[0] + cur[1], "vis": cur[2]})

    def chain(lst):
        for a, b in zip(lst, lst[1:]):
            ops[b]["prev"].append(a)

    def vcost(out, ins, two=False):
        if out[0] == "X":
            return 0.05 + SC * cnt(out) * CY
        if ins[0][0] == "X":
            return 0.05 + GA * cnt(out) * CY
        n = cnt(out)
        if two:
            c = 1.0 if (inps(ins[0]) or inps(ins[1])) else 2.0
        else:
            c = 0.5 if max([width(a) for a in [out] + ins]) == 2 else 1.0
        return max(64, c * n) * CY

    def scost(out, a):
        return 0.065 + GA * cnt(out) * CY if a[0] == "X" else max(64, cnt(out)) * CY + 0.03

    def tt(out, a, b, op):
        add({"V": vcost(out, [a, b], True)}, "tt", (out, a, b, op), [out], [a, b])

    def ts(out, a, s1, op0, s2=None, op1=None):
        add({"V": vcost(out, [a])}, "ts", (out, a, s1, s2, op0, op1), [out], [a, s1, s2])

    def lin(out, a, scale=1.0, bias=0.0, eng="VS", fn=Act.Identity):
        c = {}
        if "V" in eng:
            c["V"] = vcost(out, [a])
        if "S" in eng:
            c["S"] = scost(out, a)
        add(c, "lin", (out, a, scale, bias, fn), [out], [a, scale])

    def act(out, a, fn, scale=1.0, bias=0.0):
        add({"S": scost(out, a)}, "act", (out, a, fn, scale, bias), [out], [a, bias])

    def step(out, a, t, t2):
        add({"V": vcost(out, [a]), "S": scost(out, a)}, "step", (out, a, t, t2), [out], [a, t, t2])

    def scan(out, d0, d1, op0, op1):
        add({"V": vcost(out, [d0, d1])}, "scan", (out, d0, d1, 0.0, op0, op1), [out], [d0, d1])

    def tr(out, a):
        add({"V": vcost(out, [a])}, "tr", (out, a), [out], [a])

    def red(out, a):
        add({"V": max(64, cnt(a)) * CY}, "red", (out, a), [out], [a])

    def ms(out, val):
        add({"V": vcost(out, [out])}, "ms", (out, val), [out], [])

    def mm(lst, acc=None):
        if len(lst[0]) == 3:
            lst = [m + (i == 0 and not (acc and acc[0] == "acc"), i == len(lst) - 1 and not acc) for i, m in enumerate(lst)]
        c = sum([max(64, cnt(m[2])) * (4 if width(m[2]) == 4 else 1) for m in lst]) * PCY + 0.03
        add({"P": c}, "mm", lst, [m[0] for m in lst], [m[1] for m in lst] + [m[2] for m in lst], acc)

    def iota(out, pat, base, ch=0):
        add({"G": 0.13 + 2 * cnt(out) * CY}, "iota", (out, pat, base, ch), [out], [])

    def dma(out, a, nbytes, q="Y"):
        add({q: 0.06}, "dma", (out, a), [out], [a], lat=nbytes, sem=(DSEMS[nd[0]], 16))
        nd[0] += 1

    def rdma(pairs, sem):
        add({"G": 0.3 * len(pairs)}, "rdma", pairs, [x[0] for x in pairs], [x[1] for x in pairs], lat=2.0, sem=(sem, len(pairs)))

    CL, CE, HL = 64, 1024, 128
    col = lambda i: R("COL", i, i + 1)
    PF, PM, PG8, P32, P32B, PAR0, PAR1, NPM, KP1, T1X, TMX, TKX, TWX, AI, P256 = [col(i) for i in range(15)]
    CKM = 2048.0 - 8192.0
    ci = lambda i: R("CI", i, i + 1)
    ty = lambda i: R("TY", 16 * i, 16 * i + 16)
    li = lambda i, h=None: R("LI", 16 * i, 16 * i + 16) if h is None else R("LI", 16 * i + 8 * h, 16 * i + 8 * h + 8)
    al = lambda i: R("AL", 16 * i, 16 * i + 16)
    XA, XD, XZ = R("XW", 256, 256 + W), R("XW", 256, 256 + 2 * W), R("XW", 0, 256 + W)
    CG = R("CT", 0, W)
    names = {"BKD": 0, "BN16": 1, "BN1": 2, "BHF": 0, "B16": 1, "B1H": 2, "BK1": 3}
    ids = {"IP": 0, "IK": 1, "IKN": 2, "IBG": 3, "BOK": 4, "I1": 0, "IN1": 1, "I30": 2, "BOH": 3, "I8K": 4}

    def bv(n, k):
        if n == "B32":
            return R(n, 15 - k, 143 - k)
        o = 160 * names[n]
        return R("BB16" if n[1] in "KN" and n != "BK1" else "BH16", o + 15 - k, o + 143 - k)

    def im(n):
        return R("IB" if n in ("IP", "IK", "IKN", "IBG", "BOK", "BO1") else "IH", 128 * ids[n], 128 * ids[n] + 128)

    C2048, CN8, CR0, CGOT, CM2048 = [lambda n, o=o: R("CK", o, o + n) for o in (0, 256, 384, 448, 464)]
    rb = lambda r: R("RB", 128 * r, 128 * r + 128)

    dma(R("RP"), R("rep"), 131072)
    dma(R("NN"), R("fact"), 131072)
    dma(R("ZIN"), R("z"), 65536, "S")
    dma(R("TH", 0, 2, 1, (0, 8)), R("thr"), 64, "S")
    dma(XA, R("feat"), 1048576)
    for c in range(2):
        dma(R("MI", 2048 * c, 2048 * c + 2048), R("memb", 2048 * c, 2048 * c + 2048), 1048576)
    dma(R("XW", 256 + W, 256 + 2 * W), R("feat"), 1048576)
    chain([0, 1, 4, 5, 6, 7])

    cur[0] = "r"
    iota(ci(0), [[0, 1]], 0, 1)
    iota(R("G8"), [[1, 8], [0, 16]], 0)
    iota(al(0), [[1, 16]], 0)
    iota(R("J32"), [[1, 160]], -16, -1)
    iota(R("I6"), [[0, 16], [1, 16]], 0)
    iota(R("I7"), [[1, 16], [0, 16]], 0)
    for o, n, val in ((0, 256, 2048.0), (256, 128, -0.125), (384, 64, -14336.0), (448, 16, -47104.0), (464, 16, -2048.0)):
        ms(R("CK", o, o + n), val)
    ms(R("B32"), 0.0)
    ms(ci(8), 0)
    for i, (s, op) in enumerate(((15, Op.bitwise_and), (4, Op.arith_shift_right), (31, Op.bitwise_and), (16, Op.bitwise_and))):
        ts(ci(1 + i), ci(0), s, op)
    lin(R("COL", 0, 4), R("CI", 0, 4), eng="V")
    ts(PAR0, ci(4), 0.0, Op.is_equal)
    ts(PAR1, ci(4), 16.0, Op.is_equal)
    ts(im("BOH"), R("G8"), PG8, Op.is_equal)
    ts(al(1), al(0), PM, Op.is_equal)
    ts(R("BO32"), R("G8"), PG8, Op.is_equal)
    ts(R("J32"), R("J32"), 0.0, Op.is_equal)
    for r in range(16):
        lin(rb(r), im("BOH"), R("AL", 16 + r, 17 + r), eng="V")
    for b in range(2):
        for e in range(2):
            o, q = 16 + 16 * (b - e), 128 * (2 * b + e)
            ts(R("P4H", q, q + 128), R("J32", o, o + 128), PAR1 if b else PAR0, Op.mult)
    lin(R("B32", 15, 143, 16), R("BO32", 0, 128, 16), eng="V")
    cur[0] = "j"
    for n, s in (("IP", 1.0), ("I1", 1.0), ("IK", BAND), ("IKN", -BAND), ("IBG", -LOW), ("IN1", -1.0), ("I30", -30.0), ("I8K", 8192.0)):
        lin(im(n), R("J32", 16, 144), s)
    ts(KP1, ci(1), 1.0, Op.add)
    for n, s in (("B16", 0.0625), ("B1H", 1.0), ("BKD", 16 * KS), ("BN16", -16.0), ("BN1", 8192.0), ("BHF", 0.5), ("BK1", KP1)):
        a = bv(n, 15)
        lin(R(a[1], a[2], a[2] + 160), R("B32"), s)
    lin(R("KT1"), R("I6", 0, 64), -KS)
    lin(R("p3", 0, 256), R("I6"), 37.0)
    lin(im("BOK"), R("BO32"), BAND)
    lin(R("BOA"), R("BO32"), -1.0 / 8192)
    lin(R("WB32"), R("BO32"), KP1)
    cur[0] = "l"
    ts(P32B, ci(3), -16.0, Op.add)
    ts(NPM, ci(1), -1.0, Op.mult)
    ts(R("G8"), R("G8"), PF, Op.is_equal)
    lin(R("TY", 0, 2, 1, (0, 8)), R("TH", 0, 2, 1, (0, 8)), eng="V")
    for i, (src, p) in enumerate((("I6", P32), ("I6", P32B), ("I7", P32), ("I7", P32B))):
        ts(R("SEL", 256 * i, 256 * i + 256), R(src), p, Op.is_equal, -1.0, Op.mult)
    mm([(R("p7", 0, 2), R("G8", 0, 128, 1, (0, 8)), R("TY", 0, 2, 1, (0, 8)))])
    ts(R("RMM"), R("I6", 0, 128), 0.0, Op.is_gt, 8e9, Op.mult)
    ts(al(2), al(0), PM, Op.is_gt)
    ts(T1X, R("p7", 0, 1), 16 * KS, Op.mult, KS / 2, Op.add)
    ts(TWX, R("p7", 0, 1), 16 * KS, Op.mult, KS / 2, Op.add)
    ts(TMX, R("p7", 0, 1), -32 * KS, Op.mult, -KS, Op.add)
    ts(TKX, R("p7", 1, 2), 16.0, Op.mult, NPM, Op.add)
    ts(R("RMM"), R("RMM"), -4e9, Op.add)
    tt(al(2), al(2), al(1), Op.subtract)
    ts(li(4), al(0), 16.0, Op.mult, 15.0, Op.add)
    ts(al(3), al(0), 16.0, Op.mult, PM, Op.add)
    ts(R("KT3"), R("I6", 0, 128), 0.0, Op.mult, TKX, Op.add)
    ts(P256, ci(1), 256.0, Op.mult)
    ts(al(4), al(3), 2048.0, Op.add)
    for r in range(16):
        lin(R("TRI", 128 * r, 128 * r + 128), im("BOK"), R("AL", 32 + r, 33 + r), eng="V")
    ts(al(3), al(3), -255.0, Op.add)
    ramps = []
    for name, o, pat, base, inc in (("PG", 0, [[1, 32], [256, 16]], 0, 32), ("CT", 0, [[1, 512]], -2048, 512), ("YT", 256, [[0, 512]], 8388608, 0)):
        for h in range(8):
            iota(R(name, o + 512 * h, o + 512 * h + 512), pat, base + inc * h)
            ramps.append(len(ops) - 1)
    iota(R("MC"), [[1, 256]], -2048)
    chain([8, 9, 10, 11, 12, 13] + ramps + [len(ops) - 1])

    def turn(src, out):
        tr(R("H2"), src)
        ops[-1]["name"] = "turn"
        mm([(R(out, 32 * b + 16 * x, 32 * b + 16 * x + 16), R("P4H", 128 * (2 * x + y), 128 * (2 * x + y) + 128),
             R("H2", 32 * b + 16 * y, 32 * b + 16 * y + 16), y == 0, y == 1) for b in range(8) for x in range(2) for y in range(2)])

    def spread(bank, src, t):
        mm([(R(bank, 256 * i, 256 * i + 256), rb(2 * t + i), R(src), True, True) for i in range(2)])

    cur[0] = "u"
    lin(R("RH0"), R("RP"), 1.0, -2048.0)
    lin(R("H1"), R("NN"), 1.0, -2048.0)
    turn(R("H1"), "p4")
    lin(R("U0"), R("p4", 0, 256), 1.0, 2048.125)
    lin(R("O0"), R("p4", 0, 256), 1.0, 2048.125)
    lin(R("Z0"), R("ZIN"), 1.0, ZO)
    cur[0] = "g"
    for t in range(8):
        bank = ("p0", "p1", "p5", "p6")[t % 4]
        spread(bank, "RH0", t)
        lin(R("TT", 512 * t, 512 * t + 512), R(bank))
    cur[0] = "h"
    lin(R("REPU"), R("RP"))
    lin(R("FL0"), R("RP"), 1.0 / 15, 1025 - 7.0 / 15)
    lin(R("FA"), R("FL0"), -30.0, 28672.0)
    lin(R("FB"), R("RP"), 2.0)
    tt(R("OWN"), R("FA"), R("FB"), Op.add)
    cur[0] = "t"
    for c in range(4):
        tt(R("OH", CE * c, CE * c + CE), X(R("MI"), R("REPU", CL * c, CL * c + CL)), R("PG", CE * c, CE * c + CE), Op.is_equal)

    def tables():
        cur[0] = "h"
        for t in range(8):
            bank = ("p0", "p1", "p7")[t % 3]
            spread(bank, "FL0", t)
            lin(R("AO", 512 * t, 512 * t + 512), R(bank), 2.0, -LOW)
        cur[0] = "t"
        for t in range(8):
            bank = ("p7", "p0", "p1")[t % 3]
            mm([(R(bank, 256 * i, 256 * i + 256), a, b, j == 0, j == 1) for i in range(2)
                for j, (a, b) in enumerate(((rb(2 * t + i), R("OWN")), (im("IBG"), R("OH", 2 * t + i, W, 16))))])
            tt(R("TT", 512 * t, 512 * t + 512), R(bank), R("AO", 512 * t, 512 * t + 512), Op.min)

    def extract(out, lhs, src, c):
        return [(out, bv(lhs, k), R(src, CE * c + k, CE * c + CE, 16)) for k in range(16)]

    def dist(c, sel, out, lhs, first, acc):
        for t in (2 * c, 2 * c + 1):
            bank, rows = ("p0", "p1", "p7")[turns[0] % PARAM["rot"]], (32 * (t % 4), 32 * (t % 4) + 32)
            turns[0] += 1
            mm([(R(bank), R("ZT", 128 * (t // 4), 128 * (t // 4) + 128, 1, rows), R("SEL", 512 * sel, 512 * sel + 512, 1, rows))], ("open", turns[0]))
            mm([(R(bank), im("IP"), R("XG", 512 * t, 512 * t + 512))], ("acc", turns[0]))
            ops[-2]["name"], ops[-1]["name"] = "z%d" % t, "x%d" % t
            act(R("AB", 512 * t, 512 * t + 512), R(bank), Act.Abs)
        mm(first + extract(out, lhs, "AB", c), acc)

    def tolist(bank, o, src, n):
        return [(R(bank, o + b, o + n, 2), R("P4H", 128 * (2 * b + e), 128 * (2 * b + e) + 128), R("LH", src + e, src + n, 2))
                for b in range(2) for e in range(2)]

    def pre(v):
        cur[:] = ["a", "0" if v == 0 else "4" if v == VI - 1 else "", v]
        for c in range(4):
            s = lambda n, o=0: R(n, o + CL * c, o + CL * c + CL)
            lin(R("PB", CE * c, CE * c + CE), X(R("TT"), s("U%d" % v)), 1.0, LOW if v else 0.0, eng=PARAM["a"][v][c])
            mm([(s("p2"), im("IP"), CR0(CL) if v else C2048(CL))] + extract(s("p2"), "BHF" if v else "B16", "PB", c))
            lin(s("R0U"), s("p2"), 1.0, 0.125)
            if v:
                lin(s("FLH"), s("p2"), 1.0 / 15, 1025 - 7.0 / 15)

    pre(0)
    for v in range(VI):
        O, Z, last = "O%d" % v, "Z%d" % v, v == VI - 1
        acc = [("acc", "e%d%d" % (v, h)) for h in range(2)]
        UL, FLL, WS = R("p4", 256, 272), R("p4", 272, 288), R("p4", 288, 289)
        NEW, UP4 = R("p4", 0, 256), R("p3", 256, 512)
        idle = ("p0", "p1", "p7")[(turns[0] + 13) % PARAM["rot"]]
        cur[0] = "z"
        for h in range(2):
            mm([(R("p3", 256 + HL * h, 256 + HL * h + HL), R(Z, HL * h, HL * h + HL), im("I1"))])
            lin(R("ZT", HL * h, HL * h + HL), R("p3", 256 + HL * h, 256 + HL * h + HL), 1.0, -ZO)
        mm([(UL, bv("B1H", r), R(Z, r, L, 16)) for r in range(16)])
        lin(R("LH", 32, 48), UL, 1.0, -16 * ZO - 2048)
        mm([(NEW, im("IP"), C2048(256))] + [(R("p4", k, 256, 16), im("I1"), R("LH", 32, 48)) for k in range(16)])
        cur[0] = "f"
        tt(R("PR"), R(O), NEW, Op.mult)
        ts(R("QQ"), R("PR"), 5, Op.arith_shift_right, 4095, Op.bitwise_and)
        tt(NEW, R("QQ"), R("p3", 0, 256), Op.add)
        for c in range(4):
            s = lambda n, o=0: R(n, o + CL * c, o + CL * c + CL)
            if v:
                cur[0] = "b"
                tt(R("AO", CE * c, CE * c + CE), X(CG, s("R0U")), R("PB", CE * c, CE * c + CE), Op.max)
                mm([(s("p2", 256), im("IP"), C2048(CL)), (s("p2", 256), im("I30"), s("FLH"))] + extract(s("p2", 256), "B1H", "AO", c))
                lin(s("NU"), s("p2", 256), 1.0, 0.125)
            cur[0] = "c"
            lin(R("XG", CE * c, CE * c + CE), X(XA, s("NU" if v else "R0U")), eng=PARAM["c"][v][c])
            kd = R("p%d" % (5 + c // 2), CL * (c % 2), CL * (c % 2) + CL)
            dist(c, 0, kd, "BKD", [(kd, im("IP"), R("KT1", 0, CL))], None)
        if v == 0:
            tables()
        for h in range(2):
            s = lambda n, o=0: R(n, o + HL * h, o + HL * h + HL)
            end = lambda n, o=0: R(n, o + HL * h + 15, o + HL * h + HL, 16)
            bank = "p%d" % (5 + h)
            kd, orep, crep = R(bank, 0, 128), R(bank, 128, 256), R(bank, 256, 384)
            cur[0] = "m"
            scan(s("MX"), R("RMM"), kd, Op.min, Op.max)
            tt(s("AA"), s("MX"), kd, Op.subtract)
            for j, src in ((0, s("p2")), (1, s(O)), (2, s("p2", 256))):
                if j < 2 or v:
                    tt(s("BB", 256 * j), src, s("AA"), Op.subtract)
                    scan(s("ST", 256 * j), s("AA"), s("BB", 256 * j), Op.min, Op.max)
            cl = end("ST", 512 if v else 0)
            lin(li(0, h), end("ST"), 1.0, 0.125, "V")
            lin(s("MV"), X(R("MI"), li(0, h)))
            lin(s("MU"), s("MV"), fn=Act.Relu)
            lin(R("LH", 16 * h, 16 * h + 8), end("ST", 256), 1.0, -2048.0, "V")
            ts(R("LH", 16 * h + 8, 16 * h + 16), cl, RND, Op.add, -RND - 2048, Op.add)
            mm([(R(bank, 128, 384), im("IP"), R("CK", 128, 384))]
               + [(R(bank, 128 + r, 384, 16), rb(r), R("LH", 16 * h, 16 * h + 16)) for r in range(16)])
            tt(s("PR2"), s("MV"), orep, Op.mult)
            ts(s("QQ2"), s("PR2"), 5, Op.arith_shift_right, 4095, Op.bitwise_and)
            tt(s("SV"), s("QQ2"), s("MV"), Op.add)
            lin(s("SU"), s("SV"), fn=Act.Relu)
            cur[0] = "k"
            ts(R("TY", 8 * h, 8 * h + 8), end("MX"), TWX, Op.is_le, 8192.0, Op.mult)
            tt(R("CB", 8 * h, 8 * h + 8), R("TY", 8 * h, 8 * h + 8), R("LH", 16 * h + 8, 16 * h + 16), Op.add)
            lin(s("CREP"), crep, 1.0, 0.125)
            tt(s("DD"), X(CG, li(0, h)), s("CREP"), Op.subtract)
            ts(s("HC"), s("DD"), 0.0, Op.is_equal)
            ts(s("HF"), s("DD"), 0.125, Op.is_equal)
            act(s("EMP"), s("MV"), Act.Relu, -1.0)
            lin(s("MP"), s("MV"), 1.0, -2047.875)
            lin(s("MH"), s("MV"), 1.0, -2047.0)
            cur[0] = "f"
            step(s("MASK"), kd, T1X, TMX)
            cur[0] = "k"
            mm([(kd, R("J32", 16, 144), R("KT3"))], ("open", acc[h][1]))
            chain([max([i for i, o in enumerate(ops) if o["kind"] == "mm" and o["part"][0] == "m"]), len(ops) - 1])
            mm([(kd, im(a), s(b)) for a, b in (("IK", "HC"), ("IK", "HF"), ("IKN", "EMP"))], acc[h])
        cur[0] = "f"
        tt(NEW, NEW, R("MASK"), Op.min)
        tt(R("NN"), NEW, R(O), Op.add)
        ts(R("N%d" % v), R("NN"), 4095, Op.bitwise_and)
        if last:
            lin(R("H1"), R("N%d" % v), 1.0, -2048.0)
            turn(R("H1"), "p4")
            lin(R("MASK"), NEW, 1.0, 2048.0)
            dma(R("yo"), R("MASK"), 131072)
        else:
            lin(R("V%d" % v), R("N%d" % v))
            rdma([(R("U%d" % (v + 1)), R("V%d" % v)), (R("O%d" % (v + 1)), R("N%d" % v))], "ao%d" % (v + 1))
        cur[0] = "q"
        for b in range(16):
            ts(R("EQ", 272 * b, 256 * b + 256), R("CREP", 16 * b, 256), R("CB", b, b + 1), Op.is_equal, -1.0, Op.mult)
        for h in range(2):
            bank, lo = "p%d" % (5 + h), lambda b: max(16 * b + 16, HL * h)
            mm([(R(bank, lo(b) - HL * h, HL), im("BOK"), R("EQ", 256 * b + lo(b), 256 * b + HL * h + HL)) for b in range(8 * h + 7)], acc[h])
            mm([(R(bank, r, HL, 16), R("TRI", 128 * r, 128 * r + 128), R("EQ", 2176 * h + r, min(W, 2176 * h + 2176), 272)) for r in range(16)], acc[h])
        mm([(FLL, im("IP"), CM2048(16))] + [(FLL, bv("BN1", r), R("HF", r, L, 16)) for r in range(16)])
        tt(R("LH", 80, 96), FLL, R("ST", 15, 256, 16), Op.add)
        cur[0] = "y"
        lin(li(1), R("ST", (512 if v else 0) + 15, (512 if v else 0) + 256, 16), 1.0, 0.125, "V")
        tt(R("DC"), X(XA, li(1)), R(Z), Op.subtract)
        act(R("DC2"), R("DC"), Act.Abs, 2.0, 2 * ZO)
        mm([(UP4, im("IP"), R("DC2")), (UP4, im("IN1"), R(Z))])
        lin(R("XW", 0, 256), UP4, 1.0, ZO + 0.5)
        for c in range(4):
            s = lambda n: R(n, CL * c, CL * c + CL)
            xg = R("XG", CE * c, CE * c + CE)
            cur[0] = "d"
            lin(xg, X(XA, s("MU")), eng=PARAM["d"][v][c])
            cur[0] = "e"
            tt(xg, X(XD, s("SU")), xg, Op.min)
            dist(c, 1, R("p%d" % (5 + c // 2), CL * (c % 2), CL * (c % 2) + CL), "BN16", [], acc[c // 2])
        for h in range(2):
            s = lambda n: R(n, HL * h, HL * h + HL)
            e8 = lambda n, o: R(n, o + 8 * h, o + 8 * h + 8)
            bank = "p%d" % (5 + h)
            ke, new, best = R(bank, 0, 128), R(bank, 128, 256), R(bank, 256, 384)
            cur[0] = "w"
            tr(s("KET"), ke)
            scan(s("MX2"), R("RMM"), s("KET"), Op.min, Op.max)
            ts(s("KP"), ke, 2 * BAND - 15.5, Op.is_gt)
            tt(s("EQT"), X(s("MX2"), li(4, 0)), s("KET"), Op.is_equal)
            tr(best, s("EQT"))
            tt(s("SL"), best, s("MH"), Op.mult)
            mm([(new, im("IP"), CN8(HL)), (new, im("IN1"), s("MH")), (new, im("BOH"), s("SL"))])
            tt(s("DL"), new, s("KP"), Op.mult)
            top = R("MX2", HL * h + 15, HL * h + HL, 16)
            ts(e8("LH", 48), top, 1.5 * BAND, Op.is_le, 8192.0, Op.mult)
            mm([m + (i % 2 == 0, i % 2 == 1) for i, m in enumerate(tolist("p4", 8 * h, 48 + 8 * h, 8))]
               + [(e8("p4", 16), im("I1"), e8("LH", 80), True, False)] + [m + (False, i == 3) for i, m in enumerate(tolist("p4", 16 + 8 * h, 48 + 8 * h, 8))])
            tt(e8("TY", 32), e8("p4", 16), e8("AL", 64), Op.min)
            lin(li(2, h), e8("TY", 32), 1.0, 2048.125, "V")
            tt(X(R("CT"), li(2, h)), s("DL"), s("MP"), Op.add)
            cur[0] = "x"
            ts(e8("LH", 64), top, 2 * BAND - 15.5, Op.is_gt, 49152.0, Op.mult)
            mm([(e8(idle, 0), im("IP"), CGOT(8))] + tolist(idle, 8 * h, 64 + 8 * h, 8)
               + [(e8(idle, 0), bv("B1H", r), R("SL", HL * h + r, HL * h + HL, 16)) for r in range(16)])
            ops[-1]["name"] = "c%d" % h
            tt(e8("TY", 48), e8(idle, 0), e8("AL", 48), Op.max)
            lin(li(3, h), e8("TY", 48), 1.0, 255.125, "V")
            tt(s("DC"), X(XZ, li(3, h)), s(Z), Op.add)
            lin(s("Y%dH" % v), s("DC"), 0.5, ZO / 2 - 0.25)
            if not last:
                rdma([(s("Z%d" % (v + 1)), s("Y%dH" % v))], "az%d%d" % (v + 1, h))
        if last:
            lin(R("SV"), R("Y%dH" % v), 1.0, -ZO)
            dma(R("yz"), R("SV"), 131072)
        else:
            cur[0] = "n"
            red(AI, R("p4", 0, 16))
            mm([(WS, R("BOA"), AI)])
            tt(ci(9), WS, ci(8), Op.add)
            ts(ci(8), ci(9), 127, Op.bitwise_and)
            ts(TWX, ci(8), 16 * KS, Op.mult, T1X, Op.add)
        cur[0] = "s"
        mm([(R("p5", 128, 384), im("I8K"), R("KP")), (R("p5", 128, 384), im("I1"), R("MH"))])
        act(R("KM"), R("p5", 128, 384), Act.Relu, 1.0, CKM)
        mm([(R("p6", 128, 384), R("WB32"), R("KM"))])
        lin(R("YV"), R("p6", 128, 384))
        lin(X(R("YT"), li(3)), R("YV"), eng="V")
        if not last:
            pre(v + 1)

    cur[0] = "i"
    for c in range(8):
        lin(R("PB", 512 * c, 512 * c + 512), R("MI", 512 * c, 512 * c + 512), 1.0, -2047.0)
    mm([(R("p2", 0, 256), bv("BK1", x), R("PB", 256 * x, 256 * x + 256)) for x in range(16)])
    lin(R("Y0"), R("p2", 0, 256), 1.0, 136 * 2048.0)
    ts(R("FA"), R("Y0"), 0.0, Op.is_equal, 8388608.0, Op.mult)
    tt(R("Y0"), R("Y0"), R("FA"), Op.add)
    ops[-1]["name"] = "Y1"
    ts(R("MC"), R("MC"), P256, Op.add)
    lin(R("MC8"), R("MC"), 1.0, 0.125)
    lin(R("C1"), R("MC"), 1.0, 2049.0)
    cur[0] = "o"
    dma(R("RT"), R("YT", 256, 256 + W, 1, (0, 128, 16)), 131072)
    tt(R("RT"), R("RT"), R("Y0"), Op.min)
    for c in range(4):
        tt(R("PG", CE * c, CE * c + CE), X(CG, R("REPU", CL * c, CL * c + CL)), R("OH", CE * c, CE * c + CE), Op.mult)
        mm(extract(R("p%d" % (c // 2), CL * (c % 2), CL * (c % 2) + CL), "B32", "PG", c))
    for h in range(2):
        s = lambda n: R(n, HL * h, HL * h + HL)
        o, f0, f1 = R("p%d" % h, 0, HL), R("p3", 256 * h, 256 * h + HL), R("p3", 256 * h + HL, 256 * h + 256)
        ts(s("DD"), o, RND + 2048, Op.add, -RND, Op.add)
        tt(f0, o, s("MC"), Op.is_equal)
        tt(f1, o, s("MC8"), Op.is_equal)
        tt(s("FA"), f0, s("RT"), Op.mult)
        tt(f1, f1, s("C1"), Op.mult)
        tt(s("FB"), f1, s("FA"), Op.add)
    dma(R("yr"), R("DD"), 131072, "S")
    dma(R("yc"), R("FB"), 131072)
    return ops


def depend(ops):
    seen = {}
    for i, o in enumerate(ops):
        dep = {}
        for k in o["prev"]:
            dep[k] = None
        for w, lst in ((True, o["wr"]), (False, o["rd"])):
            for a in set(lst):
                pl, ph = (a[5] or (0, 128))[:2]
                for j, w2, lo, hi, ql, qh in seen.get(a[1], []):
                    if ph <= ql or qh <= pl:
                        continue
                    p = ops[j]
                    if o["acc"] and p["acc"] and o["acc"][1] == p["acc"][1] and p["acc"][0] == "acc":
                        continue
                    if lo < a[3] and a[2] < hi and (w or w2):
                        dep[j] = bool(dep.get(j)) or o["kind"] != "mm" or p["kind"] != "mm"
        o["dep"] = dict(sorted(dep.items()))
        o["banks"] = sorted(set([a[1] for a in o["wr"] + o["rd"] if inps(a)]))
        for w, lst in ((True, o["wr"]), (False, o["rd"])):
            for a in sorted(set(lst), key=str):
                s = seen.setdefault(a[1], [])
                if w and a[4] == 1 and a[5] is None and not o["acc"]:
                    s[:] = [x for x in s if not (a[2] <= x[2] and x[3] <= a[3] and x[0] != i)]
                s.append((i, w, a[2], a[3]) + (a[5] or (0, 128))[:2])


def tag(o):
    w = o["wr"][0]
    s = w[1].rstrip("01234H") if w[1][0] != "p" else w[1]
    return "%s %s %s" % (o["part"], o["kind"], o.get("name", s + str(w[2])))


def lat(o):
    return 1.6 + o["lat"] / DBW if o["kind"] == "dma" else o["lat"]


def after(ops, o, e, eng, end, wait):
    t = 0.0
    for j, raw in o["dep"].items():
        if raw is None and eng[j] == e:
            continue
        if eng[j] != e or ops[j]["sem"] or raw:
            t = max(t, end[j] + wait)
    return t


def finish(o, t, c, pipe):
    if o["kind"] == "dma":
        pipe[0] = max(pipe[0], t + 1.6) + o["lat"] / DBW
        return pipe[0]
    return t + c + o["lat"]


def schedule(ops, succ, pr, look, wait):
    n = len(ops)
    eng, start, end = [None] * n, [0.0] * n, [0.0] * n
    left = [len(o["dep"]) for o in ops]
    ready = {}
    for i in range(n):
        if not left[i]:
            ready[i] = [(0.0, e, c) for e, c in ops[i]["cost"].items()]
    free = {e: 0.0 for e in "VSPGY"}
    pipe, order = [0.0], []
    last, extra = {}, [[] for _ in ops]
    while ready:
        cand = []
        for i, l in ready.items():
            for t, e, c in l:
                t = max(t, free[e])
                for b in ops[i]["banks"]:
                    for e2, j in last.get(b, {}).items():
                        if e2 != e and end[j] + wait > t:
                            t = end[j] + wait
                cand.append((t, -pr[i], i, e, c))
        t, _, i, e, c = min(cand)
        for _ in range(3):
            better = [x for x in cand if x[3] == e and x[1] < -pr[i] - 1e-9 and x[0] < t + look * c]
            if not better:
                break
            t, _, i, e, c = min(better, key=lambda x: x[1])
        if len(ready[i]) > 1:
            t, _, i, e, c = min([x for x in cand if x[2] == i], key=lambda x: x[0] + x[4])
        eng[i], start[i], end[i] = e, t, finish(ops[i], t, c, pipe)
        free[e] = t + c
        for b in ops[i]["banks"]:
            extra[i] += [j for e2, j in last.setdefault(b, {}).items() if e2 != e]
            last[b][e] = i
        order.append(i)
        del ready[i]
        for j in succ[i]:
            left[j] -= 1
            if not left[j]:
                ready[j] = [(after(ops, ops[j], e2, eng, end, wait), e2, c2) for e2, c2 in ops[j]["cost"].items()]
    return order, eng, start, end, extra


def replay(ops, costs, wait, order, eng, extra):
    end, free, pipe = [0.0] * len(ops), {e: 0.0 for e in "VSPGY"}, [0.0]
    for i in order:
        e = eng[i]
        t = max([free[e], after(ops, ops[i], e, eng, end, wait)] + [end[j] + wait for j in extra[i]])
        free[e] = t + costs[i][e]
        end[i] = finish(ops[i], t, costs[i][e], pipe)
    return max(end)


def queues(ops):
    pool, used, seq = {}, set(), {"V": [], "S": []}
    for i, o in enumerate(ops):
        p, k, w = tag(o).split()
        pool.setdefault((o["vis"], p[0]), []).append((w, i))
    lists = {"V": [V_FIRST] + [V_MID] * (VI - 2) + [V_LAST], "S": [S_FIRST] + [S_MID] * (VI - 2) + [S_LAST]}
    for star in (False, True):
        for e in "VS":
            steps = [(v + {"<": -1, ">": 1}.get(t[0], 0), t.lstrip("<>")) for v in range(VI) for t in lists[e][v].split()]
            for n, (v, t) in enumerate(steps):
                p, w = t.split(".")
                if w.endswith("*") == star:
                    got = [i for x, i in pool[(v, p)] if e in ops[i]["cost"] and i not in used and (x.startswith(w[:-1]) if star else x == w)]
                    got = got if star else got[:1]
                    used.update(got)
                    seq[e] += [(n, i) for i in got]
    rank, seen, steps = {}, {}, P_ALL.split()
    for i, o in enumerate(ops):
        if o["kind"] == "mm":
            p, k, w = tag(o).split()
            t = p[0] + "." + w
            c = [n for n, x in enumerate(steps) if x.lstrip(">") in (t, p[0])]
            seen[(o["vis"], t)] = seen.get((o["vis"], t), 0) + 1
            n = c[min(seen[(o["vis"], t)], len(c)) - 1]
            rank[i] = 100 * (o["vis"] - (steps[n][0] == ">")) + n + i * 1e-5
    return dict([(e, [i for _, i in sorted(seq[e])]) for e in "VS"]), rank


def first_plan(ops, wait):
    n, (seq, rank) = len(ops), queues(ops)
    eng = [list(o["cost"])[0] for o in ops]
    for e in "VS":
        for i in seq[e]:
            eng[i] = e
    ramps = [i for i in range(n) if ops[i]["kind"] == "iota"]
    sends = [i for i in range(n) if ops[i]["kind"] == "rdma"]
    seq["G"] = ramps[:22] + sends[:1] + ramps[22:] + sends[1:]
    seq["Y"] = sorted([i for i in range(n) if eng[i] == "Y"], key=lambda i: tag(ops[i])[-3:] in ("yz0", "yc0"))
    seq["S"] = [i for i in range(8) if eng[i] == "S"] + seq["S"]
    seq = dict([(e, seq[e][::-1]) for e in seq])
    left, end, start = [len(o["pre"]) for o in ops], [0.0] * n, [0.0] * n
    free, last, pipe, ready = dict([(e, 0.0) for e in "VSPGY"]), {}, 0.0, []

    def when(i):
        t = max([free[eng[i]]] + [end[j] + wait for j, hard in ops[i]["pre"] if hard or eng[j] != eng[i]])
        return max([t] + [end[j] + wait for b in ops[i]["banks"] for e, j in last.get(b, {}).items() if e != eng[i]])

    for _ in range(n):
        c = [(when(seq[e][-1]), seq[e][-1]) for e in "VSGY" if seq[e] and not left[seq[e][-1]]]
        p = [(when(i), i) for i in ready]
        if p and (not c or min(p)[0] <= min(c)[0]):
            t, i = min([x for x in p if x[0] <= min(p)[0] + 0.15], key=lambda x: rank[x[1]])
            ready.remove(i)
        else:
            t, i = min(c)
            seq[eng[i]].pop()
        o = ops[i]
        free[eng[i]] = t + o["cost"][eng[i]]
        for b in o["banks"]:
            last.setdefault(b, {})[eng[i]] = i
        if o["lag"] < 0:
            pipe = max(pipe, t + 1.6) - o["lag"]
        start[i], end[i] = t, pipe if o["lag"] < 0 else free[eng[i]] + o["lag"]
        for j in o["succ"]:
            left[j] -= 1
            if not left[j] and eng[j] == "P":
                ready.append(j)
    return start, eng


def run(ops, cost, wait, order, eng):
    n = len(ops)
    end, why, res = [0.0] * n, [None] * n, [True] * n
    free, prev, last, pipe = dict([(e, 0.0) for e in "VSPGY"]), {}, dict([("p%d" % b, {}) for b in range(8)]), 0.0
    for i in order:
        o, e = ops[i], eng[i]
        t, w = free[e] - wait, prev.get(e)
        for j, hard in o["pre"]:
            if end[j] > t and (hard or eng[j] != e):
                t, w, res[i] = end[j], j, False
        for b in o["banks"]:
            lb = last[b]
            for e2, j in lb.items():
                if end[j] > t and e2 != e:
                    t, w, res[i] = end[j], j, True
            lb[e] = i
        t += wait + cost[i][e]
        free[e], prev[e], why[i] = t, i, w
        if o["lag"] < 0:
            pipe = max(pipe, t + 1.54) - o["lag"]
            end[i] = pipe
        else:
            end[i] = t + o["lag"]
    return max(end), end, why, res


def arrange(ops, costs):
    n = len(ops)
    seen, cls = {}, []
    for i, o in enumerate(ops):
        o["pre"] = [(j, bool(raw) or (bool(ops[j]["sem"]) and raw is not None)) for j, raw in o["dep"].items()]
        o["lag"] = -o["lat"] / DBW if o["kind"] == "dma" else o["lat"]
        o["succ"] = []
        for j in o["dep"]:
            ops[j]["succ"].append(i)
        seen[(tag(o), o["vis"])] = seen.get((tag(o), o["vis"]), 0) + 1
        cls.append((tag(o), seen[(tag(o), o["vis"])]))
    succ = [o["succ"] for o in ops]
    start, eng = first_plan(ops, MODELS[0][4])
    engs = dict([(cls[i], eng[i]) for i in range(n)])
    heads = [i for i in range(n) if cls[i][0].endswith("tt AO0")]
    x = [PARAM["seed"]]

    def draw(k=0):
        x[0] = (x[0] * 1103515245 + 12345) % 2147483648
        return int(k * x[0] / 2147483648.0) if k else x[0] / 2147483648.0

    def value(tau, engs, vis):
        key = [tau[c] + v for c, v in zip(cls, vis)]
        for i in range(n - 1, -1, -1):
            for j in succ[i]:
                if key[j] <= key[i]:
                    key[i] = key[j] - 1e-4
        eng = [engs[c] for c in cls]
        order = sorted(range(n), key=lambda i: key[i])
        rs = [run(ops, costs[m], MODELS[m][4], order, eng) for m in PARAM["models"]]
        return sum([r[0] / WEIGHT[m] for r, m in zip(rs, PARAM["models"])]), rs, key, eng, order

    def meets(cur):
        edges = []
        for _, end, why, res in cur[1]:
            i = end.index(max(end))
            while why[i] is not None:
                if res[i] and why[i] not in ops[i]["dep"]:
                    edges.append((why[i], i))
                i = why[i]
        return edges

    for rounds in range(PARAM["rounds"]):
        per = start[heads[2]] - start[heads[1]]
        off = {0: start[heads[0]] - per, 2: start[heads[1]], VI - 1: start[heads[3]]}
        vis = [o["vis"] * per for o in ops]
        tau = dict([(cls[i], start[i] - off[o["vis"]] if o["kind"] != "dma" else i * 0.01 - 100 if i < 8 else 100.0)
                    for i, o in enumerate(ops) if o["vis"] in off])
        best = cur = value(tau, engs, vis)
        edges, keep = meets(cur), engs
        for it in range(PARAM["iters"]):
            key, eng = cur[2], cur[3]
            j, i = edges[draw(len(edges))]
            t2, e2, u = dict(tau), engs, draw()
            d = (0.001, 0.001, 0.001, 0.2, 0.5, 1.0, 2.0, 4.0)[draw(8)]
            flex = [a for a in (i, j) if len(ops[a]["cost"]) > 1]
            if u >= 0.92:
                i = draw(n)
                t2[cls[i]] = key[i] - vis[i] + (draw() - 0.5) * d * 2
                flex = [i] if len(ops[i]["cost"]) > 1 and draw() < 0.5 else []
            if flex and (u < 0.2 or u >= 0.92):
                a = flex[draw(len(flex))]
                e2 = dict(engs)
                e2[cls[a]] = "V" if eng[a] == "S" else "S"
            elif u < 0.55:
                t2[cls[i]] = key[j] - vis[i] - d
            elif u < 0.92:
                stack = [(j, key[i] + d)]
                while stack:
                    a, k = stack.pop()
                    if key[a] < k and t2[cls[a]] + vis[a] < k and a != i:
                        t2[cls[a]] = k - vis[a]
                        stack += [(b, k + 1e-3) for b in succ[a]]
            new = value(t2, e2, vis)
            if new[0] <= cur[0] + PARAM["slack"] * draw() * (1 - it / PARAM["iters"]):
                cur, tau, engs = new, t2, e2
                edges = meets(cur)
                if new[0] < best[0]:
                    best, keep = new, e2
        engs = keep
        start = [best[1][0][1][i] - costs[PARAM["models"][0]][i][best[3][i]] - max(0.0, ops[i]["lag"]) for i in range(n)]
    return best[4], best[3]


def plan():
    ops = build(*MODELS[0])
    costs = [[o["cost"] for o in build(*m)] for m in MODELS]
    depend(ops)
    order, eng = arrange(ops, costs)
    ts = [run(ops, c, m[4], order, eng)[0] for c, m in zip(costs, MODELS)]
    _, end, why, _ = run(ops, costs[0], MODELS[0][4], order, eng)
    last = {}
    for i in order:
        o = ops[i]
        for b in o["banks"]:
            for e, j in last.setdefault(b, {}).items():
                if e != eng[i]:
                    o["dep"].setdefault(j, False)
            last[b][eng[i]] = i
        o["eng"], o["end"], o["ts"], o["why"] = eng[i], end[i], ts, why[i]
        o["start"] = end[i] - o["cost"][eng[i]] - max(0.0, o["lag"])
    close = {}
    for i in order:
        if ops[i]["acc"]:
            close[ops[i]["acc"][1]] = i
    for i in close.values():
        ops[i]["args"] = ops[i]["args"][:-1] + [ops[i]["args"][-1][:4] + (True,)]
    pos, at = {}, {e: 0 for e in "VSPGY"}
    for i in order:
        if not ops[i]["sem"]:
            at[ops[i]["eng"]] += 1
            pos[i] = at[ops[i]["eng"]]
    know = {e: {} for e in "VSPGY"}
    for i in order:
        o = ops[i]
        e, k, need = o["eng"], know[o["eng"]], []
        for j in sorted(o["dep"], key=lambda j: -ops[j]["end"]):
            p = ops[j]
            if o["dep"][j] is None and p["eng"] == e:
                continue
            if p["sem"]:
                key, val = ("D", j), 1
            elif p["eng"] != e or o["dep"][j] or o["sem"]:
                key, val = p["eng"], pos[j]
            else:
                continue
            if k.get(key, 0) >= val:
                continue
            need.append(j)
            k[key] = val
            if p["kind"] != "rdma":
                for kk, vv in p["know"].items():
                    k[kk] = max(k.get(kk, 0), vv)
            p["inc"] = True
        o["need"], o["know"] = need, dict(k)
    at = {e: 0 for e in "VSPGY"}
    for i in order:
        if ops[i].get("inc") and not ops[i]["sem"]:
            at[ops[i]["eng"]] += 1
            ops[i]["val"] = at[ops[i]["eng"]]
    return [ops[i] for i in order], ops, at


PLAN = []


def rank_program(g, core, T, topo):
    rank = T.rank_of(core)
    if rank is None:
        return
    if not PLAN:
        PLAN.append(plan())
    order, ops, total = PLAN[0]
    nxt = T.cores[(rank + 1) % NR]
    rid, pid = topo.addr(nxt)[0], topo.addr(nxt)[1]
    mask = topo.mask(core, nxt)
    ne = len(topo.engines(core, nxt))
    Q = {"V": g.vector, "S": g.scalar, "P": g.tensor, "G": g, "Y": g.sync}
    sent, outs = 0, []
    for o in order:
        e, a, k = o["eng"], o["args"], o["kind"]
        q = Q[e]
        for j in o["need"]:
            p = ops[j]
            if p["kind"] == "rdma":
                q.wait_ge(T.sem[p["sem"][0]], ne * p["sem"][1])
            elif p["sem"]:
                q.wait_ge(T.sem[p["sem"][0]], 16)
            else:
                q.wait_ge(T.sem["s" + p["eng"]], p["val"])
        if k == "rdma":
            for dst, src in a:
                g.remote_dma(ap(T, dst), ap(T, src), T.sem[o["sem"][0]], T.sem.sent, pid, rid, mask)
                sent += ne
            continue
        if k == "dma":
            q.dma_start(ap(T, a[0]), ap(T, a[1])).then_inc(T.sem[o["sem"][0]], 16)
            if not o.get("inc"):
                outs.append(o["sem"][0])
            continue
        if k == "mm":
            for m in a:
                ins = q.matmul(ap(T, m[0]), ap(T, m[1]), ap(T, m[2]), m[3], m[4])
        elif k == "tt":
            ins = q.tensor_tensor(ap(T, a[0]), ap(T, a[1]), ap(T, a[2]), a[3])
        elif k == "ts":
            if a[5] is None:
                ins = q.tensor_scalar(ap(T, a[0]), ap(T, a[1]), ap(T, a[2]), None, a[4])
            else:
                ins = q.tensor_scalar(ap(T, a[0]), ap(T, a[1]), ap(T, a[2]), ap(T, a[3]), a[4], a[5])
        elif k == "lin":
            if e == "S":
                ins = q.activation(ap(T, a[0]), ap(T, a[1]), a[4], bias=a[3], scale=ap(T, a[2]))
            elif a[2] == 1.0 and a[3] == 0.0:
                ins = q.tensor_copy(ap(T, a[0]), ap(T, a[1]))
            else:
                ins = q.tensor_scalar(ap(T, a[0]), ap(T, a[1]), ap(T, a[2]), a[3], Op.mult, Op.add)
        elif k == "step":
            if e == "S":
                ins = q.activation(ap(T, a[0]), ap(T, a[1]), Act.Relu, bias=ap(T, a[3]), scale=2.0)
            else:
                ins = q.tensor_scalar(ap(T, a[0]), ap(T, a[1]), ap(T, a[2]), KS, Op.is_gt, Op.mult)
        elif k == "act":
            ins = q.activation(ap(T, a[0]), ap(T, a[1]), a[2], bias=ap(T, a[4]), scale=a[3])
        elif k == "scan":
            ins = q.tensor_tensor_scan(ap(T, a[0]), ap(T, a[1]), ap(T, a[2]), a[3], a[4], a[5])
        elif k == "tr":
            ins = q.transpose(ap(T, a[0]), ap(T, a[1]))
        elif k == "red":
            ins = q.tensor_reduce(ap(T, a[0]), ap(T, a[1]), AxisListType.X, Op.add)
        elif k == "ms":
            ins = q.memset(ap(T, a[0]), a[1])
        elif SCRATCH[a[0][1]][2] == I32:
            ins = g.iota(ap(T, a[0]), a[1], a[2], a[3])
        else:
            ins = g.iota(ap(T, a[0]), a[1], a[2], a[3], allow_small_or_imprecise_dtypes=True)
        if o.get("inc"):
            ins.then_inc(T.sem["s" + e], 1)
    g.wait_ge(T.sem.sent, sent)
    for s in outs:
        g.sync.wait_ge(T.sem[s], 16)
